import numpy as np
import ml_dtypes


def mxq(x, axis, fmt="e4m3"):
    dtype, down = {"e4m3": (ml_dtypes.float8_e4m3fn, 7), "e5m2": (ml_dtypes.float8_e5m2, 14)}[fmt]
    v = np.moveaxis(np.asarray(x, np.float32).astype(ml_dtypes.bfloat16).astype(np.float64), axis, -1)
    blocks = v.reshape(v.shape[:-1] + (-1, 32))
    amax = np.abs(blocks).max(-1, keepdims=True)
    byte = np.maximum(np.where(amax > 0, np.frexp(amax)[1] - 1 + 127, 0) - down, 1)
    scale = np.exp2(byte - 127.0)
    codes = (blocks / scale).astype(np.float32).astype(dtype).astype(np.float64)
    return np.moveaxis((codes * scale).reshape(v.shape), -1, axis)


WIDE = False


def mx_kscale(k):
    if not WIDE:
        return np.ones(k)
    levels = np.array([10, -10, 5, -5, 0])
    if k % 512:
        return np.exp2(np.random.permutation(np.resize(levels, k // 32))).repeat(32)
    a = np.empty((k // 512, 16))
    for p in range(k // 512):
        a[p, :8] = np.random.permutation(np.resize(levels, 8))
        for g in range(8):
            far = levels[np.abs(levels - a[p, g]) >= 10]
            a[p, g + 8] = far[np.random.randint(len(far))]
    return np.exp2(a.ravel()).repeat(32)


def f64(x):
    return np.asarray(x).astype(np.float64)


def striped(idx):
    return np.tile(idx.reshape(-1, 16).T, (8, 1)).astype(np.uint16)


def unstriped(offs):
    return offs[:16].T.reshape(-1).astype(np.int64)


E2M1 = np.array([0.0, 0.5, 1.0, 1.5, 2.0, 3.0, 4.0, 6.0, -0.0, -0.5, -1.0, -1.5, -2.0, -3.0, -4.0, -6.0])


def pack_weight(w, fmt):
    k, n = w.shape
    w = f64(np.asarray(w, np.float32).astype(ml_dtypes.bfloat16)).reshape(k // 32, 32, n)
    amax = np.abs(w).max(1)
    if fmt == "e4m3":
        byte = np.frexp(amax)[1] - 1 + 127 - 7
    else:
        mant, ex = np.frexp(amax / 6.0)
        byte = np.where(mant > 0.5, ex, ex - 1) + 127
    byte = np.clip(np.where(amax > 0, byte, 1), 1, 254)
    scaled = (w * np.exp2(127.0 - byte)[:, None, :]).reshape(k, n).astype(np.float32)
    by_word = np.ascontiguousarray(scaled.reshape(k // 512, 128, 4, n).transpose(0, 1, 3, 2))
    if fmt == "e4m3":
        words = by_word.astype(ml_dtypes.float8_e4m3fn).view(np.uint8)
    else:
        c = by_word.astype(ml_dtypes.float4_e2m1fn).view(np.uint8) & 0xF
        words = (c[..., 0::2] | (c[..., 1::2] << 4)).reshape(k // 512, 128, 2 * n)
    return np.ascontiguousarray(words), np.ascontiguousarray(byte.astype(np.uint8).reshape(k // 512, 16, n))


def unpack_weight(words, scales, fmt):
    g, _, n = scales.shape
    words = np.ascontiguousarray(words).reshape(g, 128, n, -1)
    if fmt == "e4m3":
        vals = words.view(ml_dtypes.float8_e4m3fn).astype(np.float64)
    else:
        nib = np.empty((g, 128, n, 4), np.uint8)
        nib[..., 0::2] = words & 0xF
        nib[..., 1::2] = words >> 4
        vals = E2M1[nib]
    vals = vals * np.repeat(np.exp2(scales.astype(np.float64) - 127.0), 8, axis=1)[..., None]
    return vals.transpose(0, 1, 3, 2).reshape(g * 512, n)


def sigmoid(v):
    return 1.0 / (1.0 + np.exp(-np.maximum(v, -700.0)))


def d_sigmoid(v):
    s = 1.0 / (1.0 + np.exp(-np.maximum(v, -700.0)))
    return s * (1.0 - s)


K, T, E, C, H, N = 384, 512, 8, 128, 512, 1024


def by_expert(wq, xq):
    return np.concatenate([wq[e].T @ xq[:, e * C:(e + 1) * C] for e in range(E)], axis=1)


def setup_inputs():
    n = np.random.standard_normal
    s = mx_kscale(N)[:, None]
    u = mx_kscale(H)
    first = np.random.permutation(np.repeat(np.arange(E), T // E))
    second = (first + 1 + np.random.permutation(np.repeat(np.arange(E - 1), -(-T // (E - 1)))[:T])) % E
    while np.bincount(second, minlength=E).max() != T // E:
        load = np.bincount(second, minlength=E); hi, lo = int(load.argmax()), int(load.argmin())
        t = np.flatnonzero((second == hi) & (first != lo))[0]; second[t] = lo
    slot_token = np.empty(E * C, np.int64); pos = np.empty((2, T), np.int64); fill = np.zeros(E, np.int64)
    place = np.stack([np.random.permutation(C) for _ in range(E)])
    for r, deal in enumerate((first, second)):
        for t in np.random.permutation(T):
            e = deal[t]; j = e * C + place[e, fill[e]]; fill[e] += 1; slot_token[j] = t; pos[r, t] = j
    g = np.random.uniform(0.2, 0.8, T)
    w_slot = np.empty(E * C); w_slot[pos[0]] = g; w_slot[pos[1]] = 1.0 - g
    dy = pack_weight(n((N, T)) * s, "e4m3")
    w2 = [pack_weight(m, "e2m1") for m in n((E, N, H)) / np.sqrt(N) / s[None] * u[None, None, :]]
    w1 = [pack_weight(m, "e2m1") for m in n((E, H, K)) / np.sqrt(H) / u[None, :, None]]
    w3 = [pack_weight(m, "e2m1") for m in n((E, H, K)) / np.sqrt(H) / u[None, :, None]]
    return {
        "dy_words": dy[0],
        "dy_scales": dy[1],
        "a1": n((H, E * C)).astype(np.float32),
        "a3": n((H, E * C)).astype(np.float32),
        "w2_words": np.stack([m[0] for m in w2]),
        "w2_scales": np.stack([m[1] for m in w2]),
        "w1_words": np.stack([m[0] for m in w1]),
        "w1_scales": np.stack([m[1] for m in w1]),
        "w3_words": np.stack([m[0] for m in w3]),
        "w3_scales": np.stack([m[1] for m in w3]),
        "gate": np.tile(w_slot, (H, 1)).astype(np.float32),
        "offs": striped(slot_token),
        "pos1": striped(pos[0]),
        "pos2": striped(pos[1]),
    }


def reference(dy_words, dy_scales, a1, a3, w2_words, w2_scales, w1_words, w1_scales, w3_words, w3_scales, gate, offs, pos1, pos2):
    idx = unstriped(offs)
    w2 = np.stack([unpack_weight(w2_words[e], w2_scales[e], "e2m1") for e in range(E)])
    w1 = np.stack([unpack_weight(w1_words[e], w1_scales[e], "e2m1") for e in range(E)])
    w3 = np.stack([unpack_weight(w3_words[e], w3_scales[e], "e2m1") for e in range(E)])
    gq = unpack_weight(dy_words, dy_scales, "e4m3")[:, idx]
    dh = f64(gate) * by_expert(w2, gq)
    da1 = dh * f64(a3) * d_sigmoid(f64(a1))
    da3 = dh * sigmoid(f64(a1))
    dx = by_expert(w1, mxq(da1, 0, "e4m3")) + by_expert(w3, mxq(da3, 0, "e4m3"))
    return dx[:, unstriped(pos1)] + dx[:, unstriped(pos2)]

@@ -1,0 +1,195 @@
+from contextlib import ExitStack
+
+import concourse.mybir as mybir
+from concourse.masks import make_identity
+
+K, T, E, C, H, N = 384, 512, 8, 128, 512, 1024
+S = E * C
+FLOPS = 2 * S * (N * H + 2 * H * K)
+
+F32 = mybir.dt.float32
+BF16 = mybir.dt.bfloat16
+I32 = mybir.dt.int32
+U32 = mybir.dt.uint32
+U16 = mybir.dt.uint16
+U8 = mybir.dt.uint8
+FP8X4 = mybir.dt.float8_e4m3fn_x4
+FP4X4 = mybir.dt.float4_e2m1fn_x4
+ACT = mybir.ActivationFunctionType
+ALU = mybir.AluOpType
+
+P = 128
+PACK = 4
+PASSES = N // (P * PACK)
+KT = K // P
+PAIR = 2
+PAIRS = E // PAIR
+W = PAIR * C
+LIST = 16
+
+
+def tile_moe_bdx_glu_sigmoid_kernel(
+    tc, dy_words, dy_scales, a1, a3, w2_words, w2_scales, w1_words, w1_scales,
+    w3_words, w3_scales, gate, offs, pos1, pos2, out,
+):
+    nc = tc.nc
+    with ExitStack() as ctx:
+        keep = ctx.enter_context(tc.tile_pool(name="keep", bufs=1))
+        work = ctx.enter_context(tc.tile_pool(name="work", bufs=4))
+        ps_dh = ctx.enter_context(tc.psum_pool(name="ps_dh", bufs=2))
+        ps_tr = ctx.enter_context(tc.psum_pool(name="ps_tr", bufs=3))
+        ps_dx = ctx.enter_context(tc.psum_pool(name="ps_dx", bufs=3))
+
+        offs_t = keep.tile([P, S // LIST], U16, name="offs_t")
+        nc.sync.dma_start(offs_t[:], offs)
+
+        dy_s = keep.tile([P, T], U8, name="dy_s", align_bytes=64)
+        w2_s = keep.tile([P, E * PASSES, H], U8, name="w2_s", align_bytes=64)
+        g_s1 = keep.tile([P, S], U8, name="g_s1", align_bytes=64)
+        w13_s = [keep.tile([P, E, K], U8, name=f"w13_s{m}", align_bytes=64) for m in range(2)]
+        nc.vector.memset(dy_s[:].bitcast(I32), 0)
+        for q in range(4):
+            nc.sync.dma_start(dy_s[32 * q : 32 * q + 8, :].bitcast(I32), dy_scales[:, 4 * q : 4 * q + 4, :].bitcast(I32))
+        nc.vector.memset(w2_s[:].bitcast(I32), 0)
+        nc.vector.memset(g_s1[:].bitcast(I32), 0)
+        for m in range(2):
+            nc.gpsimd.memset(w13_s[m][:].bitcast(I32), 0)
+
+        warm = keep.tile([P, 8], F32, name="warm")
+        nc.gpsimd.memset(warm[:], 0.0)
+        nc.scalar.activation(warm[:], warm[:], ACT.Sigmoid)
+        dy_w = [keep.tile([P, T], U32, name=f"dy_w{o}", align_bytes=64) for o in range(PASSES)]
+        for o in range(PASSES):
+            nc.sync.dma_start(dy_w[o][:].bitcast(I32), dy_words[o].rearrange("p t d -> p (t d)").bitcast(I32))
+
+        w2_rows = w2_scales.rearrange("e s (q r) i -> r q (e s) i", r=4)
+        for r in range(4):
+            nc.scalar.dma_start(w2_s[r:P:32, :, :].bitcast(I32), w2_rows[r].bitcast(I32))
+
+        ident = keep.tile([P, P], F32, name="ident")
+        make_identity(nc, ident[:])
+        gate_rows = keep.tile([P, C], F32, name="gate_rows")
+        nc.gpsimd.memset(gate_rows[:], 0.0)
+        nc.sync.dma_start(gate_rows[0:E, :], gate[0].rearrange("(e c) -> e c", c=C))
+
+        w2_w, a1_t, a3_t = [], [], []
+        a1_v = a1.rearrange("(p t) j -> p t j", t=PACK)
+        a3_v = a3.rearrange("(p t) j -> p t j", t=PACK)
+        for u in range(PAIRS):
+            w2_w.append(keep.tile([P, PAIR * PASSES, 2 * H], U8, name=f"w2_w{u}", align_bytes=64))
+            nc.sync.dma_start(
+                w2_w[u][:].bitcast(I32),
+                w2_words[PAIR * u : PAIR * (u + 1)].rearrange("e s p b -> p (e s) b").bitcast(I32),
+            )
+            a1_t.append(keep.tile([P, PACK, W], F32, name=f"a1_t{u}"))
+            a3_t.append(keep.tile([P, PACK, W], F32, name=f"a3_t{u}"))
+            nc.sync.dma_start(a1_t[u][:], a1_v[:, :, u * W : (u + 1) * W])
+            nc.sync.dma_start(a3_t[u][:], a3_v[:, :, u * W : (u + 1) * W])
+
+        for m, scales in enumerate((w1_scales, w3_scales)):
+            rows = scales.rearrange("e s (q r) k -> r q (e s) k", r=4)
+            for r in range(4):
+                nc.sync.dma_start(w13_s[m][r:P:32, :, :].bitcast(I32), rows[r].bitcast(I32))
+        w13_w = {}
+        for kt in range(KT):
+            for m, words in enumerate((w1_words, w3_words)):
+                w13_w[m, kt] = keep.tile([P, E, 2 * P], U8, name=f"w13_w{m}{kt}", align_bytes=64)
+                nc.sync.dma_start(
+                    w13_w[m, kt][:].bitcast(I32),
+                    words.rearrange("e s p b -> p (e s) b")[:, :, 2 * P * kt : 2 * P * (kt + 1)].bitcast(I32),
+                )
+        pos_t = [keep.tile([P, T // LIST], U16, name=f"pos_t{r}") for r in range(2)]
+        nc.sync.dma_start(pos_t[0][:], pos1)
+        nc.sync.dma_start(pos_t[1][:], pos2)
+
+        g_s = keep.tile([P, S], U8, name="g_s", align_bytes=64)
+        g_w = [keep.tile([P, S], U32, name=f"g_w{o}", align_bytes=64) for o in range(PASSES)]
+        for u in range(PAIRS):
+            nc.vector.tensor_copy(g_s[:, u * W : (u + 1) * W], dy_s[:].indirect(offs_t[:, u * W // LIST : (u + 1) * W // LIST]))
+        nc.scalar.dma_start(g_s1[0:100, :].bitcast(I32), g_s[4:104, :].bitcast(I32))
+        g_sc = [g_s, g_s1]
+
+        gate_ps = ps_tr.tile([P, PACK, C], F32, name="dh_ps")
+        nc.tensor.transpose(gate_ps[:, 0, :], gate_rows[:], ident[:])
+        gate_col = keep.tile([P, E], F32, name="gate_col")
+        nc.scalar.copy(gate_col[:], gate_ps[:, 0, 0:E])
+
+        for u in range(PAIRS):
+            for o in range(PASSES):
+                nc.vector.tensor_copy(g_w[o][:, u * W : (u + 1) * W], dy_w[o][:].indirect(offs_t[:, u * W // LIST : (u + 1) * W // LIST]))
+
+        dx = [keep.tile([P, S], F32, name=f"dx{kt}") for kt in range(KT)]
+        groups = [(0, 2), (2, 2), (4, 2), (6, 1), (7, 1)]
+        da_w = [keep.tile([P, 2, n * C], U32, name=f"da_w{e0}", align_bytes=64) for e0, n in groups]
+        da_s = [keep.tile([P, 2, n * C], U8, name=f"da_s{e0}", align_bytes=64) for e0, n in groups]
+
+        def second_product(gs, kt):
+            e_first = groups[gs[0]][0]
+            width = sum(groups[g][1] for g in gs) * C
+            acc = ps_dx.tile([P, width], F32, name="dx_ps")
+            for g in gs:
+                e0, n = groups[g]
+                for x in range(n):
+                    e = e0 + x
+                    for m in range(2):
+                        nc.tensor.matmul_mx(
+                            acc[:, (e - e_first) * C : (e - e_first + 1) * C],
+                            lhsT=w13_w[m, kt][:, e, :].bitcast(FP4X4),
+                            lhsT_scale=w13_s[m][:, e, kt * P : (kt + 1) * P],
+                            rhs=da_w[g][:, m, x * C : (x + 1) * C].bitcast(FP8X4),
+                            rhs_scale=da_s[g][:, m, x * C : (x + 1) * C],
+                            start=(m == 0),
+                            stop=(m == 1),
+                        )
+            nc.scalar.copy(dx[kt][:, e_first * C : e_first * C + width], acc[:])
+
+        for g, (e0, n) in enumerate(groups):
+            u = e0 // PAIR
+            cols = slice((e0 - PAIR * u) * C, (e0 - PAIR * u + n) * C)
+            sig = work.tile([P, n * C, PACK], F32, name="sig")
+            nc.scalar.activation(sig[:], a1_t[u][:, :, cols].rearrange("p t j -> p j t"), ACT.Sigmoid)
+            back = work.tile([P, n * C, PACK], F32, name="back")
+            nc.vector.scalar_tensor_tensor(back[:], sig[:], 1.0, a3_t[u][:, :, cols].rearrange("p t j -> p j t"), ALU.subtract, ALU.mult)
+            da3 = work.tile([P, n * C, PACK], F32, name="da3")
+            for x in range(n):
+                e = e0 + x
+                acc = ps_dh.tile([P, H], F32, name="acc")
+                for o in range(PASSES):
+                    nc.tensor.matmul_mx(
+                        acc[:],
+                        lhsT=g_w[o][:, e * C : (e + 1) * C].bitcast(FP8X4),
+                        lhsT_scale=g_sc[o][:, e * C : (e + 1) * C],
+                        rhs=w2_w[u][:, (e % PAIR) * PASSES + o, :].bitcast(FP4X4),
+                        rhs_scale=w2_s[:, e * PASSES + o, :],
+                        start=(o == 0),
+                        stop=(o == PASSES - 1),
+                    )
+                dh_t = work.tile([P, PACK, P], F32, name="dh_t")
+                nc.scalar.activation(dh_t[:], acc[:].rearrange("c (q t) -> c t q", t=PACK), ACT.Copy, scale=gate_col[:, e : e + 1])
+                dh_ps = ps_tr.tile([P, PACK, C], F32, name="dh_ps")
+                for t in range(PACK):
+                    nc.tensor.transpose(dh_ps[:, t, :], dh_t[:, t, :], ident[:])
+                nc.vector.tensor_tensor(
+                    da3[:, x * C : (x + 1) * C, :], dh_ps[:].rearrange("p t c -> p c t"), sig[:, x * C : (x + 1) * C, :], ALU.mult
+                )
+            da = work.tile([P, 2, n * C, PACK], BF16, name="da", align_bytes=64)
+            nc.vector.scalar_tensor_tensor(da[:, 0], da3[:], -1.0, back[:], ALU.mult, ALU.mult)
+            nc.scalar.copy(da[:, 1], da3[:])
+            nc.vector.quantize_mx(
+                out=da_w[g][:].rearrange("p m j -> p (m j)").bitcast(FP8X4),
+                scales=da_s[g][:].rearrange("p m j -> p (m j)"),
+                in_=da[:].rearrange("p m j t -> p (m j t)"),
+            )
+            second_product([g], 0)
+        for kt in range(1, KT):
+            second_product([0, 1], kt)
+            second_product([2, 3, 4], kt)
+
+        for kt in range(KT):
+            first = work.tile([P, T], F32, name="first")
+            second = work.tile([P, T], F32, name="second")
+            nc.vector.tensor_copy(first[:], dx[kt][:].indirect(pos_t[0][:]))
+            nc.vector.tensor_copy(second[:], dx[kt][:].indirect(pos_t[1][:]))
+            total = work.tile([P, T], F32, name="total")
+            nc.vector.tensor_tensor(total[:], first[:], second[:], ALU.add)
+            nc.sync.dma_start(out[kt * P : (kt + 1) * P, :], total[:])

@@ -47,13 +47,11 @@ def tile_moe_bdx_glu_sigmoid_kernel(
         w2_s = keep.tile([P, E * PASSES, H], U8, name="w2_s", align_bytes=64)
         g_s1 = keep.tile([P, S], U8, name="g_s1", align_bytes=64)
         w13_s = [keep.tile([P, E, K], U8, name=f"w13_s{m}", align_bytes=64) for m in range(2)]
-        nc.vector.memset(dy_s[:].bitcast(I32), 0)
+        nc.gpsimd.memset(dy_s[:].bitcast(I32), 0)
         for q in range(4):
             nc.sync.dma_start(dy_s[32 * q : 32 * q + 8, :].bitcast(I32), dy_scales[:, 4 * q : 4 * q + 4, :].bitcast(I32))
         nc.vector.memset(w2_s[:].bitcast(I32), 0)
         nc.vector.memset(g_s1[:].bitcast(I32), 0)
-        for m in range(2):
-            nc.gpsimd.memset(w13_s[m][:].bitcast(I32), 0)
 
         warm = keep.tile([P, 8], F32, name="warm")
         nc.gpsimd.memset(warm[:], 0.0)
@@ -64,13 +62,14 @@ def tile_moe_bdx_glu_sigmoid_kernel(
 
         w2_rows = w2_scales.rearrange("e s (q r) i -> r q (e s) i", r=4)
         for r in range(4):
-            nc.scalar.dma_start(w2_s[r:P:32, :, :].bitcast(I32), w2_rows[r].bitcast(I32))
+            nc.sync.dma_start(w2_s[r:P:32, :, :].bitcast(I32), w2_rows[r].bitcast(I32))
 
         ident = keep.tile([P, P], F32, name="ident")
         make_identity(nc, ident[:])
         gate_rows = keep.tile([P, C], F32, name="gate_rows")
         nc.gpsimd.memset(gate_rows[:], 0.0)
-        nc.sync.dma_start(gate_rows[0:E, :], gate[0].rearrange("(e c) -> e c", c=C))
+        for m in range(2):
+            nc.vector.memset(w13_s[m][:].bitcast(I32), 0)
 
         w2_w, a1_t, a3_t = [], [], []
         a1_v = a1.rearrange("(p t) j -> p t j", t=PACK)
@@ -85,19 +84,23 @@ def tile_moe_bdx_glu_sigmoid_kernel(
             a3_t.append(keep.tile([P, PACK, W], F32, name=f"a3_t{u}"))
             nc.sync.dma_start(a1_t[u][:], a1_v[:, :, u * W : (u + 1) * W])
             nc.sync.dma_start(a3_t[u][:], a3_v[:, :, u * W : (u + 1) * W])
+            if u == 0:
+                nc.sync.dma_start(gate_rows[0:E, :], gate[0].rearrange("(e c) -> e c", c=C))
 
         for m, scales in enumerate((w1_scales, w3_scales)):
             rows = scales.rearrange("e s (q r) k -> r q (e s) k", r=4)
             for r in range(4):
                 nc.sync.dma_start(w13_s[m][r:P:32, :, :].bitcast(I32), rows[r].bitcast(I32))
         w13_w = {}
-        for kt in range(KT):
+        for k0, k1 in ((0, 1), (1, KT)):
             for m, words in enumerate((w1_words, w3_words)):
-                w13_w[m, kt] = keep.tile([P, E, 2 * P], U8, name=f"w13_w{m}{kt}", align_bytes=64)
+                part = keep.tile([P, E, 2 * P * (k1 - k0)], U8, name=f"w13_w{m}{k0}", align_bytes=64)
                 nc.sync.dma_start(
-                    w13_w[m, kt][:].bitcast(I32),
-                    words.rearrange("e s p b -> p (e s) b")[:, :, 2 * P * kt : 2 * P * (kt + 1)].bitcast(I32),
+                    part[:].bitcast(I32),
+                    words.rearrange("e s p b -> p (e s) b")[:, :, 2 * P * k0 : 2 * P * k1].bitcast(I32),
                 )
+                for kt in range(k0, k1):
+                    w13_w[m, kt] = part[:, :, 2 * P * (kt - k0) : 2 * P * (kt - k0 + 1)]
         pos_t = [keep.tile([P, T // LIST], U16, name=f"pos_t{r}") for r in range(2)]
         nc.sync.dma_start(pos_t[0][:], pos1)
         nc.sync.dma_start(pos_t[1][:], pos2)
@@ -112,7 +115,7 @@ def tile_moe_bdx_glu_sigmoid_kernel(
         gate_ps = ps_tr.tile([P, PACK, C], F32, name="dh_ps")
         nc.tensor.transpose(gate_ps[:, 0, :], gate_rows[:], ident[:])
         gate_col = keep.tile([P, E], F32, name="gate_col")
-        nc.scalar.copy(gate_col[:], gate_ps[:, 0, 0:E])
+        nc.scalar.activation(gate_col[:], gate_ps[:, 0, 0:E], ACT.Copy, scale=-1.0)
 
         for u in range(PAIRS):
             for o in range(PASSES):
@@ -146,11 +149,11 @@ def tile_moe_bdx_glu_sigmoid_kernel(
         for g, (e0, n) in enumerate(groups):
             u = e0 // PAIR
             cols = slice((e0 - PAIR * u) * C, (e0 - PAIR * u + n) * C)
-            sig = work.tile([P, n * C, PACK], F32, name="sig")
-            nc.scalar.activation(sig[:], a1_t[u][:, :, cols].rearrange("p t j -> p j t"), ACT.Sigmoid)
-            back = work.tile([P, n * C, PACK], F32, name="back")
-            nc.vector.scalar_tensor_tensor(back[:], sig[:], 1.0, a3_t[u][:, :, cols].rearrange("p t j -> p j t"), ALU.subtract, ALU.mult)
-            da3 = work.tile([P, n * C, PACK], F32, name="da3")
+            sig = work.tile([P, PACK, n * C], F32, name="sig")
+            nc.scalar.activation(sig[:], a1_t[u][:, :, cols], ACT.Sigmoid)
+            back = work.tile([P, PACK, n * C], F32, name="back")
+            nc.vector.scalar_tensor_tensor(back[:], sig[:], 1.0, a3_t[u][:, :, cols], ALU.subtract, ALU.mult)
+            da3 = work.tile([P, PACK, n * C], F32, name="da3")
             for x in range(n):
                 e = e0 + x
                 acc = ps_dh.tile([P, H], F32, name="acc")
@@ -170,11 +173,13 @@ def tile_moe_bdx_glu_sigmoid_kernel(
                 for t in range(PACK):
                     nc.tensor.transpose(dh_ps[:, t, :], dh_t[:, t, :], ident[:])
                 nc.vector.tensor_tensor(
-                    da3[:, x * C : (x + 1) * C, :], dh_ps[:].rearrange("p t c -> p c t"), sig[:, x * C : (x + 1) * C, :], ALU.mult
+                    da3[:, :, x * C : (x + 1) * C], dh_ps[:], sig[:, :, x * C : (x + 1) * C], ALU.mult
                 )
             da = work.tile([P, 2, n * C, PACK], BF16, name="da", align_bytes=64)
-            nc.vector.scalar_tensor_tensor(da[:, 0], da3[:], -1.0, back[:], ALU.mult, ALU.mult)
-            nc.scalar.copy(da[:, 1], da3[:])
+            woven = [da[:, m].rearrange("p (c i) t -> p c t i", i=2) for m in range(2)]
+            da3_pairs = da3[:].rearrange("p t (c i) -> p c t i", i=2)
+            nc.vector.tensor_tensor(woven[0], da3_pairs, back[:].rearrange("p t (c i) -> p c t i", i=2), ALU.mult)
+            nc.scalar.activation(woven[1], da3_pairs, ACT.Copy, scale=-1.0)
             nc.vector.quantize_mx(
                 out=da_w[g][:].rearrange("p m j -> p (m j)").bitcast(FP8X4),
                 scales=da_s[g][:].rearrange("p m j -> p (m j)"),
@@ -185,11 +190,23 @@ def tile_moe_bdx_glu_sigmoid_kernel(
             second_product([0, 1], kt)
             second_product([2, 3, 4], kt)
 
-        for kt in range(KT):
-            first = work.tile([P, T], F32, name="first")
-            second = work.tile([P, T], F32, name="second")
-            nc.vector.tensor_copy(first[:], dx[kt][:].indirect(pos_t[0][:]))
-            nc.vector.tensor_copy(second[:], dx[kt][:].indirect(pos_t[1][:]))
-            total = work.tile([P, T], F32, name="total")
-            nc.vector.tensor_tensor(total[:], first[:], second[:], ALU.add)
-            nc.sync.dma_start(out[kt * P : (kt + 1) * P, :], total[:])
+        pieces = [(0, 0, T), (1, 0, T), (2, 0, T // 2), (2, T // 2, T)]
+        fetched = {}
+
+        def fetch(i, r):
+            kt, t0, t1 = pieces[i]
+            fetched[i, r] = work.tile([P, t1 - t0], F32, name=f"fetched{r}")
+            nc.vector.tensor_copy(fetched[i, r][:], dx[kt][:].indirect(pos_t[r][:, t0 // LIST : t1 // LIST]))
+
+        def combine(i):
+            kt, t0, t1 = pieces[i]
+            total = work.tile([P, t1 - t0], F32, name="total")
+            nc.vector.tensor_tensor(total[:], fetched[i, 0][:], fetched[i, 1][:], ALU.add)
+            nc.sync.dma_start(out[kt * P : (kt + 1) * P, t0:t1], total[:])
+
+        for i in range(len(pieces)):
+            fetch(i, 0)
+            if i > 0:
+                combine(i - 1)
+            fetch(i, 1)
+        combine(len(pieces) - 1)

@@ -36,74 +36,88 @@ def tile_moe_bdx_glu_sigmoid_kernel(
     with ExitStack() as ctx:
         keep = ctx.enter_context(tc.tile_pool(name="keep", bufs=1))
         work = ctx.enter_context(tc.tile_pool(name="work", bufs=4))
-        ps_dh = ctx.enter_context(tc.psum_pool(name="ps_dh", bufs=2))
+        ps_dh = ctx.enter_context(tc.psum_pool(name="ps_dh", bufs=3))
         ps_tr = ctx.enter_context(tc.psum_pool(name="ps_tr", bufs=3))
-        ps_dx = ctx.enter_context(tc.psum_pool(name="ps_dx", bufs=3))
+        ps_dx = ctx.enter_context(tc.psum_pool(name="ps_dx", bufs=2))
 
         offs_t = keep.tile([P, S // LIST], U16, name="offs_t")
         nc.sync.dma_start(offs_t[:], offs)
 
         dy_s = keep.tile([P, T], U8, name="dy_s", align_bytes=64)
-        w2_s = keep.tile([P, E * PASSES, H], U8, name="w2_s", align_bytes=64)
-        g_s1 = keep.tile([P, S], U8, name="g_s1", align_bytes=64)
-        w13_s = [keep.tile([P, E, K], U8, name=f"w13_s{m}", align_bytes=64) for m in range(2)]
         nc.gpsimd.memset(dy_s[:].bitcast(I32), 0)
         for q in range(4):
             nc.sync.dma_start(dy_s[32 * q : 32 * q + 8, :].bitcast(I32), dy_scales[:, 4 * q : 4 * q + 4, :].bitcast(I32))
-        nc.vector.memset(w2_s[:].bitcast(I32), 0)
-        nc.vector.memset(g_s1[:].bitcast(I32), 0)
+        dy_w = keep.tile([P, PASSES, T], U32, name="dy_w", align_bytes=64)
+        nc.sync.dma_start(dy_w[:].bitcast(I32), dy_words.rearrange("o p t d -> p o (t d)").bitcast(I32))
+
+        w2_s = [keep.tile([P, E // 2 * PASSES, H], U8, name=f"w2_s{h}", align_bytes=64) for h in range(2)]
+        g_s1 = keep.tile([P, S], U8, name="g_s1", align_bytes=64)
+        k_parts = ((0, 1), (1, KT))
+        w13_s = {
+            (m, k0): keep.tile([P, E, (k1 - k0) * P], U8, name=f"w13_s{m}{k0}", align_bytes=64)
+            for k0, k1 in k_parts for m in range(2)
+        }
+        for plane in (w2_s[0], g_s1):
+            nc.vector.memset(plane[:].bitcast(I32), 0)
 
         warm = keep.tile([P, 8], F32, name="warm")
         nc.gpsimd.memset(warm[:], 0.0)
         nc.scalar.activation(warm[:], warm[:], ACT.Sigmoid)
-        dy_w = [keep.tile([P, T], U32, name=f"dy_w{o}", align_bytes=64) for o in range(PASSES)]
-        for o in range(PASSES):
-            nc.sync.dma_start(dy_w[o][:].bitcast(I32), dy_words[o].rearrange("p t d -> p (t d)").bitcast(I32))
-
-        w2_rows = w2_scales.rearrange("e s (q r) i -> r q (e s) i", r=4)
-        for r in range(4):
-            nc.sync.dma_start(w2_s[r:P:32, :, :].bitcast(I32), w2_rows[r].bitcast(I32))
-
         ident = keep.tile([P, P], F32, name="ident")
         make_identity(nc, ident[:])
         gate_rows = keep.tile([P, C], F32, name="gate_rows")
         nc.gpsimd.memset(gate_rows[:], 0.0)
-        for m in range(2):
-            nc.vector.memset(w13_s[m][:].bitcast(I32), 0)
+        for plane in (w2_s[1], *w13_s.values()):
+            nc.gpsimd.memset(plane[:].bitcast(I32), 0)
 
-        w2_w, a1_t, a3_t = [], [], []
-        a1_v = a1.rearrange("(p t) j -> p t j", t=PACK)
-        a3_v = a3.rearrange("(p t) j -> p t j", t=PACK)
-        for u in range(PAIRS):
-            w2_w.append(keep.tile([P, PAIR * PASSES, 2 * H], U8, name=f"w2_w{u}", align_bytes=64))
-            nc.sync.dma_start(
-                w2_w[u][:].bitcast(I32),
-                w2_words[PAIR * u : PAIR * (u + 1)].rearrange("e s p b -> p (e s) b").bitcast(I32),
-            )
-            a1_t.append(keep.tile([P, PACK, W], F32, name=f"a1_t{u}"))
-            a3_t.append(keep.tile([P, PACK, W], F32, name=f"a3_t{u}"))
-            nc.sync.dma_start(a1_t[u][:], a1_v[:, :, u * W : (u + 1) * W])
-            nc.sync.dma_start(a3_t[u][:], a3_v[:, :, u * W : (u + 1) * W])
-            if u == 0:
-                nc.sync.dma_start(gate_rows[0:E, :], gate[0].rearrange("(e c) -> e c", c=C))
-
-        for m, scales in enumerate((w1_scales, w3_scales)):
-            rows = scales.rearrange("e s (q r) k -> r q (e s) k", r=4)
+        def load_w2_scales(h):
+            rows = w2_scales[h * E // 2 : (h + 1) * E // 2].rearrange("e s (q r) i -> r q (e s) i", r=4)
             for r in range(4):
-                nc.sync.dma_start(w13_s[m][r:P:32, :, :].bitcast(I32), rows[r].bitcast(I32))
+                nc.sync.dma_start(w2_s[h][r:P:32, :, :].bitcast(I32), rows[r].bitcast(I32))
+
+        def load_w13_scales(m, part, r):
+            k0, k1 = k_parts[part]
+            rows = (w1_scales, w3_scales)[m].rearrange("e s (q r) k -> r q (e s) k", r=4)
+            nc.sync.dma_start(w13_s[m, k0][r:P:32, :, :].bitcast(I32), rows[r][:, :, k0 * P : k1 * P].bitcast(I32))
+
         w13_w = {}
-        for k0, k1 in ((0, 1), (1, KT)):
-            for m, words in enumerate((w1_words, w3_words)):
-                part = keep.tile([P, E, 2 * P * (k1 - k0)], U8, name=f"w13_w{m}{k0}", align_bytes=64)
-                nc.sync.dma_start(
-                    part[:].bitcast(I32),
-                    words.rearrange("e s p b -> p (e s) b")[:, :, 2 * P * k0 : 2 * P * k1].bitcast(I32),
-                )
-                for kt in range(k0, k1):
-                    w13_w[m, kt] = part[:, :, 2 * P * (kt - k0) : 2 * P * (kt - k0 + 1)]
+
+        def load_w13_words(m, part):
+            k0, k1 = k_parts[part]
+            w13_w[m, k0] = keep.tile([P, E, 2 * P * (k1 - k0)], U8, name=f"w13_w{m}{k0}", align_bytes=64)
+            nc.sync.dma_start(
+                w13_w[m, k0][:].bitcast(I32),
+                (w1_words, w3_words)[m].rearrange("e s p b -> p (e s) b")[:, :, 2 * P * k0 : 2 * P * k1].bitcast(I32),
+            )
+
+        w2_w = [keep.tile([P, PAIR * PASSES, 2 * H], U8, name=f"w2_w{u}", align_bytes=64) for u in range(PAIRS)]
+        a1_t = [keep.tile([P, PACK, W], F32, name=f"a1_t{u}") for u in range(PAIRS)]
+        a3_t = [keep.tile([P, PACK, W], F32, name=f"a3_t{u}") for u in range(PAIRS)]
+        big = []
+        for u in range(PAIRS):
+            big.append((w2_w[u][:].bitcast(I32), w2_words[PAIR * u : PAIR * (u + 1)].rearrange("e s p b -> p (e s) b").bitcast(I32)))
+            big.append((a1_t[u][:], a1.rearrange("(p t) j -> p t j", t=PACK)[:, :, u * W : (u + 1) * W]))
+            big.append((a3_t[u][:], a3.rearrange("(p t) j -> p t j", t=PACK)[:, :, u * W : (u + 1) * W]))
+        small = [(m, r) for m in range(2) for r in range(4)]
+        load_w2_scales(0)
+        for i, (dst, src) in enumerate(big):
+            nc.sync.dma_start(dst, src)
+            if i == 2:
+                nc.sync.dma_start(gate_rows[0:E, :], gate[0].rearrange("(e c) -> e c", c=C))
+            if i == 5:
+                load_w2_scales(1)
+            if 6 <= i < 10:
+                for m, r in small[2 * (i - 6) : 2 * (i - 5)]:
+                    load_w13_scales(m, 0, r)
         pos_t = [keep.tile([P, T // LIST], U16, name=f"pos_t{r}") for r in range(2)]
+        for m in range(2):
+            load_w13_words(m, 0)
         nc.sync.dma_start(pos_t[0][:], pos1)
         nc.sync.dma_start(pos_t[1][:], pos2)
+        for m in range(2):
+            load_w13_words(m, 1)
+            for r in range(4):
+                load_w13_scales(m, 1, r)
 
         g_s = keep.tile([P, S], U8, name="g_s", align_bytes=64)
         g_w = [keep.tile([P, S], U32, name=f"g_w{o}", align_bytes=64) for o in range(PASSES)]
@@ -119,76 +133,101 @@ def tile_moe_bdx_glu_sigmoid_kernel(
 
         for u in range(PAIRS):
             for o in range(PASSES):
-                nc.vector.tensor_copy(g_w[o][:, u * W : (u + 1) * W], dy_w[o][:].indirect(offs_t[:, u * W // LIST : (u + 1) * W // LIST]))
+                nc.vector.tensor_copy(g_w[o][:, u * W : (u + 1) * W], dy_w[:, o, :].indirect(offs_t[:, u * W // LIST : (u + 1) * W // LIST]))
 
         dx = [keep.tile([P, S], F32, name=f"dx{kt}") for kt in range(KT)]
-        groups = [(0, 2), (2, 2), (4, 2), (6, 1), (7, 1)]
-        da_w = [keep.tile([P, 2, n * C], U32, name=f"da_w{e0}", align_bytes=64) for e0, n in groups]
-        da_s = [keep.tile([P, 2, n * C], U8, name=f"da_s{e0}", align_bytes=64) for e0, n in groups]
+        groups = [(0, 2), (2, 4), (4, 6), (6, 7), (7, 8)]
+        group_of = {e: g for g, (e0, e1) in enumerate(groups) for e in range(e0, e1)}
+        da_w = [keep.tile([P, 2, (e1 - e0) * C], U32, name=f"da_w{e0}", align_bytes=64) for e0, e1 in groups]
+        da_s = [keep.tile([P, 2, (e1 - e0) * C], U8, name=f"da_s{e0}", align_bytes=64) for e0, e1 in groups]
+        sig, back, da3, da = {}, {}, {}, {}
 
-        def second_product(gs, kt):
-            e_first = groups[gs[0]][0]
-            width = sum(groups[g][1] for g in gs) * C
-            acc = ps_dx.tile([P, width], F32, name="dx_ps")
-            for g in gs:
-                e0, n = groups[g]
-                for x in range(n):
-                    e = e0 + x
-                    for m in range(2):
-                        nc.tensor.matmul_mx(
-                            acc[:, (e - e_first) * C : (e - e_first + 1) * C],
-                            lhsT=w13_w[m, kt][:, e, :].bitcast(FP4X4),
-                            lhsT_scale=w13_s[m][:, e, kt * P : (kt + 1) * P],
-                            rhs=da_w[g][:, m, x * C : (x + 1) * C].bitcast(FP8X4),
-                            rhs_scale=da_s[g][:, m, x * C : (x + 1) * C],
-                            start=(m == 0),
-                            stop=(m == 1),
-                        )
-            nc.scalar.copy(dx[kt][:, e_first * C : e_first * C + width], acc[:])
-
-        for g, (e0, n) in enumerate(groups):
+        def saved(tiles, e0, e1):
             u = e0 // PAIR
-            cols = slice((e0 - PAIR * u) * C, (e0 - PAIR * u + n) * C)
-            sig = work.tile([P, PACK, n * C], F32, name="sig")
-            nc.scalar.activation(sig[:], a1_t[u][:, :, cols], ACT.Sigmoid)
-            back = work.tile([P, PACK, n * C], F32, name="back")
-            nc.vector.scalar_tensor_tensor(back[:], sig[:], 1.0, a3_t[u][:, :, cols], ALU.subtract, ALU.mult)
-            da3 = work.tile([P, PACK, n * C], F32, name="da3")
-            for x in range(n):
-                e = e0 + x
-                acc = ps_dh.tile([P, H], F32, name="acc")
-                for o in range(PASSES):
-                    nc.tensor.matmul_mx(
-                        acc[:],
-                        lhsT=g_w[o][:, e * C : (e + 1) * C].bitcast(FP8X4),
-                        lhsT_scale=g_sc[o][:, e * C : (e + 1) * C],
-                        rhs=w2_w[u][:, (e % PAIR) * PASSES + o, :].bitcast(FP4X4),
-                        rhs_scale=w2_s[:, e * PASSES + o, :],
-                        start=(o == 0),
-                        stop=(o == PASSES - 1),
-                    )
-                dh_t = work.tile([P, PACK, P], F32, name="dh_t")
-                nc.scalar.activation(dh_t[:], acc[:].rearrange("c (q t) -> c t q", t=PACK), ACT.Copy, scale=gate_col[:, e : e + 1])
-                dh_ps = ps_tr.tile([P, PACK, C], F32, name="dh_ps")
-                for t in range(PACK):
-                    nc.tensor.transpose(dh_ps[:, t, :], dh_t[:, t, :], ident[:])
-                nc.vector.tensor_tensor(
-                    da3[:, :, x * C : (x + 1) * C], dh_ps[:], sig[:, :, x * C : (x + 1) * C], ALU.mult
+            return tiles[u][:, :, (e0 - u * PAIR) * C : (e1 - u * PAIR) * C]
+
+        def pairs_of(planes):
+            return planes.rearrange("p t (c i) -> p c t i", i=2)
+
+        def woven(words):
+            return words.rearrange("p (c i) t -> p c t i", i=2)
+
+        def make_back(g):
+            e0, e1 = groups[g]
+            sig[g] = work.tile([P, PACK, (e1 - e0) * C], F32, name="sig")
+            nc.scalar.activation(sig[g][:], saved(a1_t, e0, e1), ACT.Sigmoid)
+            back[g] = work.tile([P, PACK, (e1 - e0) * C], F32, name="back")
+            nc.vector.scalar_tensor_tensor(back[g][:], sig[g][:], 1.0, saved(a3_t, e0, e1), ALU.subtract, ALU.mult)
+            da3[g] = work.tile([P, PACK, (e1 - e0) * C], F32, name="da3")
+            da[g] = work.tile([P, 2, (e1 - e0) * C, PACK], BF16, name="da", align_bytes=64)
+
+        def make_da3(e):
+            g = group_of[e]
+            cols = slice((e - groups[g][0]) * C, (e - groups[g][0] + 1) * C)
+            acc = ps_dh.tile([P, H], F32, name="acc")
+            for o in range(PASSES):
+                nc.tensor.matmul_mx(
+                    acc[:],
+                    lhsT=g_w[o][:, e * C : (e + 1) * C].bitcast(FP8X4),
+                    lhsT_scale=g_sc[o][:, e * C : (e + 1) * C],
+                    rhs=w2_w[e // PAIR][:, e % PAIR * PASSES + o, :].bitcast(FP4X4),
+                    rhs_scale=w2_s[e // (E // 2)][:, e % (E // 2) * PASSES + o, :],
+                    start=(o == 0),
+                    stop=(o == PASSES - 1),
                 )
-            da = work.tile([P, 2, n * C, PACK], BF16, name="da", align_bytes=64)
-            woven = [da[:, m].rearrange("p (c i) t -> p c t i", i=2) for m in range(2)]
-            da3_pairs = da3[:].rearrange("p t (c i) -> p c t i", i=2)
-            nc.vector.tensor_tensor(woven[0], da3_pairs, back[:].rearrange("p t (c i) -> p c t i", i=2), ALU.mult)
-            nc.scalar.activation(woven[1], da3_pairs, ACT.Copy, scale=-1.0)
+            dh_t = work.tile([P, PACK, P], F32, name="dh_t")
+            nc.scalar.activation(dh_t[:], acc[:].rearrange("c (q t) -> c t q", t=PACK), ACT.Copy, scale=gate_col[:, e : e + 1])
+            dh_ps = ps_tr.tile([P, PACK, C], F32, name="dh_ps")
+            for t in range(PACK):
+                nc.tensor.transpose(dh_ps[:, t, :], dh_t[:, t, :], ident[:])
+            nc.vector.tensor_tensor(da3[g][:, :, cols], dh_ps[:], sig[g][:, :, cols], ALU.mult)
+            nc.scalar.activation(woven(da[g][:, 1, cols]), pairs_of(da3[g][:, :, cols]), ACT.Copy, scale=-1.0)
+
+        def make_da1(g):
+            nc.vector.tensor_tensor(woven(da[g][:, 0]), pairs_of(da3[g][:]), pairs_of(back[g][:]), ALU.mult)
+
+        def quantise(g):
             nc.vector.quantize_mx(
                 out=da_w[g][:].rearrange("p m j -> p (m j)").bitcast(FP8X4),
                 scales=da_s[g][:].rearrange("p m j -> p (m j)"),
-                in_=da[:].rearrange("p m j t -> p (m j t)"),
+                in_=da[g][:].rearrange("p m j t -> p (m j t)"),
             )
-            second_product([g], 0)
+
+        def second_product(e0, e1, kt):
+            k0 = min(kt, 1)
+            acc = ps_dx.tile([P, (e1 - e0) * C], F32, name="dx_ps")
+            for e in range(e0, e1):
+                g = group_of[e]
+                cols = slice((e - groups[g][0]) * C, (e - groups[g][0] + 1) * C)
+                for m in range(2):
+                    nc.tensor.matmul_mx(
+                        acc[:, (e - e0) * C : (e - e0 + 1) * C],
+                        lhsT=w13_w[m, k0][:, e, 2 * P * (kt - k0) : 2 * P * (kt - k0 + 1)].bitcast(FP4X4),
+                        lhsT_scale=w13_s[m, k0][:, e, P * (kt - k0) : P * (kt - k0 + 1)],
+                        rhs=da_w[g][:, m, cols].bitcast(FP8X4),
+                        rhs_scale=da_s[g][:, m, cols],
+                        start=(m == 0),
+                        stop=(m == 1),
+                    )
+            nc.scalar.copy(dx[kt][:, e0 * C : e1 * C], acc[:])
+
+        for g in range(len(groups) + 1):
+            experts = range(*groups[g]) if g < len(groups) else []
+            if experts:
+                make_back(g)
+            if g > 0:
+                make_da1(g - 1)
+            for e in experts[:1]:
+                make_da3(e)
+            if g > 0:
+                quantise(g - 1)
+            for e in experts[1:]:
+                make_da3(e)
+        for e0, e1 in ((0, 4), (4, 6), (6, 7), (7, 8)):
+            second_product(e0, e1, 0)
         for kt in range(1, KT):
-            second_product([0, 1], kt)
-            second_product([2, 3, 4], kt)
+            second_product(0, 4, kt)
+            second_product(4, 8, kt)
 
         pieces = [(0, 0, T), (1, 0, T), (2, 0, T // 2), (2, T // 2, T)]
         fetched = {}

@@ -36,9 +36,7 @@ def tile_moe_bdx_glu_sigmoid_kernel(
     with ExitStack() as ctx:
         keep = ctx.enter_context(tc.tile_pool(name="keep", bufs=1))
         work = ctx.enter_context(tc.tile_pool(name="work", bufs=4))
-        ps_dh = ctx.enter_context(tc.psum_pool(name="ps_dh", bufs=3))
-        ps_tr = ctx.enter_context(tc.psum_pool(name="ps_tr", bufs=3))
-        ps_dx = ctx.enter_context(tc.psum_pool(name="ps_dx", bufs=2))
+        psum = ctx.enter_context(tc.psum_pool(name="psum", bufs=1))
 
         offs_t = keep.tile([P, S // LIST], U16, name="offs_t")
         nc.sync.dma_start(offs_t[:], offs)
@@ -67,18 +65,16 @@ def tile_moe_bdx_glu_sigmoid_kernel(
         make_identity(nc, ident[:])
         gate_rows = keep.tile([P, C], F32, name="gate_rows")
         nc.gpsimd.memset(gate_rows[:], 0.0)
-        for plane in (w2_s[1], *w13_s.values()):
-            nc.gpsimd.memset(plane[:].bitcast(I32), 0)
 
-        def load_w2_scales(h):
+        def load_w2_scales(queue, h):
             rows = w2_scales[h * E // 2 : (h + 1) * E // 2].rearrange("e s (q r) i -> r q (e s) i", r=4)
             for r in range(4):
-                nc.sync.dma_start(w2_s[h][r:P:32, :, :].bitcast(I32), rows[r].bitcast(I32))
+                queue.dma_start(w2_s[h][r:P:32, :, :].bitcast(I32), rows[r].bitcast(I32))
 
-        def load_w13_scales(m, part, r):
+        def load_w13_scales(queue, m, part, r):
             k0, k1 = k_parts[part]
             rows = (w1_scales, w3_scales)[m].rearrange("e s (q r) k -> r q (e s) k", r=4)
-            nc.sync.dma_start(w13_s[m, k0][r:P:32, :, :].bitcast(I32), rows[r][:, :, k0 * P : k1 * P].bitcast(I32))
+            queue.dma_start(w13_s[m, k0][r:P:32, :, :].bitcast(I32), rows[r][:, :, k0 * P : k1 * P].bitcast(I32))
 
         w13_w = {}
 
@@ -98,17 +94,19 @@ def tile_moe_bdx_glu_sigmoid_kernel(
             big.append((w2_w[u][:].bitcast(I32), w2_words[PAIR * u : PAIR * (u + 1)].rearrange("e s p b -> p (e s) b").bitcast(I32)))
             big.append((a1_t[u][:], a1.rearrange("(p t) j -> p t j", t=PACK)[:, :, u * W : (u + 1) * W]))
             big.append((a3_t[u][:], a3.rearrange("(p t) j -> p t j", t=PACK)[:, :, u * W : (u + 1) * W]))
-        small = [(m, r) for m in range(2) for r in range(4)]
-        load_w2_scales(0)
+        load_w2_scales(nc.sync, 0)
+        nc.gpsimd.memset(w2_s[1][:].bitcast(I32), 0)
+        load_w2_scales(nc.gpsimd, 1)
+        for m in range(2):
+            nc.gpsimd.memset(w13_s[m, 0][:].bitcast(I32), 0)
+            for r in range(4):
+                load_w13_scales(nc.gpsimd, m, 0, r)
+        for m in range(2):
+            nc.gpsimd.memset(w13_s[m, 1][:].bitcast(I32), 0)
         for i, (dst, src) in enumerate(big):
             nc.sync.dma_start(dst, src)
             if i == 2:
                 nc.sync.dma_start(gate_rows[0:E, :], gate[0].rearrange("(e c) -> e c", c=C))
-            if i == 5:
-                load_w2_scales(1)
-            if 6 <= i < 10:
-                for m, r in small[2 * (i - 6) : 2 * (i - 5)]:
-                    load_w13_scales(m, 0, r)
         pos_t = [keep.tile([P, T // LIST], U16, name=f"pos_t{r}") for r in range(2)]
         for m in range(2):
             load_w13_words(m, 0)
@@ -117,23 +115,24 @@ def tile_moe_bdx_glu_sigmoid_kernel(
         for m in range(2):
             load_w13_words(m, 1)
             for r in range(4):
-                load_w13_scales(m, 1, r)
+                load_w13_scales(nc.sync, m, 1, r)
 
         g_s = keep.tile([P, S], U8, name="g_s", align_bytes=64)
         g_w = [keep.tile([P, S], U32, name=f"g_w{o}", align_bytes=64) for o in range(PASSES)]
-        for u in range(PAIRS):
-            nc.vector.tensor_copy(g_s[:, u * W : (u + 1) * W], dy_s[:].indirect(offs_t[:, u * W // LIST : (u + 1) * W // LIST]))
+        cuts = ((0, 256), (256, 640), (640, S))
+        for j0, j1 in cuts:
+            nc.vector.tensor_copy(g_s[:, j0:j1], dy_s[:].indirect(offs_t[:, j0 // LIST : j1 // LIST]))
         nc.scalar.dma_start(g_s1[0:100, :].bitcast(I32), g_s[4:104, :].bitcast(I32))
         g_sc = [g_s, g_s1]
 
-        gate_ps = ps_tr.tile([P, PACK, C], F32, name="dh_ps")
+        gate_ps = psum.tile([P, PACK, C], F32, name="turn3")
         nc.tensor.transpose(gate_ps[:, 0, :], gate_rows[:], ident[:])
         gate_col = keep.tile([P, E], F32, name="gate_col")
         nc.scalar.activation(gate_col[:], gate_ps[:, 0, 0:E], ACT.Copy, scale=-1.0)
 
-        for u in range(PAIRS):
+        for j0, j1 in cuts:
             for o in range(PASSES):
-                nc.vector.tensor_copy(g_w[o][:, u * W : (u + 1) * W], dy_w[:, o, :].indirect(offs_t[:, u * W // LIST : (u + 1) * W // LIST]))
+                nc.vector.tensor_copy(g_w[o][:, j0:j1], dy_w[:, o, :].indirect(offs_t[:, j0 // LIST : j1 // LIST]))
 
         dx = [keep.tile([P, S], F32, name=f"dx{kt}") for kt in range(KT)]
         groups = [(0, 2), (2, 4), (4, 6), (6, 7), (7, 8)]
@@ -164,7 +163,7 @@ def tile_moe_bdx_glu_sigmoid_kernel(
         def make_da3(e):
             g = group_of[e]
             cols = slice((e - groups[g][0]) * C, (e - groups[g][0] + 1) * C)
-            acc = ps_dh.tile([P, H], F32, name="acc")
+            acc = psum.tile([P, H], F32, name=f"acc{e % 4}")
             for o in range(PASSES):
                 nc.tensor.matmul_mx(
                     acc[:],
@@ -177,7 +176,7 @@ def tile_moe_bdx_glu_sigmoid_kernel(
                 )
             dh_t = work.tile([P, PACK, P], F32, name="dh_t")
             nc.scalar.activation(dh_t[:], acc[:].rearrange("c (q t) -> c t q", t=PACK), ACT.Copy, scale=gate_col[:, e : e + 1])
-            dh_ps = ps_tr.tile([P, PACK, C], F32, name="dh_ps")
+            dh_ps = psum.tile([P, PACK, C], F32, name=f"turn{e % 4}")
             for t in range(PACK):
                 nc.tensor.transpose(dh_ps[:, t, :], dh_t[:, t, :], ident[:])
             nc.vector.tensor_tensor(da3[g][:, :, cols], dh_ps[:], sig[g][:, :, cols], ALU.mult)
@@ -193,9 +192,9 @@ def tile_moe_bdx_glu_sigmoid_kernel(
                 in_=da[g][:].rearrange("p m j t -> p (m j t)"),
             )
 
-        def second_product(e0, e1, kt):
+        def second_product(e0, e1, kt, bank):
             k0 = min(kt, 1)
-            acc = ps_dx.tile([P, (e1 - e0) * C], F32, name="dx_ps")
+            acc = psum.tile([P, (e1 - e0) * C], F32, name=bank)
             for e in range(e0, e1):
                 g = group_of[e]
                 cols = slice((e - groups[g][0]) * C, (e - groups[g][0] + 1) * C)
@@ -223,11 +222,11 @@ def tile_moe_bdx_glu_sigmoid_kernel(
                 quantise(g - 1)
             for e in experts[1:]:
                 make_da3(e)
-        for e0, e1 in ((0, 4), (4, 6), (6, 7), (7, 8)):
-            second_product(e0, e1, 0)
+        for e0, e1, bank in ((0, 4, "acc3"), (4, 6, "acc2"), (6, 7, "acc1"), (7, 8, "acc0")):
+            second_product(e0, e1, 0, bank)
         for kt in range(1, KT):
-            second_product(0, 4, kt)
-            second_product(4, 8, kt)
+            second_product(0, 4, kt, f"turn{2 * kt - 2}")
+            second_product(4, 8, kt, f"turn{2 * kt - 1}")
 
         pieces = [(0, 0, T), (1, 0, T), (2, 0, T // 2), (2, T // 2, T)]
         fetched = {}
@@ -240,7 +239,8 @@ def tile_moe_bdx_glu_sigmoid_kernel(
         def combine(i):
             kt, t0, t1 = pieces[i]
             total = work.tile([P, t1 - t0], F32, name="total")
-            nc.vector.tensor_tensor(total[:], fetched[i, 0][:], fetched[i, 1][:], ALU.add)
+            adder = nc.vector if i == len(pieces) - 1 else nc.gpsimd
+            adder.tensor_tensor(total[:], fetched[i, 0][:], fetched[i, 1][:], ALU.add)
             nc.sync.dma_start(out[kt * P : (kt + 1) * P, t0:t1], total[:])
 
         for i in range(len(pieces)):

@@ -26,6 +26,7 @@ PAIR = 2
 PAIRS = E // PAIR
 W = PAIR * C
 LIST = 16
+BANK = 2048
 
 
 def tile_moe_bdx_glu_sigmoid_kernel(
@@ -50,32 +51,26 @@ def tile_moe_bdx_glu_sigmoid_kernel(
 
         w2_s = [keep.tile([P, E // 2 * PASSES, H], U8, name=f"w2_s{h}", align_bytes=64) for h in range(2)]
         g_s1 = keep.tile([P, S], U8, name="g_s1", align_bytes=64)
-        k_parts = ((0, 1), (1, KT))
-        w13_s = {
-            (m, k0): keep.tile([P, E, (k1 - k0) * P], U8, name=f"w13_s{m}{k0}", align_bytes=64)
-            for k0, k1 in k_parts for m in range(2)
-        }
-        for plane in (w2_s[0], g_s1):
+        w13_s = [keep.tile([P, E, K], U8, name=f"w13_s{m}", align_bytes=64) for m in range(2)]
+        for plane in (w2_s[0], g_s1, w2_s[1]):
             nc.vector.memset(plane[:].bitcast(I32), 0)
 
         warm = keep.tile([P, 8], F32, name="warm")
         nc.gpsimd.memset(warm[:], 0.0)
         nc.scalar.activation(warm[:], warm[:], ACT.Sigmoid)
-        ident = keep.tile([P, P], F32, name="ident")
-        make_identity(nc, ident[:])
         gate_rows = keep.tile([P, C], F32, name="gate_rows")
         nc.gpsimd.memset(gate_rows[:], 0.0)
+        ident = keep.tile([P, P], F32, name="ident")
+        make_identity(nc, ident[:])
+        for plane in w13_s:
+            nc.gpsimd.memset(plane[:].bitcast(I32), 0)
 
-        def load_w2_scales(queue, h):
-            rows = w2_scales[h * E // 2 : (h + 1) * E // 2].rearrange("e s (q r) i -> r q (e s) i", r=4)
+        def load_scales(plane, rows):
+            by_row = rows.rearrange("e s (q r) i -> r q (e s) i", r=4)
             for r in range(4):
-                queue.dma_start(w2_s[h][r:P:32, :, :].bitcast(I32), rows[r].bitcast(I32))
+                nc.sync.dma_start(plane[r:P:32, :, :].bitcast(I32), by_row[r].bitcast(I32))
 
-        def load_w13_scales(queue, m, part, r):
-            k0, k1 = k_parts[part]
-            rows = (w1_scales, w3_scales)[m].rearrange("e s (q r) k -> r q (e s) k", r=4)
-            queue.dma_start(w13_s[m, k0][r:P:32, :, :].bitcast(I32), rows[r][:, :, k0 * P : k1 * P].bitcast(I32))
-
+        k_parts = ((0, 1), (1, KT))
         w13_w = {}
 
         def load_w13_words(m, part):
@@ -89,43 +84,36 @@ def tile_moe_bdx_glu_sigmoid_kernel(
         w2_w = [keep.tile([P, PAIR * PASSES, 2 * H], U8, name=f"w2_w{u}", align_bytes=64) for u in range(PAIRS)]
         a1_t = [keep.tile([P, PACK, W], F32, name=f"a1_t{u}") for u in range(PAIRS)]
         a3_t = [keep.tile([P, PACK, W], F32, name=f"a3_t{u}") for u in range(PAIRS)]
-        big = []
         for u in range(PAIRS):
-            big.append((w2_w[u][:].bitcast(I32), w2_words[PAIR * u : PAIR * (u + 1)].rearrange("e s p b -> p (e s) b").bitcast(I32)))
-            big.append((a1_t[u][:], a1.rearrange("(p t) j -> p t j", t=PACK)[:, :, u * W : (u + 1) * W]))
-            big.append((a3_t[u][:], a3.rearrange("(p t) j -> p t j", t=PACK)[:, :, u * W : (u + 1) * W]))
-        load_w2_scales(nc.sync, 0)
-        nc.gpsimd.memset(w2_s[1][:].bitcast(I32), 0)
-        load_w2_scales(nc.gpsimd, 1)
-        for m in range(2):
-            nc.gpsimd.memset(w13_s[m, 0][:].bitcast(I32), 0)
-            for r in range(4):
-                load_w13_scales(nc.gpsimd, m, 0, r)
-        for m in range(2):
-            nc.gpsimd.memset(w13_s[m, 1][:].bitcast(I32), 0)
-        for i, (dst, src) in enumerate(big):
-            nc.sync.dma_start(dst, src)
-            if i == 2:
+            if u == 0:
+                nc.sync.dma_start(a1_t[u][:], a1.rearrange("(p t) j -> p t j", t=PACK)[:, :, u * W : (u + 1) * W])
+            nc.sync.dma_start(w2_w[u][:].bitcast(I32), w2_words[PAIR * u : PAIR * (u + 1)].rearrange("e s p b -> p (e s) b").bitcast(I32))
+            if u % 2 == 0:
+                load_scales(w2_s[u // 2], w2_scales[PAIR * u : PAIR * (u + 2)])
+            if u > 0:
+                nc.sync.dma_start(a1_t[u][:], a1.rearrange("(p t) j -> p t j", t=PACK)[:, :, u * W : (u + 1) * W])
+            else:
                 nc.sync.dma_start(gate_rows[0:E, :], gate[0].rearrange("(e c) -> e c", c=C))
-        pos_t = [keep.tile([P, T // LIST], U16, name=f"pos_t{r}") for r in range(2)]
+            nc.sync.dma_start(a3_t[u][:], a3.rearrange("(p t) j -> p t j", t=PACK)[:, :, u * W : (u + 1) * W])
         for m in range(2):
+            load_scales(w13_s[m], (w1_scales, w3_scales)[m])
             load_w13_words(m, 0)
+        pos_t = [keep.tile([P, T // LIST], U16, name=f"pos_t{r}") for r in range(2)]
         nc.sync.dma_start(pos_t[0][:], pos1)
         nc.sync.dma_start(pos_t[1][:], pos2)
         for m in range(2):
             load_w13_words(m, 1)
-            for r in range(4):
-                load_w13_scales(nc.sync, m, 1, r)
 
         g_s = keep.tile([P, S], U8, name="g_s", align_bytes=64)
         g_w = [keep.tile([P, S], U32, name=f"g_w{o}", align_bytes=64) for o in range(PASSES)]
         cuts = ((0, 256), (256, 640), (640, S))
         for j0, j1 in cuts:
             nc.vector.tensor_copy(g_s[:, j0:j1], dy_s[:].indirect(offs_t[:, j0 // LIST : j1 // LIST]))
-        nc.scalar.dma_start(g_s1[0:100, :].bitcast(I32), g_s[4:104, :].bitcast(I32))
+        for j0, j1 in ((0, W), (W, S)):
+            nc.scalar.dma_start(g_s1[0:100, j0:j1].bitcast(I32), g_s[4:104, j0:j1].bitcast(I32))
         g_sc = [g_s, g_s1]
 
-        gate_ps = psum.tile([P, PACK, C], F32, name="turn3")
+        gate_ps = psum.tile([P, PACK, C], F32, name="bank7", offset=7 * BANK)
         nc.tensor.transpose(gate_ps[:, 0, :], gate_rows[:], ident[:])
         gate_col = keep.tile([P, E], F32, name="gate_col")
         nc.scalar.activation(gate_col[:], gate_ps[:, 0, 0:E], ACT.Copy, scale=-1.0)
@@ -139,7 +127,7 @@ def tile_moe_bdx_glu_sigmoid_kernel(
         group_of = {e: g for g, (e0, e1) in enumerate(groups) for e in range(e0, e1)}
         da_w = [keep.tile([P, 2, (e1 - e0) * C], U32, name=f"da_w{e0}", align_bytes=64) for e0, e1 in groups]
         da_s = [keep.tile([P, 2, (e1 - e0) * C], U8, name=f"da_s{e0}", align_bytes=64) for e0, e1 in groups]
-        sig, back, da3, da = {}, {}, {}, {}
+        sig, off_sq, slope, da, dh_ps = {}, {}, {}, {}, {}
 
         def saved(tiles, e0, e1):
             u = e0 // PAIR
@@ -151,19 +139,21 @@ def tile_moe_bdx_glu_sigmoid_kernel(
         def woven(words):
             return words.rearrange("p (c i) t -> p c t i", i=2)
 
-        def make_back(g):
+        def columns(e):
+            e0 = groups[group_of[e]][0]
+            return slice((e - e0) * C, (e - e0 + 1) * C)
+
+        def make_sigmoid(g):
             e0, e1 = groups[g]
-            sig[g] = work.tile([P, PACK, (e1 - e0) * C], F32, name="sig")
-            nc.scalar.activation(sig[g][:], saved(a1_t, e0, e1), ACT.Sigmoid)
-            back[g] = work.tile([P, PACK, (e1 - e0) * C], F32, name="back")
-            nc.vector.scalar_tensor_tensor(back[g][:], sig[g][:], 1.0, saved(a3_t, e0, e1), ALU.subtract, ALU.mult)
-            da3[g] = work.tile([P, PACK, (e1 - e0) * C], F32, name="da3")
+            sig[g] = work.tile([P, (e1 - e0) * C, PACK], F32, name="sig")
+            nc.scalar.activation(woven(sig[g][:]), pairs_of(saved(a1_t, e0, e1)), ACT.Sigmoid)
+            off_sq[g] = work.tile([P, (e1 - e0) * C, PACK], F32, name="off_sq")
+            nc.scalar.activation(off_sq[g][:], sig[g][:], ACT.Square, bias=-0.5)
+            slope[g] = work.tile([P, (e1 - e0) * C, PACK], F32, name="slope")
             da[g] = work.tile([P, 2, (e1 - e0) * C, PACK], BF16, name="da", align_bytes=64)
 
-        def make_da3(e):
-            g = group_of[e]
-            cols = slice((e - groups[g][0]) * C, (e - groups[g][0] + 1) * C)
-            acc = psum.tile([P, H], F32, name=f"acc{e % 4}")
+        def make_dh(e):
+            acc = psum.tile([P, H], F32, name=f"bank{e % 4}", offset=e % 4 * BANK)
             for o in range(PASSES):
                 nc.tensor.matmul_mx(
                     acc[:],
@@ -176,14 +166,22 @@ def tile_moe_bdx_glu_sigmoid_kernel(
                 )
             dh_t = work.tile([P, PACK, P], F32, name="dh_t")
             nc.scalar.activation(dh_t[:], acc[:].rearrange("c (q t) -> c t q", t=PACK), ACT.Copy, scale=gate_col[:, e : e + 1])
-            dh_ps = psum.tile([P, PACK, C], F32, name=f"turn{e % 4}")
+            dh_ps[e] = psum.tile([P, PACK, C], F32, name=f"bank{4 + e % 4}", offset=(4 + e % 4) * BANK)
             for t in range(PACK):
-                nc.tensor.transpose(dh_ps[:, t, :], dh_t[:, t, :], ident[:])
-            nc.vector.tensor_tensor(da3[g][:, :, cols], dh_ps[:], sig[g][:, :, cols], ALU.mult)
-            nc.scalar.activation(woven(da[g][:, 1, cols]), pairs_of(da3[g][:, :, cols]), ACT.Copy, scale=-1.0)
+                nc.tensor.transpose(dh_ps[e][:, t, :], dh_t[:, t, :], ident[:])
+
+        def make_da3(e):
+            g = group_of[e]
+            nc.vector.scalar_tensor_tensor(
+                da[g][:, 1, columns(e)], sig[g][:, columns(e)], -1.0, dh_ps[e][:].rearrange("p t c -> p c t"), ALU.mult, ALU.mult)
+
+        def make_slope(e):
+            g = group_of[e]
+            nc.vector.scalar_tensor_tensor(
+                slope[g][:, columns(e)], off_sq[g][:, columns(e)], 0.25, dh_ps[e][:].rearrange("p t c -> p c t"), ALU.subtract, ALU.mult)
 
         def make_da1(g):
-            nc.vector.tensor_tensor(woven(da[g][:, 0]), pairs_of(da3[g][:]), pairs_of(back[g][:]), ALU.mult)
+            nc.vector.tensor_tensor(woven(da[g][:, 0]), woven(slope[g][:]), pairs_of(saved(a3_t, *groups[g])), ALU.mult)
 
         def quantise(g):
             nc.vector.quantize_mx(
@@ -192,60 +190,64 @@ def tile_moe_bdx_glu_sigmoid_kernel(
                 in_=da[g][:].rearrange("p m j t -> p (m j t)"),
             )
 
-        def second_product(e0, e1, kt, bank):
+        def second_product(e0, e1, kt, bank, banks=1):
             k0 = min(kt, 1)
-            acc = psum.tile([P, (e1 - e0) * C], F32, name=bank)
+            acc = psum.tile([P, banks * H], F32, name=f"bank{bank}" + "_wide" * (banks > 1), offset=bank * BANK)
             for e in range(e0, e1):
                 g = group_of[e]
-                cols = slice((e - groups[g][0]) * C, (e - groups[g][0] + 1) * C)
-                for m in range(2):
+                for m in (1, 0):
                     nc.tensor.matmul_mx(
                         acc[:, (e - e0) * C : (e - e0 + 1) * C],
                         lhsT=w13_w[m, k0][:, e, 2 * P * (kt - k0) : 2 * P * (kt - k0 + 1)].bitcast(FP4X4),
-                        lhsT_scale=w13_s[m, k0][:, e, P * (kt - k0) : P * (kt - k0 + 1)],
-                        rhs=da_w[g][:, m, cols].bitcast(FP8X4),
-                        rhs_scale=da_s[g][:, m, cols],
-                        start=(m == 0),
-                        stop=(m == 1),
+                        lhsT_scale=w13_s[m][:, e, P * kt : P * (kt + 1)],
+                        rhs=da_w[g][:, m, columns(e)].bitcast(FP8X4),
+                        rhs_scale=da_s[g][:, m, columns(e)],
+                        start=(m == 1),
+                        stop=(m == 0),
                     )
-            nc.scalar.copy(dx[kt][:, e0 * C : e1 * C], acc[:])
+            nc.scalar.copy(dx[kt][:, e0 * C : e1 * C], acc[:, : (e1 - e0) * C])
 
-        for g in range(len(groups) + 1):
-            experts = range(*groups[g]) if g < len(groups) else []
-            if experts:
-                make_back(g)
-            if g > 0:
-                make_da1(g - 1)
-            for e in experts[:1]:
+        for g, (e0, e1) in enumerate(groups):
+            make_sigmoid(g)
+            for e in range(e0, e1):
+                make_dh(e)
+            for e in range(e0, e1):
+                if e == e0 and e1 - e0 == 1:
+                    make_slope(e)
+                    quantise(g - 1)
+                    make_da3(e)
+                    continue
+                make_slope(e)
+                if e == e0 and g > 0:
+                    quantise(g - 1)
                 make_da3(e)
-            if g > 0:
-                quantise(g - 1)
-            for e in experts[1:]:
-                make_da3(e)
-        for e0, e1, bank in ((0, 4, "acc3"), (4, 6, "acc2"), (6, 7, "acc1"), (7, 8, "acc0")):
-            second_product(e0, e1, 0, bank)
-        for kt in range(1, KT):
-            second_product(0, 4, kt, f"turn{2 * kt - 2}")
-            second_product(4, 8, kt, f"turn{2 * kt - 1}")
+            make_da1(g)
+        quantise(len(groups) - 1)
+        second_product(0, 4, 0, 3)
+        second_product(4, 6, 0, 2)
+        second_product(6, 7, 0, 1)
+        second_product(7, 8, 0, 4, banks=4)
+        second_product(0, 4, 1, 0)
+        second_product(4, 8, 1, 4)
+        second_product(0, 4, 2, 5)
+        second_product(4, 8, 2, 6)
 
         pieces = [(0, 0, T), (1, 0, T), (2, 0, T // 2), (2, T // 2, T)]
         fetched = {}
 
-        def fetch(i, r):
+        def fetch(i):
             kt, t0, t1 = pieces[i]
-            fetched[i, r] = work.tile([P, t1 - t0], F32, name=f"fetched{r}")
-            nc.vector.tensor_copy(fetched[i, r][:], dx[kt][:].indirect(pos_t[r][:, t0 // LIST : t1 // LIST]))
+            fetched[i] = work.tile([P, t1 - t0], F32, name="fetched")
+            nc.vector.tensor_copy(fetched[i][:], dx[kt][:].indirect(pos_t[0][:, t0 // LIST : t1 // LIST]))
 
         def combine(i):
             kt, t0, t1 = pieces[i]
             total = work.tile([P, t1 - t0], F32, name="total")
-            adder = nc.vector if i == len(pieces) - 1 else nc.gpsimd
-            adder.tensor_tensor(total[:], fetched[i, 0][:], fetched[i, 1][:], ALU.add)
+            nc.vector.tensor_tensor(total[:], dx[kt][:].indirect(pos_t[1][:, t0 // LIST : t1 // LIST]), fetched[i][:], ALU.add)
             nc.sync.dma_start(out[kt * P : (kt + 1) * P, t0:t1], total[:])
 
+        fetch(0)
         for i in range(len(pieces)):
-            fetch(i, 0)
-            if i > 0:
-                combine(i - 1)
-            fetch(i, 1)
-        combine(len(pieces) - 1)
+            if i + 1 < len(pieces):
+                fetch(i + 1)
+            combine(i)

@@ -24,7 +24,7 @@ PASSES = N // (P * PACK)
 KT = K // P
 PAIR = 2
 PAIRS = E // PAIR
-W = PAIR * C
+HALF = S // 2
 LIST = 16
 BANK = 2048
 
@@ -42,17 +42,16 @@ def tile_moe_bdx_glu_sigmoid_kernel(
         offs_t = keep.tile([P, S // LIST], U16, name="offs_t")
         nc.sync.dma_start(offs_t[:], offs)
 
-        dy_s = keep.tile([P, T], U8, name="dy_s", align_bytes=64)
+        dy_s = keep.tile([P, PASSES, T], U8, name="dy_s", align_bytes=64)
         nc.gpsimd.memset(dy_s[:].bitcast(I32), 0)
-        for q in range(4):
-            nc.sync.dma_start(dy_s[32 * q : 32 * q + 8, :].bitcast(I32), dy_scales[:, 4 * q : 4 * q + 4, :].bitcast(I32))
+        for r in range(4):
+            nc.sync.dma_start(dy_s[r:P:32, :, :].bitcast(I32), dy_scales.rearrange("o (q r) t -> r q o t", r=4)[r].bitcast(I32))
         dy_w = keep.tile([P, PASSES, T], U32, name="dy_w", align_bytes=64)
         nc.sync.dma_start(dy_w[:].bitcast(I32), dy_words.rearrange("o p t d -> p o (t d)").bitcast(I32))
 
         w2_s = [keep.tile([P, E // 2 * PASSES, H], U8, name=f"w2_s{h}", align_bytes=64) for h in range(2)]
-        g_s1 = keep.tile([P, S], U8, name="g_s1", align_bytes=64)
         w13_s = [keep.tile([P, E, K], U8, name=f"w13_s{m}", align_bytes=64) for m in range(2)]
-        for plane in (w2_s[0], g_s1, w2_s[1]):
+        for plane in w2_s:
             nc.vector.memset(plane[:].bitcast(I32), 0)
 
         warm = keep.tile([P, 8], F32, name="warm")
@@ -82,19 +81,27 @@ def tile_moe_bdx_glu_sigmoid_kernel(
             )
 
         w2_w = [keep.tile([P, PAIR * PASSES, 2 * H], U8, name=f"w2_w{u}", align_bytes=64) for u in range(PAIRS)]
-        a1_t = [keep.tile([P, PACK, W], F32, name=f"a1_t{u}") for u in range(PAIRS)]
-        a3_t = [keep.tile([P, PACK, W], F32, name=f"a3_t{u}") for u in range(PAIRS)]
-        for u in range(PAIRS):
-            if u == 0:
-                nc.sync.dma_start(a1_t[u][:], a1.rearrange("(p t) j -> p t j", t=PACK)[:, :, u * W : (u + 1) * W])
+        a1_t = [keep.tile([P, PACK, HALF], F32, name=f"a1_t{h}") for h in range(2)]
+        a3_t = [keep.tile([P, PACK, HALF], F32, name=f"a3_t{h}") for h in range(2)]
+
+        def load_w2_words(u):
             nc.sync.dma_start(w2_w[u][:].bitcast(I32), w2_words[PAIR * u : PAIR * (u + 1)].rearrange("e s p b -> p (e s) b").bitcast(I32))
-            if u % 2 == 0:
-                load_scales(w2_s[u // 2], w2_scales[PAIR * u : PAIR * (u + 2)])
-            if u > 0:
-                nc.sync.dma_start(a1_t[u][:], a1.rearrange("(p t) j -> p t j", t=PACK)[:, :, u * W : (u + 1) * W])
-            else:
+
+        def load_saved(tiles, rows, h):
+            nc.sync.dma_start(tiles[h][:], rows.rearrange("(p t) j -> p t j", t=PACK)[:, :, h * HALF : (h + 1) * HALF])
+
+        for h in range(2):
+            if h == 0:
+                load_w2_words(0)
+                load_saved(a1_t, a1, 0)
+            load_scales(w2_s[h], w2_scales[h * E // 2 : (h + 1) * E // 2])
+            if h == 0:
                 nc.sync.dma_start(gate_rows[0:E, :], gate[0].rearrange("(e c) -> e c", c=C))
-            nc.sync.dma_start(a3_t[u][:], a3.rearrange("(p t) j -> p t j", t=PACK)[:, :, u * W : (u + 1) * W])
+            else:
+                load_w2_words(2)
+                load_saved(a1_t, a1, 1)
+            load_w2_words(2 * h + 1)
+            load_saved(a3_t, a3, h)
         for m in range(2):
             load_scales(w13_s[m], (w1_scales, w3_scales)[m])
             load_w13_words(m, 0)
@@ -104,23 +111,17 @@ def tile_moe_bdx_glu_sigmoid_kernel(
         for m in range(2):
             load_w13_words(m, 1)
 
-        g_s = keep.tile([P, S], U8, name="g_s", align_bytes=64)
+        g_s = [keep.tile([P, S], U8, name=f"g_s{o}", align_bytes=64) for o in range(PASSES)]
         g_w = [keep.tile([P, S], U32, name=f"g_w{o}", align_bytes=64) for o in range(PASSES)]
-        cuts = ((0, 256), (256, 640), (640, S))
-        for j0, j1 in cuts:
-            nc.vector.tensor_copy(g_s[:, j0:j1], dy_s[:].indirect(offs_t[:, j0 // LIST : j1 // LIST]))
-        for j0, j1 in ((0, W), (W, S)):
-            nc.scalar.dma_start(g_s1[0:100, j0:j1].bitcast(I32), g_s[4:104, j0:j1].bitcast(I32))
-        g_sc = [g_s, g_s1]
+        for j0, j1 in ((0, 256), (256, 640), (640, S)):
+            for gathered, table in ((g_s, dy_s), (g_w, dy_w)):
+                for o in range(PASSES):
+                    nc.vector.tensor_copy(gathered[o][:, j0:j1], table[:, o, :].indirect(offs_t[:, j0 // LIST : j1 // LIST]))
 
         gate_ps = psum.tile([P, PACK, C], F32, name="bank7", offset=7 * BANK)
         nc.tensor.transpose(gate_ps[:, 0, :], gate_rows[:], ident[:])
         gate_col = keep.tile([P, E], F32, name="gate_col")
         nc.scalar.activation(gate_col[:], gate_ps[:, 0, 0:E], ACT.Copy, scale=-1.0)
-
-        for j0, j1 in cuts:
-            for o in range(PASSES):
-                nc.vector.tensor_copy(g_w[o][:, j0:j1], dy_w[:, o, :].indirect(offs_t[:, j0 // LIST : j1 // LIST]))
 
         dx = [keep.tile([P, S], F32, name=f"dx{kt}") for kt in range(KT)]
         groups = [(0, 2), (2, 4), (4, 6), (6, 7), (7, 8)]
@@ -130,8 +131,8 @@ def tile_moe_bdx_glu_sigmoid_kernel(
         sig, off_sq, slope, da, dh_ps = {}, {}, {}, {}, {}
 
         def saved(tiles, e0, e1):
-            u = e0 // PAIR
-            return tiles[u][:, :, (e0 - u * PAIR) * C : (e1 - u * PAIR) * C]
+            h = e0 * C // HALF
+            return tiles[h][:, :, e0 * C - h * HALF : e1 * C - h * HALF]
 
         def pairs_of(planes):
             return planes.rearrange("p t (c i) -> p c t i", i=2)
@@ -158,7 +159,7 @@ def tile_moe_bdx_glu_sigmoid_kernel(
                 nc.tensor.matmul_mx(
                     acc[:],
                     lhsT=g_w[o][:, e * C : (e + 1) * C].bitcast(FP8X4),
-                    lhsT_scale=g_sc[o][:, e * C : (e + 1) * C],
+                    lhsT_scale=g_s[o][:, e * C : (e + 1) * C],
                     rhs=w2_w[e // PAIR][:, e % PAIR * PASSES + o, :].bitcast(FP4X4),
                     rhs_scale=w2_s[e // (E // 2)][:, e % (E // 2) * PASSES + o, :],
                     start=(o == 0),

@@ -42,22 +42,19 @@ def tile_moe_bdx_glu_sigmoid_kernel(
         offs_t = keep.tile([P, S // LIST], U16, name="offs_t")
         nc.sync.dma_start(offs_t[:], offs)
 
-        dy_s = keep.tile([P, PASSES, T], U8, name="dy_s", align_bytes=64)
+        dy_s = keep.tile([P, PASSES + 1, T], U8, name="dy_s", align_bytes=64)
         nc.gpsimd.memset(dy_s[:].bitcast(I32), 0)
         for r in range(4):
-            nc.sync.dma_start(dy_s[r:P:32, :, :].bitcast(I32), dy_scales.rearrange("o (q r) t -> r q o t", r=4)[r].bitcast(I32))
-        dy_w = keep.tile([P, PASSES, T], U32, name="dy_w", align_bytes=64)
-        nc.sync.dma_start(dy_w[:].bitcast(I32), dy_words.rearrange("o p t d -> p o (t d)").bitcast(I32))
+            nc.sync.dma_start(dy_s[r:P:32, :PASSES, :].bitcast(I32), dy_scales.rearrange("o (q r) t -> r q o t", r=4)[r].bitcast(I32))
+        dy_w = keep.tile([P, PASSES + 1, T], U32, name="dy_w", align_bytes=64)
+        nc.sync.dma_start(dy_w[:, :PASSES, :].bitcast(I32), dy_words.rearrange("o p t d -> p o (t d)").bitcast(I32))
 
         w2_s = [keep.tile([P, E // 2 * PASSES, H], U8, name=f"w2_s{h}", align_bytes=64) for h in range(2)]
         w13_s = [keep.tile([P, E, K], U8, name=f"w13_s{m}", align_bytes=64) for m in range(2)]
         for plane in w2_s:
             nc.vector.memset(plane[:].bitcast(I32), 0)
 
-        warm = keep.tile([P, 8], F32, name="warm")
-        nc.gpsimd.memset(warm[:], 0.0)
-        nc.scalar.activation(warm[:], warm[:], ACT.Sigmoid)
-        gate_rows = keep.tile([P, C], F32, name="gate_rows")
+        gate_rows = keep.tile([P, C], F32, name="gate_rows", align_bytes=64)
         nc.gpsimd.memset(gate_rows[:], 0.0)
         ident = keep.tile([P, P], F32, name="ident")
         make_identity(nc, ident[:])
@@ -81,29 +78,31 @@ def tile_moe_bdx_glu_sigmoid_kernel(
             )
 
         w2_w = [keep.tile([P, PAIR * PASSES, 2 * H], U8, name=f"w2_w{u}", align_bytes=64) for u in range(PAIRS)]
-        a1_t = [keep.tile([P, PACK, HALF], F32, name=f"a1_t{h}") for h in range(2)]
-        a3_t = [keep.tile([P, PACK, HALF], F32, name=f"a3_t{h}") for h in range(2)]
+        a1_cuts = ((0, 2), (2, 4), (4, 6), (6, 8))
+        a3_cuts = a1_cuts
+        a1_t, a3_t = {}, {}
 
         def load_w2_words(u):
             nc.sync.dma_start(w2_w[u][:].bitcast(I32), w2_words[PAIR * u : PAIR * (u + 1)].rearrange("e s p b -> p (e s) b").bitcast(I32))
 
-        def load_saved(tiles, rows, h):
-            nc.sync.dma_start(tiles[h][:], rows.rearrange("(p t) j -> p t j", t=PACK)[:, :, h * HALF : (h + 1) * HALF])
+        def load_saved(tiles, rows, name, e0, e1):
+            tiles[e0, e1] = keep.tile([P, PACK, (e1 - e0) * C], F32, name=f"{name}{e0}")
+            nc.sync.dma_start(tiles[e0, e1][:], rows.rearrange("(p t) j -> p t j", t=PACK)[:, :, e0 * C : e1 * C])
 
-        for h in range(2):
-            if h == 0:
-                load_w2_words(0)
-                load_saved(a1_t, a1, 0)
-            load_scales(w2_s[h], w2_scales[h * E // 2 : (h + 1) * E // 2])
-            if h == 0:
-                nc.sync.dma_start(gate_rows[0:E, :], gate[0].rearrange("(e c) -> e c", c=C))
-            else:
-                load_w2_words(2)
-                load_saved(a1_t, a1, 1)
-            load_w2_words(2 * h + 1)
-            load_saved(a3_t, a3, h)
+        load_w2_words(0)
+        load_saved(a1_t, a1, "a1_t", *a1_cuts[0])
+        load_scales(w2_s[0], w2_scales[: E // 2])
+        nc.sync.dma_start(gate_rows[0:E, :], gate[0].rearrange("(e c) -> e c", c=C))
+        for u in range(1, PAIRS):
+            if u == PAIRS // 2:
+                load_scales(w2_s[1], w2_scales[E // 2 :])
+            load_w2_words(u)
+            load_saved(a1_t, a1, "a1_t", *a1_cuts[u])
+            load_saved(a3_t, a3, "a3_t", *a3_cuts[u - 1])
+        load_saved(a3_t, a3, "a3_t", *a3_cuts[PAIRS - 1])
         for m in range(2):
             load_scales(w13_s[m], (w1_scales, w3_scales)[m])
+        for m in range(2):
             load_w13_words(m, 0)
         pos_t = [keep.tile([P, T // LIST], U16, name=f"pos_t{r}") for r in range(2)]
         nc.sync.dma_start(pos_t[0][:], pos1)
@@ -111,17 +110,20 @@ def tile_moe_bdx_glu_sigmoid_kernel(
         for m in range(2):
             load_w13_words(m, 1)
 
-        g_s = [keep.tile([P, S], U8, name=f"g_s{o}", align_bytes=64) for o in range(PASSES)]
-        g_w = [keep.tile([P, S], U32, name=f"g_w{o}", align_bytes=64) for o in range(PASSES)]
-        for j0, j1 in ((0, 256), (256, 640), (640, S)):
-            for gathered, table in ((g_s, dy_s), (g_w, dy_w)):
-                for o in range(PASSES):
-                    nc.vector.tensor_copy(gathered[o][:, j0:j1], table[:, o, :].indirect(offs_t[:, j0 // LIST : j1 // LIST]))
-
         gate_ps = psum.tile([P, PACK, C], F32, name="bank7", offset=7 * BANK)
         nc.tensor.transpose(gate_ps[:, 0, :], gate_rows[:], ident[:])
-        gate_col = keep.tile([P, E], F32, name="gate_col")
-        nc.scalar.activation(gate_col[:], gate_ps[:, 0, 0:E], ACT.Copy, scale=-1.0)
+        g_s = [keep.tile([P, PASSES, HALF], U8, name=name, align_bytes=64) for name in ("g_s", "gate_rows")]
+        g_w = [keep.tile([P, PASSES, HALF], U32, name=f"g_w{h}", align_bytes=64) for h in range(2)]
+        for gathered, table, h in ((g_s, dy_s, 0), (g_w, dy_w, 0), (g_w, dy_w, 1), (g_s, dy_s, 1)):
+            for o in range(PASSES):
+                nc.vector.tensor_copy(
+                    gathered[h][:, o, :],
+                    table[:, o : o + 2, :].rearrange("p o t -> p (o t)").indirect(offs_t[:, h * HALF // LIST : (h + 1) * HALF // LIST]),
+                )
+
+        gate_col = [keep.tile([P, PAIR], F32, name=f"turn_taker{u}") for u in range(PAIRS)]
+        for u in range(PAIRS):
+            nc.scalar.activation(gate_col[u][:], gate_ps[:, 0, PAIR * u : PAIR * (u + 1)], ACT.Copy, scale=-1.0)
 
         dx = [keep.tile([P, S], F32, name=f"dx{kt}") for kt in range(KT)]
         groups = [(0, 2), (2, 4), (4, 6), (6, 7), (7, 8)]
@@ -131,8 +133,8 @@ def tile_moe_bdx_glu_sigmoid_kernel(
         sig, off_sq, slope, da, dh_ps = {}, {}, {}, {}, {}
 
         def saved(tiles, e0, e1):
-            h = e0 * C // HALF
-            return tiles[h][:, :, e0 * C - h * HALF : e1 * C - h * HALF]
+            first, last = [cut for cut in tiles if cut[0] <= e0 < cut[1]][0]
+            return tiles[first, last][:, :, (e0 - first) * C : (e1 - first) * C]
 
         def pairs_of(planes):
             return planes.rearrange("p t (c i) -> p c t i", i=2)
@@ -146,7 +148,10 @@ def tile_moe_bdx_glu_sigmoid_kernel(
 
         def make_sigmoid(g):
             e0, e1 = groups[g]
-            sig[g] = work.tile([P, (e1 - e0) * C, PACK], F32, name="sig")
+            if 0 < g < PAIRS:
+                sig[g] = keep.tile([P, (e1 - e0) * C, PACK], F32, name=f"turn_taker{g - 1}")
+            else:
+                sig[g] = work.tile([P, (e1 - e0) * C, PACK], F32, name="sig")
             nc.scalar.activation(woven(sig[g][:]), pairs_of(saved(a1_t, e0, e1)), ACT.Sigmoid)
             off_sq[g] = work.tile([P, (e1 - e0) * C, PACK], F32, name="off_sq")
             nc.scalar.activation(off_sq[g][:], sig[g][:], ACT.Square, bias=-0.5)
@@ -154,20 +159,20 @@ def tile_moe_bdx_glu_sigmoid_kernel(
             da[g] = work.tile([P, 2, (e1 - e0) * C, PACK], BF16, name="da", align_bytes=64)
 
         def make_dh(e):
-            acc = psum.tile([P, H], F32, name=f"bank{e % 4}", offset=e % 4 * BANK)
+            acc = psum.tile([P, H], F32, name=f"bank{e % 2}", offset=e % 2 * BANK)
             for o in range(PASSES):
                 nc.tensor.matmul_mx(
                     acc[:],
-                    lhsT=g_w[o][:, e * C : (e + 1) * C].bitcast(FP8X4),
-                    lhsT_scale=g_s[o][:, e * C : (e + 1) * C],
+                    lhsT=g_w[e // 4][:, o, e % 4 * C : (e % 4 + 1) * C].bitcast(FP8X4),
+                    lhsT_scale=g_s[e // 4][:, o, e % 4 * C : (e % 4 + 1) * C],
                     rhs=w2_w[e // PAIR][:, e % PAIR * PASSES + o, :].bitcast(FP4X4),
                     rhs_scale=w2_s[e // (E // 2)][:, e % (E // 2) * PASSES + o, :],
                     start=(o == 0),
                     stop=(o == PASSES - 1),
                 )
             dh_t = work.tile([P, PACK, P], F32, name="dh_t")
-            nc.scalar.activation(dh_t[:], acc[:].rearrange("c (q t) -> c t q", t=PACK), ACT.Copy, scale=gate_col[:, e : e + 1])
-            dh_ps[e] = psum.tile([P, PACK, C], F32, name=f"bank{4 + e % 4}", offset=(4 + e % 4) * BANK)
+            nc.scalar.activation(dh_t[:], acc[:].rearrange("c (q t) -> c t q", t=PACK), ACT.Copy, scale=gate_col[e // PAIR][:, e % PAIR : e % PAIR + 1])
+            dh_ps[e] = psum.tile([P, PACK, C], F32, name=f"bank{2 + e % 6}", offset=(2 + e % 6) * BANK)
             for t in range(PACK):
                 nc.tensor.transpose(dh_ps[e][:, t, :], dh_t[:, t, :], ident[:])
 
@@ -224,16 +229,16 @@ def tile_moe_bdx_glu_sigmoid_kernel(
                 make_da3(e)
             make_da1(g)
         quantise(len(groups) - 1)
-        second_product(0, 4, 0, 3)
-        second_product(4, 6, 0, 2)
-        second_product(6, 7, 0, 1)
-        second_product(7, 8, 0, 4, banks=4)
-        second_product(0, 4, 1, 0)
-        second_product(4, 8, 1, 4)
-        second_product(0, 4, 2, 5)
+        second_product(0, 4, 0, 0)
+        second_product(4, 6, 0, 1)
+        second_product(6, 7, 0, 4)
+        second_product(7, 8, 0, 5, banks=2)
+        second_product(0, 4, 1, 7)
+        second_product(4, 8, 1, 5)
+        second_product(0, 4, 2, 2)
         second_product(4, 8, 2, 6)
 
-        pieces = [(0, 0, T), (1, 0, T), (2, 0, T // 2), (2, T // 2, T)]
+        pieces = [(0, 0, T), (1, 0, T), (2, 0, T - C), (2, T - C, T)]
         fetched = {}
 
         def fetch(i):

@@ -47,7 +47,6 @@ def tile_moe_bdx_glu_sigmoid_kernel(
         for r in range(4):
             nc.sync.dma_start(dy_s[r:P:32, :PASSES, :].bitcast(I32), dy_scales.rearrange("o (q r) t -> r q o t", r=4)[r].bitcast(I32))
         dy_w = keep.tile([P, PASSES + 1, T], U32, name="dy_w", align_bytes=64)
-        nc.sync.dma_start(dy_w[:, :PASSES, :].bitcast(I32), dy_words.rearrange("o p t d -> p o (t d)").bitcast(I32))
 
         w2_s = [keep.tile([P, E // 2 * PASSES, H], U8, name=f"w2_s{h}", align_bytes=64) for h in range(2)]
         w13_s = [keep.tile([P, E, K], U8, name=f"w13_s{m}", align_bytes=64) for m in range(2)]
@@ -78,7 +77,7 @@ def tile_moe_bdx_glu_sigmoid_kernel(
             )
 
         w2_w = [keep.tile([P, PAIR * PASSES, 2 * H], U8, name=f"w2_w{u}", align_bytes=64) for u in range(PAIRS)]
-        a1_cuts = ((0, 2), (2, 4), (4, 6), (6, 8))
+        a1_cuts = ((0, 4), (4, 6), (6, 8))
         a3_cuts = a1_cuts
         a1_t, a3_t = {}, {}
 
@@ -89,17 +88,20 @@ def tile_moe_bdx_glu_sigmoid_kernel(
             tiles[e0, e1] = keep.tile([P, PACK, (e1 - e0) * C], F32, name=f"{name}{e0}")
             nc.sync.dma_start(tiles[e0, e1][:], rows.rearrange("(p t) j -> p t j", t=PACK)[:, :, e0 * C : e1 * C])
 
+        nc.sync.dma_start(dy_w[:, :PASSES, :].bitcast(I32), dy_words.rearrange("o p t d -> p o (t d)").bitcast(I32))
         load_w2_words(0)
         load_saved(a1_t, a1, "a1_t", *a1_cuts[0])
-        load_scales(w2_s[0], w2_scales[: E // 2])
         nc.sync.dma_start(gate_rows[0:E, :], gate[0].rearrange("(e c) -> e c", c=C))
-        for u in range(1, PAIRS):
-            if u == PAIRS // 2:
-                load_scales(w2_s[1], w2_scales[E // 2 :])
-            load_w2_words(u)
-            load_saved(a1_t, a1, "a1_t", *a1_cuts[u])
-            load_saved(a3_t, a3, "a3_t", *a3_cuts[u - 1])
-        load_saved(a3_t, a3, "a3_t", *a3_cuts[PAIRS - 1])
+        for h in range(2):
+            load_scales(w2_s[h], w2_scales[h * E // 2 : (h + 1) * E // 2])
+        load_w2_words(1)
+        load_saved(a3_t, a3, "a3_t", *a3_cuts[0])
+        load_w2_words(2)
+        load_saved(a1_t, a1, "a1_t", *a1_cuts[1])
+        load_w2_words(3)
+        load_saved(a3_t, a3, "a3_t", *a3_cuts[1])
+        load_saved(a1_t, a1, "a1_t", *a1_cuts[2])
+        load_saved(a3_t, a3, "a3_t", *a3_cuts[2])
         for m in range(2):
             load_scales(w13_s[m], (w1_scales, w3_scales)[m])
         for m in range(2):
@@ -152,9 +154,10 @@ def tile_moe_bdx_glu_sigmoid_kernel(
                 sig[g] = keep.tile([P, (e1 - e0) * C, PACK], F32, name=f"turn_taker{g - 1}")
             else:
                 sig[g] = work.tile([P, (e1 - e0) * C, PACK], F32, name="sig")
-            nc.scalar.activation(woven(sig[g][:]), pairs_of(saved(a1_t, e0, e1)), ACT.Sigmoid)
             off_sq[g] = work.tile([P, (e1 - e0) * C, PACK], F32, name="off_sq")
-            nc.scalar.activation(off_sq[g][:], sig[g][:], ACT.Square, bias=-0.5)
+            for e in range(e0, e1):
+                nc.scalar.activation(woven(sig[g][:, columns(e)]), pairs_of(saved(a1_t, e, e + 1)), ACT.Sigmoid)
+                nc.scalar.activation(off_sq[g][:, columns(e)], sig[g][:, columns(e)], ACT.Square, bias=-0.5)
             slope[g] = work.tile([P, (e1 - e0) * C, PACK], F32, name="slope")
             da[g] = work.tile([P, 2, (e1 - e0) * C, PACK], BF16, name="da", align_bytes=64)
 

@@ -49,68 +49,59 @@ def tile_moe_bdx_glu_sigmoid_kernel(
         dy_w = keep.tile([P, PASSES + 1, T], U32, name="dy_w", align_bytes=64)
 
         w2_s = [keep.tile([P, E // 2 * PASSES, H], U8, name=f"w2_s{h}", align_bytes=64) for h in range(2)]
-        w13_s = [keep.tile([P, E, K], U8, name=f"w13_s{m}", align_bytes=64) for m in range(2)]
-        for plane in w2_s:
+        for plane in reversed(w2_s):
             nc.vector.memset(plane[:].bitcast(I32), 0)
 
         gate_rows = keep.tile([P, C], F32, name="gate_rows", align_bytes=64)
         nc.gpsimd.memset(gate_rows[:], 0.0)
         ident = keep.tile([P, P], F32, name="ident")
         make_identity(nc, ident[:])
-        for plane in w13_s:
-            nc.gpsimd.memset(plane[:].bitcast(I32), 0)
 
-        def load_scales(plane, rows):
+        def load_scales(queue, plane, rows):
             by_row = rows.rearrange("e s (q r) i -> r q (e s) i", r=4)
             for r in range(4):
-                nc.sync.dma_start(plane[r:P:32, :, :].bitcast(I32), by_row[r].bitcast(I32))
+                queue.dma_start(plane[r:P:32, :, :].bitcast(I32), by_row[r].bitcast(I32))
 
-        k_parts = ((0, 1), (1, KT))
-        w13_w = {}
+        w13_w, w13_s = {}, {}
 
-        def load_w13_words(m, part):
-            k0, k1 = k_parts[part]
-            w13_w[m, k0] = keep.tile([P, E, 2 * P * (k1 - k0)], U8, name=f"w13_w{m}{k0}", align_bytes=64)
-            nc.sync.dma_start(
-                w13_w[m, k0][:].bitcast(I32),
-                (w1_words, w3_words)[m].rearrange("e s p b -> p (e s) b")[:, :, 2 * P * k0 : 2 * P * k1].bitcast(I32),
-            )
+        def load_w13(kt):
+            for m in range(2):
+                w13_w[m, kt] = keep.tile([P, E, 2 * P], U8, name=f"w13_w{m}{kt}", align_bytes=64)
+                nc.sync.dma_start(
+                    w13_w[m, kt][:].bitcast(I32),
+                    (w1_words, w3_words)[m].rearrange("e s p b -> p (e s) b")[:, :, 2 * P * kt : 2 * P * (kt + 1)].bitcast(I32),
+                )
 
         w2_w = [keep.tile([P, PAIR * PASSES, 2 * H], U8, name=f"w2_w{u}", align_bytes=64) for u in range(PAIRS)]
         a1_cuts = ((0, 4), (4, 6), (6, 8))
-        a3_cuts = a1_cuts
+        a3_cuts = ((0, 2), (2, 4), (4, 6), (6, 8))
         a1_t, a3_t = {}, {}
 
         def load_w2_words(u):
             nc.sync.dma_start(w2_w[u][:].bitcast(I32), w2_words[PAIR * u : PAIR * (u + 1)].rearrange("e s p b -> p (e s) b").bitcast(I32))
 
         def load_saved(tiles, rows, name, e0, e1):
-            tiles[e0, e1] = keep.tile([P, PACK, (e1 - e0) * C], F32, name=f"{name}{e0}")
+            tiles[e0, e1] = keep.tile([P, PACK, (e1 - e0) * C], F32, name=f"{name}{e0}", align_bytes=64)
             nc.sync.dma_start(tiles[e0, e1][:], rows.rearrange("(p t) j -> p t j", t=PACK)[:, :, e0 * C : e1 * C])
 
         nc.sync.dma_start(dy_w[:, :PASSES, :].bitcast(I32), dy_words.rearrange("o p t d -> p o (t d)").bitcast(I32))
         load_w2_words(0)
         load_saved(a1_t, a1, "a1_t", *a1_cuts[0])
         nc.sync.dma_start(gate_rows[0:E, :], gate[0].rearrange("(e c) -> e c", c=C))
-        for h in range(2):
-            load_scales(w2_s[h], w2_scales[h * E // 2 : (h + 1) * E // 2])
-        load_w2_words(1)
+        load_scales(nc.sync, w2_s[0], w2_scales[: E // 2])
+        load_scales(nc.gpsimd, w2_s[1], w2_scales[E // 2 :])
         load_saved(a3_t, a3, "a3_t", *a3_cuts[0])
-        load_w2_words(2)
+        load_w2_words(1)
         load_saved(a1_t, a1, "a1_t", *a1_cuts[1])
-        load_w2_words(3)
         load_saved(a3_t, a3, "a3_t", *a3_cuts[1])
         load_saved(a1_t, a1, "a1_t", *a1_cuts[2])
+        load_w2_words(2)
         load_saved(a3_t, a3, "a3_t", *a3_cuts[2])
-        for m in range(2):
-            load_scales(w13_s[m], (w1_scales, w3_scales)[m])
-        for m in range(2):
-            load_w13_words(m, 0)
+        load_w2_words(3)
+        load_saved(a3_t, a3, "a3_t", *a3_cuts[3])
         pos_t = [keep.tile([P, T // LIST], U16, name=f"pos_t{r}") for r in range(2)]
         nc.sync.dma_start(pos_t[0][:], pos1)
         nc.sync.dma_start(pos_t[1][:], pos2)
-        for m in range(2):
-            load_w13_words(m, 1)
 
         gate_ps = psum.tile([P, PACK, C], F32, name="bank7", offset=7 * BANK)
         nc.tensor.transpose(gate_ps[:, 0, :], gate_rows[:], ident[:])
@@ -123,16 +114,13 @@ def tile_moe_bdx_glu_sigmoid_kernel(
                     table[:, o : o + 2, :].rearrange("p o t -> p (o t)").indirect(offs_t[:, h * HALF // LIST : (h + 1) * HALF // LIST]),
                 )
 
-        gate_col = [keep.tile([P, PAIR], F32, name=f"turn_taker{u}") for u in range(PAIRS)]
-        for u in range(PAIRS):
-            nc.scalar.activation(gate_col[u][:], gate_ps[:, 0, PAIR * u : PAIR * (u + 1)], ACT.Copy, scale=-1.0)
+        gate_col = keep.tile([P, E], F32, name="gate_col")
+        nc.scalar.activation(gate_col[:], gate_ps[:, 0, :E], ACT.Copy)
 
         dx = [keep.tile([P, S], F32, name=f"dx{kt}") for kt in range(KT)]
         groups = [(0, 2), (2, 4), (4, 6), (6, 7), (7, 8)]
         group_of = {e: g for g, (e0, e1) in enumerate(groups) for e in range(e0, e1)}
-        da_w = [keep.tile([P, 2, (e1 - e0) * C], U32, name=f"da_w{e0}", align_bytes=64) for e0, e1 in groups]
-        da_s = [keep.tile([P, 2, (e1 - e0) * C], U8, name=f"da_s{e0}", align_bytes=64) for e0, e1 in groups]
-        sig, off_sq, slope, da, dh_ps = {}, {}, {}, {}, {}
+        da_w, da_s, da, sig_t, sig_minus, rest, sums, da3_ps = {}, {}, {}, {}, {}, {}, {}, {}
 
         def saved(tiles, e0, e1):
             first, last = [cut for cut in tiles if cut[0] <= e0 < cut[1]][0]
@@ -148,24 +136,28 @@ def tile_moe_bdx_glu_sigmoid_kernel(
             e0 = groups[group_of[e]][0]
             return slice((e - e0) * C, (e - e0 + 1) * C)
 
-        def make_sigmoid(g):
-            e0, e1 = groups[g]
-            if 0 < g < PAIRS:
-                sig[g] = keep.tile([P, (e1 - e0) * C, PACK], F32, name=f"turn_taker{g - 1}")
-            else:
-                sig[g] = work.tile([P, (e1 - e0) * C, PACK], F32, name="sig")
-            off_sq[g] = work.tile([P, (e1 - e0) * C, PACK], F32, name="off_sq")
-            for e in range(e0, e1):
-                nc.scalar.activation(woven(sig[g][:, columns(e)]), pairs_of(saved(a1_t, e, e + 1)), ACT.Sigmoid)
-                nc.scalar.activation(off_sq[g][:, columns(e)], sig[g][:, columns(e)], ACT.Square, bias=-0.5)
-            slope[g] = work.tile([P, (e1 - e0) * C, PACK], F32, name="slope")
-            da[g] = work.tile([P, 2, (e1 - e0) * C, PACK], BF16, name="da", align_bytes=64)
+        def make_sigmoid(e):
+            turned = psum.tile([P, PACK, P], F32, name=f"bank{6 + e % 2}", offset=(6 + e % 2) * BANK)
+            for t in range(PACK):
+                nc.tensor.transpose(turned[:, t, :], saved(a1_t, e, e + 1)[:, t, :], ident[:])
+            sig_t[e] = keep.tile([P, PACK, P], F32, name=f"sig_t{e}", align_bytes=64)
+            nc.scalar.activation(sig_t[e][:], turned[:], ACT.Sigmoid)
 
-        def make_dh(e):
-            acc = psum.tile([P, H], F32, name=f"bank{e % 2}", offset=e % 2 * BANK)
+        def make_sigmoid_minus(u):
+            sig_minus[u] = keep.tile([P, PACK, PAIR * C], F32, name=f"sig_minus{u}", align_bytes=64)
+            nc.scalar.activation(sig_minus[u][:], saved(a1_t, PAIR * u, PAIR * (u + 1)), ACT.Sigmoid, scale=-1.0)
+
+        def make_rest(u, engine, name, parts):
+            rest[u] = keep.tile([P, PACK, PAIR * C], F32, name=name, align_bytes=64)
+            for c0 in range(0, PAIR * C, PAIR * C // parts):
+                cols = slice(c0, c0 + PAIR * C // parts)
+                engine.tensor_tensor(rest[u][:, :, cols], sig_minus[u][:, :, cols], saved(a3_t, PAIR * u, PAIR * (u + 1))[:, :, cols], ALU.mult)
+
+        def first_product(e):
+            sums[e] = psum.tile([P, H], F32, name=f"bank{e % 3}", offset=e % 3 * BANK)
             for o in range(PASSES):
                 nc.tensor.matmul_mx(
-                    acc[:],
+                    sums[e][:],
                     lhsT=g_w[e // 4][:, o, e % 4 * C : (e % 4 + 1) * C].bitcast(FP8X4),
                     lhsT_scale=g_s[e // 4][:, o, e % 4 * C : (e % 4 + 1) * C],
                     rhs=w2_w[e // PAIR][:, e % PAIR * PASSES + o, :].bitcast(FP4X4),
@@ -173,41 +165,49 @@ def tile_moe_bdx_glu_sigmoid_kernel(
                     start=(o == 0),
                     stop=(o == PASSES - 1),
                 )
-            dh_t = work.tile([P, PACK, P], F32, name="dh_t")
-            nc.scalar.activation(dh_t[:], acc[:].rearrange("c (q t) -> c t q", t=PACK), ACT.Copy, scale=gate_col[e // PAIR][:, e % PAIR : e % PAIR + 1])
-            dh_ps[e] = psum.tile([P, PACK, C], F32, name=f"bank{2 + e % 6}", offset=(2 + e % 6) * BANK)
-            for t in range(PACK):
-                nc.tensor.transpose(dh_ps[e][:, t, :], dh_t[:, t, :], ident[:])
 
         def make_da3(e):
-            g = group_of[e]
+            da3_t = work.tile([P, PACK, P], F32, name="da3_t")
             nc.vector.scalar_tensor_tensor(
-                da[g][:, 1, columns(e)], sig[g][:, columns(e)], -1.0, dh_ps[e][:].rearrange("p t c -> p c t"), ALU.mult, ALU.mult)
+                da3_t[:], sums[e][:].rearrange("c (q t) -> c t q", t=PACK), gate_col[:, e : e + 1], sig_t[e][:], ALU.mult, ALU.mult)
+            da3_ps[e] = psum.tile([P, PACK, C], F32, name=f"bank{3 + e % 3}", offset=(3 + e % 3) * BANK)
+            for t in range(PACK):
+                nc.tensor.transpose(da3_ps[e][:, t, :], da3_t[:, t, :], ident[:])
 
-        def make_slope(e):
+        def rounded(e, m):
             g = group_of[e]
-            nc.vector.scalar_tensor_tensor(
-                slope[g][:, columns(e)], off_sq[g][:, columns(e)], 0.25, dh_ps[e][:].rearrange("p t c -> p c t"), ALU.subtract, ALU.mult)
+            if (g, m) not in da:
+                name = f"a1_t{PAIR * (g + 2)}" if m == 1 and g < 2 else f"da{g}{m}"
+                da[g, m] = keep.tile([P, (groups[g][1] - e) * C, PACK], BF16, name=name, align_bytes=64)
+            return da[g, m][:, columns(e)]
 
-        def make_da1(g):
-            nc.vector.tensor_tensor(woven(da[g][:, 0]), woven(slope[g][:]), pairs_of(saved(a3_t, *groups[g])), ALU.mult)
+        def round_da3(e):
+            nc.scalar.copy(rounded(e, 1), da3_ps[e][:].rearrange("p t c -> p c t"))
 
-        def quantise(g):
-            nc.vector.quantize_mx(
-                out=da_w[g][:].rearrange("p m j -> p (m j)").bitcast(FP8X4),
-                scales=da_s[g][:].rearrange("p m j -> p (m j)"),
-                in_=da[g][:].rearrange("p m j t -> p (m j t)"),
+        def make_da1(e):
+            nc.vector.tensor_tensor(
+                woven(rounded(e, 0)),
+                pairs_of(rest[e // PAIR][:, :, e % PAIR * C : (e % PAIR + 1) * C]),
+                pairs_of(da3_ps[e][:]),
+                ALU.mult,
             )
 
-        def second_product(e0, e1, kt, bank, banks=1):
-            k0 = min(kt, 1)
-            acc = psum.tile([P, banks * H], F32, name=f"bank{bank}" + "_wide" * (banks > 1), offset=bank * BANK)
+        def quantise(g, name):
+            e0, e1 = groups[g]
+            da_w[g] = keep.tile([P, 2, (e1 - e0) * C], U32, name=name, align_bytes=64)
+            da_s[g] = keep.tile([P, 2, (e1 - e0) * C], U8, name=f"da_s{g}", align_bytes=64)
+            for m in (1, 0):
+                nc.vector.quantize_mx(
+                    out=da_w[g][:, m, :].bitcast(FP8X4), scales=da_s[g][:, m, :], in_=da[g, m][:].rearrange("p j t -> p (j t)"))
+
+        def second_product(e0, e1, kt, bank):
+            acc = psum.tile([P, H], F32, name=f"bank{bank}", offset=bank * BANK)
             for e in range(e0, e1):
                 g = group_of[e]
                 for m in (1, 0):
                     nc.tensor.matmul_mx(
                         acc[:, (e - e0) * C : (e - e0 + 1) * C],
-                        lhsT=w13_w[m, k0][:, e, 2 * P * (kt - k0) : 2 * P * (kt - k0 + 1)].bitcast(FP4X4),
+                        lhsT=w13_w[m, kt][:, e, :].bitcast(FP4X4),
                         lhsT_scale=w13_s[m][:, e, P * kt : P * (kt + 1)],
                         rhs=da_w[g][:, m, columns(e)].bitcast(FP8X4),
                         rhs_scale=da_s[g][:, m, columns(e)],
@@ -216,30 +216,50 @@ def tile_moe_bdx_glu_sigmoid_kernel(
                     )
             nc.scalar.copy(dx[kt][:, e0 * C : e1 * C], acc[:, : (e1 - e0) * C])
 
-        for g, (e0, e1) in enumerate(groups):
-            make_sigmoid(g)
-            for e in range(e0, e1):
-                make_dh(e)
-            for e in range(e0, e1):
-                if e == e0 and e1 - e0 == 1:
-                    make_slope(e)
-                    quantise(g - 1)
-                    make_da3(e)
-                    continue
-                make_slope(e)
-                if e == e0 and g > 0:
-                    quantise(g - 1)
+        def front(u):
+            for e in (PAIR * u, PAIR * u + 1):
+                make_sigmoid(e)
+            make_sigmoid_minus(u)
+
+        front(0)
+        front(1)
+        for u in range(PAIRS):
+            first, second = PAIR * u, PAIR * u + 1
+            for e in (first, second):
+                first_product(e)
+            for e in (first, second):
                 make_da3(e)
-            make_da1(g)
-        quantise(len(groups) - 1)
-        second_product(0, 4, 0, 0)
-        second_product(4, 6, 0, 1)
-        second_product(6, 7, 0, 4)
-        second_product(7, 8, 0, 5, banks=2)
-        second_product(0, 4, 1, 7)
-        second_product(4, 8, 1, 5)
-        second_product(0, 4, 2, 2)
-        second_product(4, 8, 2, 6)
+            if u > 0:
+                quantise(u - 1, f"sig_t{second}")
+            if u == 0:
+                make_rest(u, nc.vector, "rest0", PAIR)
+            else:
+                make_rest(u, nc.gpsimd, ("sig_minus0", "da00", "da10")[u - 1], 1)
+            if u < 2:
+                front(u + 2)
+            if u == 2:
+                for m, name in enumerate(("dy_w", "g_w0")):
+                    w13_s[m] = keep.tile([P, E, K], U8, name=name, align_bytes=64)
+                    load_scales(nc.sync, w13_s[m], (w1_scales, w3_scales)[m])
+                for kt in range(KT):
+                    load_w13(kt)
+            for e in (first, second):
+                if u < PAIRS - 1:
+                    make_da1(e)
+                    round_da3(e)
+                else:
+                    round_da3(e)
+                    make_da1(e)
+        quantise(3, "da_w3")
+        quantise(4, "da_w4")
+        second_product(0, 4, 0, 6)
+        second_product(4, 6, 0, 7)
+        second_product(6, 7, 0, 2)
+        second_product(7, 8, 0, 3)
+        second_product(0, 4, 1, 0)
+        second_product(4, 8, 1, 1)
+        second_product(0, 4, 2, 5)
+        second_product(4, 8, 2, 4)
 
         pieces = [(0, 0, T), (1, 0, T), (2, 0, T - C), (2, T - C, T)]
         fetched = {}

@@ -64,13 +64,16 @@ def tile_moe_bdx_glu_sigmoid_kernel(
 
         w13_w, w13_s = {}, {}
 
-        def load_w13(kt):
+        def load_w13(e0, e1, k0, k1):
             for m in range(2):
-                w13_w[m, kt] = keep.tile([P, E, 2 * P], U8, name=f"w13_w{m}{kt}", align_bytes=64)
+                words = keep.tile([P, e1 - e0, 2 * P * (k1 - k0)], U8, name=f"w13_w{m}{e0}{k0}", align_bytes=64)
                 nc.sync.dma_start(
-                    w13_w[m, kt][:].bitcast(I32),
-                    (w1_words, w3_words)[m].rearrange("e s p b -> p (e s) b")[:, :, 2 * P * kt : 2 * P * (kt + 1)].bitcast(I32),
+                    words[:].bitcast(I32),
+                    (w1_words, w3_words)[m][e0:e1].rearrange("e s p b -> p (e s) b")[:, :, 2 * P * k0 : 2 * P * k1].bitcast(I32),
                 )
+                for e in range(e0, e1):
+                    for kt in range(k0, k1):
+                        w13_w[m, e, kt] = words[:, e - e0, 2 * P * (kt - k0) : 2 * P * (kt - k0 + 1)]
 
         w2_w = [keep.tile([P, PAIR * PASSES, 2 * H], U8, name=f"w2_w{u}", align_bytes=64) for u in range(PAIRS)]
         a1_cuts = ((0, 4), (4, 6), (6, 8))
@@ -114,9 +117,6 @@ def tile_moe_bdx_glu_sigmoid_kernel(
                     table[:, o : o + 2, :].rearrange("p o t -> p (o t)").indirect(offs_t[:, h * HALF // LIST : (h + 1) * HALF // LIST]),
                 )
 
-        gate_col = keep.tile([P, E], F32, name="gate_col")
-        nc.scalar.activation(gate_col[:], gate_ps[:, 0, :E], ACT.Copy)
-
         dx = [keep.tile([P, S], F32, name=f"dx{kt}") for kt in range(KT)]
         groups = [(0, 2), (2, 4), (4, 6), (6, 7), (7, 8)]
         group_of = {e: g for g, (e0, e1) in enumerate(groups) for e in range(e0, e1)}
@@ -137,7 +137,7 @@ def tile_moe_bdx_glu_sigmoid_kernel(
             return slice((e - e0) * C, (e - e0 + 1) * C)
 
         def make_sigmoid(e):
-            turned = psum.tile([P, PACK, P], F32, name=f"bank{6 + e % 2}", offset=(6 + e % 2) * BANK)
+            turned = psum.tile([P, PACK, P], F32, name=f"bank{5 + e % 2}", offset=(5 + e % 2) * BANK)
             for t in range(PACK):
                 nc.tensor.transpose(turned[:, t, :], saved(a1_t, e, e + 1)[:, t, :], ident[:])
             sig_t[e] = keep.tile([P, PACK, P], F32, name=f"sig_t{e}", align_bytes=64)
@@ -154,7 +154,7 @@ def tile_moe_bdx_glu_sigmoid_kernel(
                 engine.tensor_tensor(rest[u][:, :, cols], sig_minus[u][:, :, cols], saved(a3_t, PAIR * u, PAIR * (u + 1))[:, :, cols], ALU.mult)
 
         def first_product(e):
-            sums[e] = psum.tile([P, H], F32, name=f"bank{e % 3}", offset=e % 3 * BANK)
+            sums[e] = psum.tile([P, H], F32, name=f"bank{e % 2}", offset=e % 2 * BANK)
             for o in range(PASSES):
                 nc.tensor.matmul_mx(
                     sums[e][:],
@@ -169,8 +169,8 @@ def tile_moe_bdx_glu_sigmoid_kernel(
         def make_da3(e):
             da3_t = work.tile([P, PACK, P], F32, name="da3_t")
             nc.vector.scalar_tensor_tensor(
-                da3_t[:], sums[e][:].rearrange("c (q t) -> c t q", t=PACK), gate_col[:, e : e + 1], sig_t[e][:], ALU.mult, ALU.mult)
-            da3_ps[e] = psum.tile([P, PACK, C], F32, name=f"bank{3 + e % 3}", offset=(3 + e % 3) * BANK)
+                da3_t[:], sig_t[e][:], gate_ps[:, 0, e : e + 1], sums[e][:].rearrange("c (q t) -> c t q", t=PACK), ALU.mult, ALU.mult)
+            da3_ps[e] = psum.tile([P, PACK, C], F32, name=f"bank{2 + e % 3}", offset=(2 + e % 3) * BANK)
             for t in range(PACK):
                 nc.tensor.transpose(da3_ps[e][:, t, :], da3_t[:, t, :], ident[:])
 
@@ -207,7 +207,7 @@ def tile_moe_bdx_glu_sigmoid_kernel(
                 for m in (1, 0):
                     nc.tensor.matmul_mx(
                         acc[:, (e - e0) * C : (e - e0 + 1) * C],
-                        lhsT=w13_w[m, kt][:, e, :].bitcast(FP4X4),
+                        lhsT=w13_w[m, e, kt].bitcast(FP4X4),
                         lhsT_scale=w13_s[m][:, e, P * kt : P * (kt + 1)],
                         rhs=da_w[g][:, m, columns(e)].bitcast(FP8X4),
                         rhs_scale=da_s[g][:, m, columns(e)],
@@ -241,8 +241,9 @@ def tile_moe_bdx_glu_sigmoid_kernel(
                 for m, name in enumerate(("dy_w", "g_w0")):
                     w13_s[m] = keep.tile([P, E, K], U8, name=name, align_bytes=64)
                     load_scales(nc.sync, w13_s[m], (w1_scales, w3_scales)[m])
-                for kt in range(KT):
-                    load_w13(kt)
+                load_w13(0, E // 2, 0, KT - 1)
+                load_w13(E // 2, E, 0, KT - 1)
+                load_w13(0, E, KT - 1, KT)
             for e in (first, second):
                 if u < PAIRS - 1:
                     make_da1(e)
@@ -252,14 +253,14 @@ def tile_moe_bdx_glu_sigmoid_kernel(
                     make_da1(e)
         quantise(3, "da_w3")
         quantise(4, "da_w4")
-        second_product(0, 4, 0, 6)
-        second_product(4, 6, 0, 7)
-        second_product(6, 7, 0, 2)
-        second_product(7, 8, 0, 3)
-        second_product(0, 4, 1, 0)
-        second_product(4, 8, 1, 1)
-        second_product(0, 4, 2, 5)
-        second_product(4, 8, 2, 4)
+        second_product(0, 4, 0, 5)
+        second_product(4, 6, 0, 6)
+        second_product(6, 7, 0, 0)
+        second_product(7, 8, 0, 1)
+        second_product(0, 4, 1, 7)
+        second_product(4, 8, 1, 2)
+        second_product(0, 4, 2, 4)
+        second_product(4, 8, 2, 3)
 
         pieces = [(0, 0, T), (1, 0, T), (2, 0, T - C), (2, T - C, T)]
         fetched = {}

@@ -77,7 +77,7 @@ def tile_moe_bdx_glu_sigmoid_kernel(
 
         w2_w = [keep.tile([P, PAIR * PASSES, 2 * H], U8, name=f"w2_w{u}", align_bytes=64) for u in range(PAIRS)]
         a1_cuts = ((0, 4), (4, 6), (6, 8))
-        a3_cuts = ((0, 2), (2, 4), (4, 6), (6, 8))
+        a3_cuts = a1_cuts
         a1_t, a3_t = {}, {}
 
         def load_w2_words(u):
@@ -93,15 +93,17 @@ def tile_moe_bdx_glu_sigmoid_kernel(
         nc.sync.dma_start(gate_rows[0:E, :], gate[0].rearrange("(e c) -> e c", c=C))
         load_scales(nc.sync, w2_s[0], w2_scales[: E // 2])
         load_scales(nc.gpsimd, w2_s[1], w2_scales[E // 2 :])
-        load_saved(a3_t, a3, "a3_t", *a3_cuts[0])
+        w13_s[0] = keep.tile([P, E, K], U8, name="w1_s", align_bytes=64)
+        nc.gpsimd.memset(w13_s[0][:].bitcast(I32), 0)
+        load_scales(nc.gpsimd, w13_s[0], w1_scales)
         load_w2_words(1)
+        load_saved(a3_t, a3, "a3_t", *a3_cuts[0])
         load_saved(a1_t, a1, "a1_t", *a1_cuts[1])
-        load_saved(a3_t, a3, "a3_t", *a3_cuts[1])
-        load_saved(a1_t, a1, "a1_t", *a1_cuts[2])
         load_w2_words(2)
-        load_saved(a3_t, a3, "a3_t", *a3_cuts[2])
+        load_saved(a1_t, a1, "a1_t", *a1_cuts[2])
+        load_saved(a3_t, a3, "a3_t", *a3_cuts[1])
         load_w2_words(3)
-        load_saved(a3_t, a3, "a3_t", *a3_cuts[3])
+        load_saved(a3_t, a3, "a3_t", *a3_cuts[2])
         pos_t = [keep.tile([P, T // LIST], U16, name=f"pos_t{r}") for r in range(2)]
         nc.sync.dma_start(pos_t[0][:], pos1)
         nc.sync.dma_start(pos_t[1][:], pos2)
@@ -137,21 +139,21 @@ def tile_moe_bdx_glu_sigmoid_kernel(
             return slice((e - e0) * C, (e - e0 + 1) * C)
 
         def make_sigmoid(e):
-            turned = psum.tile([P, PACK, P], F32, name=f"bank{5 + e % 2}", offset=(5 + e % 2) * BANK)
+            bank = 4 if e == 5 else 5 + e % 2
+            turned = psum.tile([P, PACK, P], F32, name=f"bank{bank}", offset=bank * BANK)
             for t in range(PACK):
                 nc.tensor.transpose(turned[:, t, :], saved(a1_t, e, e + 1)[:, t, :], ident[:])
             sig_t[e] = keep.tile([P, PACK, P], F32, name=f"sig_t{e}", align_bytes=64)
             nc.scalar.activation(sig_t[e][:], turned[:], ACT.Sigmoid)
 
-        def make_sigmoid_minus(u):
-            sig_minus[u] = keep.tile([P, PACK, PAIR * C], F32, name=f"sig_minus{u}", align_bytes=64)
-            nc.scalar.activation(sig_minus[u][:], saved(a1_t, PAIR * u, PAIR * (u + 1)), ACT.Sigmoid, scale=-1.0)
+        def make_sigmoid_minus(e0, e1):
+            sig_minus[e0] = keep.tile([P, PACK, (e1 - e0) * C], F32, name=f"sig_minus{e0}", align_bytes=64)
+            nc.scalar.activation(sig_minus[e0][:], saved(a1_t, e0, e1), ACT.Sigmoid, scale=-1.0)
 
-        def make_rest(u, engine, name, parts):
-            rest[u] = keep.tile([P, PACK, PAIR * C], F32, name=name, align_bytes=64)
-            for c0 in range(0, PAIR * C, PAIR * C // parts):
-                cols = slice(c0, c0 + PAIR * C // parts)
-                engine.tensor_tensor(rest[u][:, :, cols], sig_minus[u][:, :, cols], saved(a3_t, PAIR * u, PAIR * (u + 1))[:, :, cols], ALU.mult)
+        def make_rest(engine, tile, first, e0, e1, made_from):
+            cols = slice((e0 - first) * C, (e1 - first) * C)
+            engine.tensor_tensor(
+                tile[:, :, cols], sig_minus[made_from][:, :, (e0 - made_from) * C : (e1 - made_from) * C], saved(a3_t, e0, e1), ALU.mult)
 
         def first_product(e):
             sums[e] = psum.tile([P, H], F32, name=f"bank{e % 2}", offset=e % 2 * BANK)
@@ -167,17 +169,22 @@ def tile_moe_bdx_glu_sigmoid_kernel(
                 )
 
         def make_da3(e):
-            da3_t = work.tile([P, PACK, P], F32, name="da3_t")
+            if e == PAIR:
+                da3_t = keep.tile([P, PACK, P], F32, name="sig_minus0", align_bytes=64)
+            else:
+                da3_t = work.tile([P, PACK, P], F32, name="da3_t")
             nc.vector.scalar_tensor_tensor(
                 da3_t[:], sig_t[e][:], gate_ps[:, 0, e : e + 1], sums[e][:].rearrange("c (q t) -> c t q", t=PACK), ALU.mult, ALU.mult)
             da3_ps[e] = psum.tile([P, PACK, C], F32, name=f"bank{2 + e % 3}", offset=(2 + e % 3) * BANK)
             for t in range(PACK):
                 nc.tensor.transpose(da3_ps[e][:, t, :], da3_t[:, t, :], ident[:])
 
+        takes_bytes_of = {(0, 1): "a1_t4", (1, 1): "a1_t6", (0, 0): "sig_t2", (1, 0): "a1_t4", (2, 0): "a1_t6"}
+
         def rounded(e, m):
             g = group_of[e]
             if (g, m) not in da:
-                name = f"a1_t{PAIR * (g + 2)}" if m == 1 and g < 2 else f"da{g}{m}"
+                name = takes_bytes_of.get((g, m), f"da{g}{m}")
                 da[g, m] = keep.tile([P, (groups[g][1] - e) * C, PACK], BF16, name=name, align_bytes=64)
             return da[g, m][:, columns(e)]
 
@@ -219,38 +226,48 @@ def tile_moe_bdx_glu_sigmoid_kernel(
         def front(u):
             for e in (PAIR * u, PAIR * u + 1):
                 make_sigmoid(e)
-            make_sigmoid_minus(u)
+            for e0, e1 in ((0, 1), (1, 2)) if u == 0 else ((PAIR * u, PAIR * (u + 1)),):
+                make_sigmoid_minus(e0, e1)
+
+        def finish(e):
+            if e < E - PAIR:
+                make_da1(e)
+                round_da3(e)
+            else:
+                round_da3(e)
+                make_da1(e)
 
         front(0)
         front(1)
-        for u in range(PAIRS):
-            first, second = PAIR * u, PAIR * u + 1
-            for e in (first, second):
-                first_product(e)
-            for e in (first, second):
-                make_da3(e)
-            if u > 0:
-                quantise(u - 1, f"sig_t{second}")
-            if u == 0:
-                make_rest(u, nc.vector, "rest0", PAIR)
-            else:
-                make_rest(u, nc.gpsimd, ("sig_minus0", "da00", "da10")[u - 1], 1)
-            if u < 2:
-                front(u + 2)
-            if u == 2:
-                for m, name in enumerate(("dy_w", "g_w0")):
-                    w13_s[m] = keep.tile([P, E, K], U8, name=name, align_bytes=64)
-                    load_scales(nc.sync, w13_s[m], (w1_scales, w3_scales)[m])
+        for e in range(PAIR):
+            first_product(e)
+            make_da3(e)
+        rest[0] = keep.tile([P, PACK, PAIR * C], F32, name="rest0", align_bytes=64)
+        for e in range(PAIR):
+            make_rest(nc.vector, rest[0], 0, e, e + 1, e)
+        rest[1] = keep.tile([P, PACK, PAIR * C], F32, name="sig_minus1", align_bytes=64)
+        make_rest(nc.gpsimd, rest[1], 2, 2, 4, 2)
+        front(2)
+        for e in range(PAIR, E):
+            first_product(e)
+            make_da3(e)
+            if e in (4, 6):
+                u = e // PAIR
+                quantise(u - 2, f"sig_t{e}")
+                rest[u] = keep.tile([P, PACK, PAIR * C], F32, name=("sig_t2", "a1_t4")[u - 2], align_bytes=64)
+                for e0, e1 in ((4, 6),) if e == 4 else ((6, 7), (7, 8)):
+                    make_rest(nc.gpsimd, rest[u], e, e0, e1, e)
+            finish(e - PAIR)
+            if e == 3:
+                front(3)
+                w13_s[1] = keep.tile([P, E, K], U8, name="dy_w", align_bytes=64)
+                load_scales(nc.sync, w13_s[1], w3_scales)
                 load_w13(0, E // 2, 0, KT - 1)
                 load_w13(E // 2, E, 0, KT - 1)
                 load_w13(0, E, KT - 1, KT)
-            for e in (first, second):
-                if u < PAIRS - 1:
-                    make_da1(e)
-                    round_da3(e)
-                else:
-                    round_da3(e)
-                    make_da1(e)
+        finish(6)
+        quantise(2, "bank_free_da_w2")
+        finish(7)
         quantise(3, "da_w3")
         quantise(4, "da_w4")
         second_product(0, 4, 0, 5)

@@ -43,23 +43,23 @@ def tile_moe_bdx_glu_sigmoid_kernel(
         nc.sync.dma_start(offs_t[:], offs)
 
         dy_s = keep.tile([P, PASSES + 1, T], U8, name="dy_s", align_bytes=64)
-        nc.gpsimd.memset(dy_s[:].bitcast(I32), 0)
+        nc.gpsimd.memset(dy_s[:, :PASSES, :].bitcast(I32), 0)
         for r in range(4):
             nc.sync.dma_start(dy_s[r:P:32, :PASSES, :].bitcast(I32), dy_scales.rearrange("o (q r) t -> r q o t", r=4)[r].bitcast(I32))
         dy_w = keep.tile([P, PASSES + 1, T], U32, name="dy_w", align_bytes=64)
 
-        w2_s = [keep.tile([P, E // 2 * PASSES, H], U8, name=f"w2_s{h}", align_bytes=64) for h in range(2)]
-        for plane in reversed(w2_s):
-            nc.vector.memset(plane[:].bitcast(I32), 0)
-
         gate_rows = keep.tile([P, C], F32, name="gate_rows", align_bytes=64)
-        nc.gpsimd.memset(gate_rows[:], 0.0)
         ident = keep.tile([P, P], F32, name="ident")
-        make_identity(nc, ident[:])
+        w2_s = [keep.tile([P, n * PASSES, H], U8, name=f"w2_s{n}", align_bytes=64) for n in (PAIR, E - PAIR)]
+        nc.vector.memset(ident[:], 0.0)
+        nc.vector.memset(gate_rows[:], 0.0)
+        for plane in w2_s:
+            nc.vector.memset(plane[:].bitcast(I32), 0)
+        make_identity(nc, ident[:], nomemset=True)
 
-        def load_scales(queue, plane, rows):
+        def load_scales(queues, plane, rows):
             by_row = rows.rearrange("e s (q r) i -> r q (e s) i", r=4)
-            for r in range(4):
+            for r, queue in enumerate(queues):
                 queue.dma_start(plane[r:P:32, :, :].bitcast(I32), by_row[r].bitcast(I32))
 
         w13_w, w13_s = {}, {}
@@ -91,11 +91,8 @@ def tile_moe_bdx_glu_sigmoid_kernel(
         load_w2_words(0)
         load_saved(a1_t, a1, "a1_t", *a1_cuts[0])
         nc.sync.dma_start(gate_rows[0:E, :], gate[0].rearrange("(e c) -> e c", c=C))
-        load_scales(nc.sync, w2_s[0], w2_scales[: E // 2])
-        load_scales(nc.gpsimd, w2_s[1], w2_scales[E // 2 :])
-        w13_s[0] = keep.tile([P, E, K], U8, name="w1_s", align_bytes=64)
-        nc.gpsimd.memset(w13_s[0][:].bitcast(I32), 0)
-        load_scales(nc.gpsimd, w13_s[0], w1_scales)
+        load_scales((nc.sync,) * 4, w2_s[0], w2_scales[:PAIR])
+        load_scales((nc.gpsimd, nc.gpsimd, nc.sync, nc.sync), w2_s[1], w2_scales[PAIR:])
         load_w2_words(1)
         load_saved(a3_t, a3, "a3_t", *a3_cuts[0])
         load_saved(a1_t, a1, "a1_t", *a1_cuts[1])
@@ -163,7 +160,7 @@ def tile_moe_bdx_glu_sigmoid_kernel(
                     lhsT=g_w[e // 4][:, o, e % 4 * C : (e % 4 + 1) * C].bitcast(FP8X4),
                     lhsT_scale=g_s[e // 4][:, o, e % 4 * C : (e % 4 + 1) * C],
                     rhs=w2_w[e // PAIR][:, e % PAIR * PASSES + o, :].bitcast(FP4X4),
-                    rhs_scale=w2_s[e // (E // 2)][:, e % (E // 2) * PASSES + o, :],
+                    rhs_scale=w2_s[0][:, e * PASSES + o, :] if e < PAIR else w2_s[1][:, (e - PAIR) * PASSES + o, :],
                     start=(o == 0),
                     stop=(o == PASSES - 1),
                 )
@@ -260,8 +257,10 @@ def tile_moe_bdx_glu_sigmoid_kernel(
             finish(e - PAIR)
             if e == 3:
                 front(3)
-                w13_s[1] = keep.tile([P, E, K], U8, name="dy_w", align_bytes=64)
-                load_scales(nc.sync, w13_s[1], w3_scales)
+            if e == 4:
+                for m, name in enumerate(("dy_w", "g_w0")):
+                    w13_s[m] = keep.tile([P, E, K], U8, name=name, align_bytes=64)
+                    load_scales((nc.sync,) * 4, w13_s[m], (w1_scales, w3_scales)[m])
                 load_w13(0, E // 2, 0, KT - 1)
                 load_w13(E // 2, E, 0, KT - 1)
                 load_w13(0, E, KT - 1, KT)

@@ -64,6 +64,13 @@ def tile_moe_bdx_glu_sigmoid_kernel(
 
         w13_w, w13_s = {}, {}
 
+        def load_w13_scales(k0, k1, names):
+            for m, name in enumerate(names):
+                plane = keep.tile([P, E, P * (k1 - k0)], U8, name=name, align_bytes=64)
+                load_scales((nc.sync,) * 4, plane, (w1_scales, w3_scales)[m][:, :, :, P * k0 : P * k1])
+                for kt in range(k0, k1):
+                    w13_s[m, kt] = plane[:, :, P * (kt - k0) : P * (kt - k0 + 1)]
+
         def load_w13(e0, e1, k0, k1):
             for m in range(2):
                 words = keep.tile([P, e1 - e0, 2 * P * (k1 - k0)], U8, name=f"w13_w{m}{e0}{k0}", align_bytes=64)
@@ -206,13 +213,13 @@ def tile_moe_bdx_glu_sigmoid_kernel(
 
         def second_product(e0, e1, kt, bank):
             acc = psum.tile([P, H], F32, name=f"bank{bank}", offset=bank * BANK)
-            for e in range(e0, e1):
+            for e in reversed(range(e0, e1)):
                 g = group_of[e]
                 for m in (1, 0):
                     nc.tensor.matmul_mx(
                         acc[:, (e - e0) * C : (e - e0 + 1) * C],
                         lhsT=w13_w[m, e, kt].bitcast(FP4X4),
-                        lhsT_scale=w13_s[m][:, e, P * kt : P * (kt + 1)],
+                        lhsT_scale=w13_s[m, kt][:, e, :],
                         rhs=da_w[g][:, m, columns(e)].bitcast(FP8X4),
                         rhs_scale=da_s[g][:, m, columns(e)],
                         start=(m == 1),
@@ -258,12 +265,12 @@ def tile_moe_bdx_glu_sigmoid_kernel(
             if e == 3:
                 front(3)
             if e == 4:
-                for m, name in enumerate(("dy_w", "g_w0")):
-                    w13_s[m] = keep.tile([P, E, K], U8, name=name, align_bytes=64)
-                    load_scales((nc.sync,) * 4, w13_s[m], (w1_scales, w3_scales)[m])
+                load_w13_scales(0, KT - 1, ("dy_w", "g_w0"))
                 load_w13(0, E // 2, 0, KT - 1)
-                load_w13(E // 2, E, 0, KT - 1)
-                load_w13(0, E, KT - 1, KT)
+                load_w13(E // 2, E, 0, 1)
+                load_w13(E // 2, E, 1, KT)
+                load_w13_scales(KT - 1, KT, ("w2_w0", "w2_w1"))
+                load_w13(0, E // 2, KT - 1, KT)
         finish(6)
         quantise(2, "bank_free_da_w2")
         finish(7)
@@ -275,7 +282,7 @@ def tile_moe_bdx_glu_sigmoid_kernel(
         second_product(7, 8, 0, 1)
         second_product(0, 4, 1, 7)
         second_product(4, 8, 1, 2)
-        second_product(0, 4, 2, 4)
+        second_product(0, 4, 2, 1)
         second_product(4, 8, 2, 3)
 
         pieces = [(0, 0, T), (1, 0, T), (2, 0, T - C), (2, T - C, T)]

@@ -20,13 +20,18 @@ ALU = mybir.AluOpType
 
 P = 128
 PACK = 4
+QUADRANT = 32
+ROWS = 4
 PASSES = N // (P * PACK)
 KT = K // P
 PAIR = 2
-PAIRS = E // PAIR
+MID = E // 2
 HALF = S // 2
 LIST = 16
 BANK = 2048
+W1, W3 = 0, 1
+
+SUM_BANKS, DA3_BANKS, A1_BANKS, GATE_BANK = (0, 1), (2, 3, 4), (5, 6), 7
 
 
 def tile_moe_bdx_glu_sigmoid_kernel(
@@ -39,80 +44,78 @@ def tile_moe_bdx_glu_sigmoid_kernel(
         work = ctx.enter_context(tc.tile_pool(name="work", bufs=4))
         psum = ctx.enter_context(tc.psum_pool(name="psum", bufs=1))
 
+        def bank_tile(bank, shape):
+            return psum.tile(shape, F32, name=f"bank{bank}", offset=bank * BANK)
+
         offs_t = keep.tile([P, S // LIST], U16, name="offs_t")
         nc.sync.dma_start(offs_t[:], offs)
 
         dy_s = keep.tile([P, PASSES + 1, T], U8, name="dy_s", align_bytes=64)
         nc.gpsimd.memset(dy_s[:, :PASSES, :].bitcast(I32), 0)
-        for r in range(4):
-            nc.sync.dma_start(dy_s[r:P:32, :PASSES, :].bitcast(I32), dy_scales.rearrange("o (q r) t -> r q o t", r=4)[r].bitcast(I32))
+        for r in range(ROWS):
+            nc.sync.dma_start(
+                dy_s[r:P:QUADRANT, :PASSES, :].bitcast(I32),
+                dy_scales.rearrange("o (q r) t -> r q o t", r=ROWS)[r].bitcast(I32),
+            )
         dy_w = keep.tile([P, PASSES + 1, T], U32, name="dy_w", align_bytes=64)
 
         gate_rows = keep.tile([P, C], F32, name="gate_rows", align_bytes=64)
         ident = keep.tile([P, P], F32, name="ident")
-        w2_s = [keep.tile([P, n * PASSES, H], U8, name=f"w2_s{n}", align_bytes=64) for n in (PAIR, E - PAIR)]
-        nc.vector.memset(ident[:], 0.0)
+        w2_s_first = keep.tile([P, PAIR * PASSES, H], U8, name="w2_s_first", align_bytes=64)
+        w2_s_others = keep.tile([P, (E - PAIR) * PASSES, H], U8, name="w2_s_others", align_bytes=64)
+        make_identity(nc, ident[:])
+        nc.vector.memset(w2_s_others[:].bitcast(I32), 0)
+        nc.vector.memset(w2_s_first[:].bitcast(I32), 0)
         nc.vector.memset(gate_rows[:], 0.0)
-        for plane in w2_s:
-            nc.vector.memset(plane[:].bitcast(I32), 0)
-        make_identity(nc, ident[:], nomemset=True)
 
         def load_scales(queues, plane, rows):
-            by_row = rows.rearrange("e s (q r) i -> r q (e s) i", r=4)
+            by_row = rows.rearrange("e s (q r) i -> r q (e s) i", r=ROWS)
             for r, queue in enumerate(queues):
-                queue.dma_start(plane[r:P:32, :, :].bitcast(I32), by_row[r].bitcast(I32))
+                queue.dma_start(plane[r:P:QUADRANT, :, :].bitcast(I32), by_row[r].bitcast(I32))
 
-        w13_w, w13_s = {}, {}
+        w2_w, w13_w, w13_s, a1_t, a3_t = {}, {}, {}, {}, {}
 
-        def load_w13_scales(k0, k1, names):
-            for m, name in enumerate(names):
-                plane = keep.tile([P, E, P * (k1 - k0)], U8, name=name, align_bytes=64)
-                load_scales((nc.sync,) * 4, plane, (w1_scales, w3_scales)[m][:, :, :, P * k0 : P * k1])
-                for kt in range(k0, k1):
-                    w13_s[m, kt] = plane[:, :, P * (kt - k0) : P * (kt - k0 + 1)]
-
-        def load_w13(e0, e1, k0, k1):
-            for m in range(2):
-                words = keep.tile([P, e1 - e0, 2 * P * (k1 - k0)], U8, name=f"w13_w{m}{e0}{k0}", align_bytes=64)
-                nc.sync.dma_start(
-                    words[:].bitcast(I32),
-                    (w1_words, w3_words)[m][e0:e1].rearrange("e s p b -> p (e s) b")[:, :, 2 * P * k0 : 2 * P * k1].bitcast(I32),
-                )
-                for e in range(e0, e1):
-                    for kt in range(k0, k1):
-                        w13_w[m, e, kt] = words[:, e - e0, 2 * P * (kt - k0) : 2 * P * (kt - k0 + 1)]
-
-        w2_w = [keep.tile([P, PAIR * PASSES, 2 * H], U8, name=f"w2_w{u}", align_bytes=64) for u in range(PAIRS)]
-        a1_cuts = ((0, 4), (4, 6), (6, 8))
-        a3_cuts = a1_cuts
-        a1_t, a3_t = {}, {}
-
-        def load_w2_words(u):
-            nc.sync.dma_start(w2_w[u][:].bitcast(I32), w2_words[PAIR * u : PAIR * (u + 1)].rearrange("e s p b -> p (e s) b").bitcast(I32))
+        def load_w2_words(e0, e1):
+            words = keep.tile([P, (e1 - e0) * PASSES, 2 * H], U8, name=f"w2_w{e0}", align_bytes=64)
+            nc.sync.dma_start(words[:].bitcast(I32), w2_words[e0:e1].rearrange("e s p b -> p (e s) b").bitcast(I32))
+            for e in range(e0, e1):
+                w2_w[e] = words[:, (e - e0) * PASSES : (e - e0 + 1) * PASSES, :]
 
         def load_saved(tiles, rows, name, e0, e1):
             tiles[e0, e1] = keep.tile([P, PACK, (e1 - e0) * C], F32, name=f"{name}{e0}", align_bytes=64)
             nc.sync.dma_start(tiles[e0, e1][:], rows.rearrange("(p t) j -> p t j", t=PACK)[:, :, e0 * C : e1 * C])
 
+        def load_w13_words(e0, e1, k0, k1):
+            for m, rows in ((W1, w1_words), (W3, w3_words)):
+                words = keep.tile([P, e1 - e0, 2 * P * (k1 - k0)], U8, name=f"w13_w{m}{e0}{k0}", align_bytes=64)
+                nc.sync.dma_start(
+                    words[:].bitcast(I32),
+                    rows[e0:e1].rearrange("e s p b -> p (e s) b")[:, :, 2 * P * k0 : 2 * P * k1].bitcast(I32),
+                )
+                for e in range(e0, e1):
+                    for kt in range(k0, k1):
+                        w13_w[m, e, kt] = words[:, e - e0, 2 * P * (kt - k0) : 2 * P * (kt - k0 + 1)]
+
         nc.sync.dma_start(dy_w[:, :PASSES, :].bitcast(I32), dy_words.rearrange("o p t d -> p o (t d)").bitcast(I32))
-        load_w2_words(0)
-        load_saved(a1_t, a1, "a1_t", *a1_cuts[0])
+        load_w2_words(0, PAIR)
+        load_saved(a1_t, a1, "a1_t", 0, MID)
         nc.sync.dma_start(gate_rows[0:E, :], gate[0].rearrange("(e c) -> e c", c=C))
-        load_scales((nc.sync,) * 4, w2_s[0], w2_scales[:PAIR])
-        load_scales((nc.gpsimd, nc.gpsimd, nc.sync, nc.sync), w2_s[1], w2_scales[PAIR:])
-        load_w2_words(1)
-        load_saved(a3_t, a3, "a3_t", *a3_cuts[0])
-        load_saved(a1_t, a1, "a1_t", *a1_cuts[1])
-        load_w2_words(2)
-        load_saved(a1_t, a1, "a1_t", *a1_cuts[2])
-        load_saved(a3_t, a3, "a3_t", *a3_cuts[1])
-        load_w2_words(3)
-        load_saved(a3_t, a3, "a3_t", *a3_cuts[2])
+        load_scales((nc.sync,) * ROWS, w2_s_first, w2_scales[:PAIR])
+        load_scales((nc.gpsimd, nc.gpsimd, nc.gpsimd, nc.sync), w2_s_others, w2_scales[PAIR:])
+        load_w2_words(PAIR, MID)
+        load_saved(a3_t, a3, "a3_t", 0, MID)
+        load_saved(a1_t, a1, "a1_t", MID, MID + PAIR)
+        load_w2_words(MID, MID + 1)
+        load_saved(a1_t, a1, "a1_t", MID + PAIR, E)
+        load_saved(a3_t, a3, "a3_t", MID, MID + PAIR)
+        for e in range(MID + 1, E):
+            load_w2_words(e, e + 1)
+        load_saved(a3_t, a3, "a3_t", MID + PAIR, E)
         pos_t = [keep.tile([P, T // LIST], U16, name=f"pos_t{r}") for r in range(2)]
         nc.sync.dma_start(pos_t[0][:], pos1)
         nc.sync.dma_start(pos_t[1][:], pos2)
 
-        gate_ps = psum.tile([P, PACK, C], F32, name="bank7", offset=7 * BANK)
+        gate_ps = bank_tile(GATE_BANK, [P, PACK, C])
         nc.tensor.transpose(gate_ps[:, 0, :], gate_rows[:], ident[:])
         g_s = [keep.tile([P, PASSES, HALF], U8, name=name, align_bytes=64) for name in ("g_s", "gate_rows")]
         g_w = [keep.tile([P, PASSES, HALF], U32, name=f"g_w{h}", align_bytes=64) for h in range(2)]
@@ -126,48 +129,42 @@ def tile_moe_bdx_glu_sigmoid_kernel(
         dx = [keep.tile([P, S], F32, name=f"dx{kt}") for kt in range(KT)]
         groups = [(0, 2), (2, 4), (4, 6), (6, 7), (7, 8)]
         group_of = {e: g for g, (e0, e1) in enumerate(groups) for e in range(e0, e1)}
-        da_w, da_s, da, sig_t, sig_minus, rest, sums, da3_ps = {}, {}, {}, {}, {}, {}, {}, {}
+        da_w, da_s, da, sig_t, sig_minus, factor, sums, da3_ps = {}, {}, {}, {}, {}, {}, {}, {}
 
         def saved(tiles, e0, e1):
             first, last = [cut for cut in tiles if cut[0] <= e0 < cut[1]][0]
             return tiles[first, last][:, :, (e0 - first) * C : (e1 - first) * C]
 
-        def pairs_of(planes):
-            return planes.rearrange("p t (c i) -> p c t i", i=2)
-
-        def woven(words):
-            return words.rearrange("p (c i) t -> p c t i", i=2)
-
         def columns(e):
             e0 = groups[group_of[e]][0]
             return slice((e - e0) * C, (e - e0 + 1) * C)
 
-        def make_sigmoid(e):
-            bank = 4 if e == 5 else 5 + e % 2
-            turned = psum.tile([P, PACK, P], F32, name=f"bank{bank}", offset=bank * BANK)
+        def make_sigmoid(e, bank):
+            turned = bank_tile(bank, [P, PACK, P])
             for t in range(PACK):
                 nc.tensor.transpose(turned[:, t, :], saved(a1_t, e, e + 1)[:, t, :], ident[:])
             sig_t[e] = keep.tile([P, PACK, P], F32, name=f"sig_t{e}", align_bytes=64)
             nc.scalar.activation(sig_t[e][:], turned[:], ACT.Sigmoid)
 
         def make_sigmoid_minus(e0, e1):
-            sig_minus[e0] = keep.tile([P, PACK, (e1 - e0) * C], F32, name=f"sig_minus{e0}", align_bytes=64)
-            nc.scalar.activation(sig_minus[e0][:], saved(a1_t, e0, e1), ACT.Sigmoid, scale=-1.0)
+            tile = keep.tile([P, PACK, (e1 - e0) * C], F32, name=f"sig_minus{e0}", align_bytes=64)
+            nc.scalar.activation(tile[:], saved(a1_t, e0, e1), ACT.Sigmoid, scale=-1.0)
+            sig_minus[e0, e1] = tile
 
-        def make_rest(engine, tile, first, e0, e1, made_from):
-            cols = slice((e0 - first) * C, (e1 - first) * C)
-            engine.tensor_tensor(
-                tile[:, :, cols], sig_minus[made_from][:, :, (e0 - made_from) * C : (e1 - made_from) * C], saved(a3_t, e0, e1), ALU.mult)
+        def make_factor(engine, name, first, cuts):
+            factor[first, first + PAIR] = keep.tile([P, PACK, PAIR * C], F32, name=name, align_bytes=64)
+            for e0, e1 in cuts:
+                engine.tensor_tensor(saved(factor, e0, e1), saved(sig_minus, e0, e1), saved(a3_t, e0, e1), ALU.mult)
 
         def first_product(e):
-            sums[e] = psum.tile([P, H], F32, name=f"bank{e % 2}", offset=e % 2 * BANK)
+            sums[e] = bank_tile(SUM_BANKS[e % len(SUM_BANKS)], [P, H])
             for o in range(PASSES):
                 nc.tensor.matmul_mx(
                     sums[e][:],
-                    lhsT=g_w[e // 4][:, o, e % 4 * C : (e % 4 + 1) * C].bitcast(FP8X4),
-                    lhsT_scale=g_s[e // 4][:, o, e % 4 * C : (e % 4 + 1) * C],
-                    rhs=w2_w[e // PAIR][:, e % PAIR * PASSES + o, :].bitcast(FP4X4),
-                    rhs_scale=w2_s[0][:, e * PASSES + o, :] if e < PAIR else w2_s[1][:, (e - PAIR) * PASSES + o, :],
+                    lhsT=g_w[e // MID][:, o, e % MID * C : (e % MID + 1) * C].bitcast(FP8X4),
+                    lhsT_scale=g_s[e // MID][:, o, e % MID * C : (e % MID + 1) * C],
+                    rhs=w2_w[e][:, o, :].bitcast(FP4X4),
+                    rhs_scale=w2_s_first[:, e * PASSES + o, :] if e < PAIR else w2_s_others[:, (e - PAIR) * PASSES + o, :],
                     start=(o == 0),
                     stop=(o == PASSES - 1),
                 )
@@ -178,12 +175,12 @@ def tile_moe_bdx_glu_sigmoid_kernel(
             else:
                 da3_t = work.tile([P, PACK, P], F32, name="da3_t")
             nc.vector.scalar_tensor_tensor(
-                da3_t[:], sig_t[e][:], gate_ps[:, 0, e : e + 1], sums[e][:].rearrange("c (q t) -> c t q", t=PACK), ALU.mult, ALU.mult)
-            da3_ps[e] = psum.tile([P, PACK, C], F32, name=f"bank{2 + e % 3}", offset=(2 + e % 3) * BANK)
+                da3_t[:], sig_t[e][:], gate_ps[:, 0, e : e + 1], sums[e][:].rearrange("c (p t) -> c t p", t=PACK), ALU.mult, ALU.mult)
+            da3_ps[e] = bank_tile(DA3_BANKS[e % len(DA3_BANKS)], [P, PACK, C])
             for t in range(PACK):
                 nc.tensor.transpose(da3_ps[e][:, t, :], da3_t[:, t, :], ident[:])
 
-        takes_bytes_of = {(0, 1): "a1_t4", (1, 1): "a1_t6", (0, 0): "sig_t2", (1, 0): "a1_t4", (2, 0): "a1_t6"}
+        takes_bytes_of = {(0, W3): "a1_t4", (1, W3): "a1_t6", (0, W1): "sig_t2", (1, W1): "a1_t4", (2, W1): "a1_t6"}
 
         def rounded(e, m):
             g = group_of[e]
@@ -193,114 +190,118 @@ def tile_moe_bdx_glu_sigmoid_kernel(
             return da[g, m][:, columns(e)]
 
         def round_da3(e):
-            nc.scalar.copy(rounded(e, 1), da3_ps[e][:].rearrange("p t c -> p c t"))
+            nc.scalar.copy(rounded(e, W3), da3_ps[e][:].rearrange("p t c -> p c t"))
 
         def make_da1(e):
             nc.vector.tensor_tensor(
-                woven(rounded(e, 0)),
-                pairs_of(rest[e // PAIR][:, :, e % PAIR * C : (e % PAIR + 1) * C]),
-                pairs_of(da3_ps[e][:]),
+                rounded(e, W1).rearrange("p (c i) t -> p c t i", i=2),
+                saved(factor, e, e + 1).rearrange("p t (c i) -> p c t i", i=2),
+                da3_ps[e][:].rearrange("p t (c i) -> p c t i", i=2),
                 ALU.mult,
             )
+
+        def finish(e):
+            for step in (make_da1, round_da3) if e < E - PAIR else (round_da3, make_da1):
+                step(e)
 
         def quantise(g, name):
             e0, e1 = groups[g]
             da_w[g] = keep.tile([P, 2, (e1 - e0) * C], U32, name=name, align_bytes=64)
             da_s[g] = keep.tile([P, 2, (e1 - e0) * C], U8, name=f"da_s{g}", align_bytes=64)
-            for m in (1, 0):
+            for m in (W3, W1):
                 nc.vector.quantize_mx(
-                    out=da_w[g][:, m, :].bitcast(FP8X4), scales=da_s[g][:, m, :], in_=da[g, m][:].rearrange("p j t -> p (j t)"))
+                    out=da_w[g][:, m, :].bitcast(FP8X4), scales=da_s[g][:, m, :], in_=da[g, m][:].rearrange("p c t -> p (c t)"))
 
         def second_product(e0, e1, kt, bank):
-            acc = psum.tile([P, H], F32, name=f"bank{bank}", offset=bank * BANK)
+            acc = bank_tile(bank, [P, H])
             for e in reversed(range(e0, e1)):
                 g = group_of[e]
-                for m in (1, 0):
+                for m in (W3, W1):
                     nc.tensor.matmul_mx(
                         acc[:, (e - e0) * C : (e - e0 + 1) * C],
                         lhsT=w13_w[m, e, kt].bitcast(FP4X4),
-                        lhsT_scale=w13_s[m, kt][:, e, :],
+                        lhsT_scale=w13_s[m][:, e, P * kt : P * (kt + 1)],
                         rhs=da_w[g][:, m, columns(e)].bitcast(FP8X4),
                         rhs_scale=da_s[g][:, m, columns(e)],
-                        start=(m == 1),
-                        stop=(m == 0),
+                        start=(m == W3),
+                        stop=(m == W1),
                     )
             nc.scalar.copy(dx[kt][:, e0 * C : e1 * C], acc[:, : (e1 - e0) * C])
 
-        def front(u):
-            for e in (PAIR * u, PAIR * u + 1):
-                make_sigmoid(e)
-            for e0, e1 in ((0, 1), (1, 2)) if u == 0 else ((PAIR * u, PAIR * (u + 1)),):
+        def singly(first):
+            return ((first, first + 1), (first + 1, first + PAIR))
+
+        def together(first):
+            return ((first, first + PAIR),)
+
+        def sigmoids(first, banks, cuts):
+            for e, bank in zip((first, first + 1), banks):
+                make_sigmoid(e, bank)
+            for e0, e1 in cuts:
                 make_sigmoid_minus(e0, e1)
 
-        def finish(e):
-            if e < E - PAIR:
-                make_da1(e)
-                round_da3(e)
-            else:
-                round_da3(e)
-                make_da1(e)
-
-        front(0)
-        front(1)
+        sigmoids(0, A1_BANKS, singly(0))
+        sigmoids(2, A1_BANKS, together(2))
         for e in range(PAIR):
             first_product(e)
             make_da3(e)
-        rest[0] = keep.tile([P, PACK, PAIR * C], F32, name="rest0", align_bytes=64)
-        for e in range(PAIR):
-            make_rest(nc.vector, rest[0], 0, e, e + 1, e)
-        rest[1] = keep.tile([P, PACK, PAIR * C], F32, name="sig_minus1", align_bytes=64)
-        make_rest(nc.gpsimd, rest[1], 2, 2, 4, 2)
-        front(2)
-        for e in range(PAIR, E):
+        make_factor(nc.vector, "factor0", 0, singly(0))
+        make_factor(nc.gpsimd, "sig_minus1", 2, together(2))
+        sigmoids(4, (A1_BANKS[0], DA3_BANKS[2]), together(4))
+        for e in (2, 3):
             first_product(e)
             make_da3(e)
-            if e in (4, 6):
-                u = e // PAIR
-                quantise(u - 2, f"sig_t{e}")
-                rest[u] = keep.tile([P, PACK, PAIR * C], F32, name=("sig_t2", "a1_t4")[u - 2], align_bytes=64)
-                for e0, e1 in ((4, 6),) if e == 4 else ((6, 7), (7, 8)):
-                    make_rest(nc.gpsimd, rest[u], e, e0, e1, e)
             finish(e - PAIR)
-            if e == 3:
-                front(3)
-            if e == 4:
-                load_w13_scales(0, KT - 1, ("dy_w", "g_w0"))
-                load_w13(0, E // 2, 0, KT - 1)
-                load_w13(E // 2, E, 0, 1)
-                load_w13(E // 2, E, 1, KT)
-                load_w13_scales(KT - 1, KT, ("w2_w0", "w2_w1"))
-                load_w13(0, E // 2, KT - 1, KT)
+        sigmoids(6, A1_BANKS, together(6))
+
+        first_product(4)
+        make_da3(4)
+        quantise(0, "sig_t4")
+        make_factor(nc.gpsimd, takes_bytes_of[0, W1], 4, together(4))
+        finish(2)
+
+        for m, name, rows in ((W1, "dy_w", w1_scales), (W3, "g_w0", w3_scales)):
+            w13_s[m] = keep.tile([P, E, K], U8, name=name, align_bytes=64)
+            load_scales((nc.sync,) * ROWS, w13_s[m], rows)
+        load_w13_words(0, MID, 0, KT - 1)
+        load_w13_words(MID, E, 0, 1)
+        load_w13_words(MID, E, 1, KT)
+        load_w13_words(0, MID, KT - 1, KT)
+
+        first_product(5)
+        make_da3(5)
+        finish(3)
+        first_product(6)
+        make_da3(6)
+        quantise(1, "sig_t6")
+        make_factor(nc.gpsimd, takes_bytes_of[1, W1], 6, singly(6))
+        finish(4)
+        first_product(7)
+        make_da3(7)
+        finish(5)
         finish(6)
-        quantise(2, "bank_free_da_w2")
+        quantise(2, "da_w2")
         finish(7)
         quantise(3, "da_w3")
         quantise(4, "da_w4")
-        second_product(0, 4, 0, 5)
-        second_product(4, 6, 0, 6)
-        second_product(6, 7, 0, 0)
-        second_product(7, 8, 0, 1)
-        second_product(0, 4, 1, 7)
-        second_product(4, 8, 1, 2)
-        second_product(0, 4, 2, 1)
-        second_product(4, 8, 2, 3)
 
-        pieces = [(0, 0, T), (1, 0, T), (2, 0, T - C), (2, T - C, T)]
-        fetched = {}
+        second_product(0, MID, 0, A1_BANKS[0])
+        second_product(*groups[2], 0, A1_BANKS[1])
+        second_product(*groups[3], 0, SUM_BANKS[0])
+        second_product(*groups[4], 0, SUM_BANKS[1])
+        second_product(MID, E, 1, SUM_BANKS[0])
+        second_product(0, MID, 1, SUM_BANKS[1])
+        second_product(MID, E, 2, DA3_BANKS[0])
+        second_product(0, MID, 2, SUM_BANKS[0])
 
-        def fetch(i):
-            kt, t0, t1 = pieces[i]
-            fetched[i] = work.tile([P, t1 - t0], F32, name="fetched")
-            nc.vector.tensor_copy(fetched[i][:], dx[kt][:].indirect(pos_t[0][:, t0 // LIST : t1 // LIST]))
-
-        def combine(i):
-            kt, t0, t1 = pieces[i]
-            total = work.tile([P, t1 - t0], F32, name="total")
-            nc.vector.tensor_tensor(total[:], dx[kt][:].indirect(pos_t[1][:, t0 // LIST : t1 // LIST]), fetched[i][:], ALU.add)
-            nc.sync.dma_start(out[kt * P : (kt + 1) * P, t0:t1], total[:])
-
-        fetch(0)
-        for i in range(len(pieces)):
-            if i + 1 < len(pieces):
-                fetch(i + 1)
-            combine(i)
+        for kt in range(KT):
+            cut = T // 2 if kt < KT - 1 else T - C
+            pieces = ((0, cut), (cut, T))
+            fetched = {}
+            for t0, t1 in pieces:
+                fetched[t0] = work.tile([P, t1 - t0], F32, name="fetched")
+                nc.vector.tensor_copy(fetched[t0][:], dx[kt][:].indirect(pos_t[0][:, t0 // LIST : t1 // LIST]))
+            for t0, t1 in pieces:
+                total = work.tile([P, t1 - t0], F32, name="total")
+                nc.vector.tensor_tensor(total[:], dx[kt][:].indirect(pos_t[1][:, t0 // LIST : t1 // LIST]), fetched[t0][:], ALU.add)
+                nc.sync.dma_start(out[kt * P : (kt + 1) * P, t0:t1], total[:])

@@ -212,7 +212,7 @@ def tile_moe_bdx_glu_sigmoid_kernel(
                 nc.vector.quantize_mx(
                     out=da_w[g][:, m, :].bitcast(FP8X4), scales=da_s[g][:, m, :], in_=da[g, m][:].rearrange("p c t -> p (c t)"))
 
-        def second_product(e0, e1, kt, bank):
+        def second_product(e0, e1, kt, bank, copier=nc.scalar.copy):
             acc = bank_tile(bank, [P, H])
             for e in reversed(range(e0, e1)):
                 g = group_of[e]
@@ -226,7 +226,7 @@ def tile_moe_bdx_glu_sigmoid_kernel(
                         start=(m == W3),
                         stop=(m == W1),
                     )
-            nc.scalar.copy(dx[kt][:, e0 * C : e1 * C], acc[:, : (e1 - e0) * C])
+            copier(dx[kt][:, e0 * C : e1 * C], acc[:, : (e1 - e0) * C])
 
         def singly(first):
             return ((first, first + 1), (first + 1, first + PAIR))
@@ -291,17 +291,14 @@ def tile_moe_bdx_glu_sigmoid_kernel(
         second_product(*groups[4], 0, SUM_BANKS[1])
         second_product(MID, E, 1, SUM_BANKS[0])
         second_product(0, MID, 1, SUM_BANKS[1])
-        second_product(MID, E, 2, DA3_BANKS[0])
-        second_product(0, MID, 2, SUM_BANKS[0])
+        second_product(MID, E, 2, DA3_BANKS[0], nc.vector.tensor_copy)
+        second_product(0, MID, 2, DA3_BANKS[1], nc.vector.tensor_copy)
 
+        cuts = ((0, 2 * C, T), (0, 2 * C, T), (0, 2 * C, 3 * C, T))
         for kt in range(KT):
-            cut = T // 2 if kt < KT - 1 else T - C
-            pieces = ((0, cut), (cut, T))
-            fetched = {}
-            for t0, t1 in pieces:
-                fetched[t0] = work.tile([P, t1 - t0], F32, name="fetched")
-                nc.vector.tensor_copy(fetched[t0][:], dx[kt][:].indirect(pos_t[0][:, t0 // LIST : t1 // LIST]))
-            for t0, t1 in pieces:
-                total = work.tile([P, t1 - t0], F32, name="total")
-                nc.vector.tensor_tensor(total[:], dx[kt][:].indirect(pos_t[1][:, t0 // LIST : t1 // LIST]), fetched[t0][:], ALU.add)
+            for t0, t1 in zip(cuts[kt], cuts[kt][1:]):
+                fetched = keep.tile([P, t1 - t0], F32, name=f"fetched{kt}_{t0}")
+                nc.scalar.activation(fetched[:], dx[kt][:].indirect(pos_t[0][:, t0 // LIST : t1 // LIST]), ACT.Copy)
+                total = keep.tile([P, t1 - t0], F32, name=f"total{kt}_{t0}")
+                nc.vector.tensor_tensor(total[:], dx[kt][:].indirect(pos_t[1][:, t0 // LIST : t1 // LIST]), fetched[:], ALU.add)
                 nc.sync.dma_start(out[kt * P : (kt + 1) * P, t0:t1], total[:])

@@ -50,6 +50,9 @@ def tile_moe_bdx_glu_sigmoid_kernel(
         offs_t = keep.tile([P, S // LIST], U16, name="offs_t")
         nc.sync.dma_start(offs_t[:], offs)
 
+        dy_w = keep.tile([P, PASSES + 1, T], U32, name="dy_w", align_bytes=64)
+        for o in range(PASSES):
+            nc.sync.dma_start(dy_w[:, PASSES - 1 - o, :].bitcast(I32), dy_words[o].rearrange("p t d -> p (t d)").bitcast(I32))
         dy_s = keep.tile([P, PASSES + 1, T], U8, name="dy_s", align_bytes=64)
         nc.gpsimd.memset(dy_s[:, :PASSES, :].bitcast(I32), 0)
         for r in range(ROWS):
@@ -57,7 +60,6 @@ def tile_moe_bdx_glu_sigmoid_kernel(
                 dy_s[r:P:QUADRANT, :PASSES, :].bitcast(I32),
                 dy_scales.rearrange("o (q r) t -> r q o t", r=ROWS)[r].bitcast(I32),
             )
-        dy_w = keep.tile([P, PASSES + 1, T], U32, name="dy_w", align_bytes=64)
 
         gate_rows = keep.tile([P, C], F32, name="gate_rows", align_bytes=64)
         ident = keep.tile([P, P], F32, name="ident")
@@ -68,9 +70,9 @@ def tile_moe_bdx_glu_sigmoid_kernel(
         nc.vector.memset(w2_s_first[:].bitcast(I32), 0)
         nc.vector.memset(gate_rows[:], 0.0)
 
-        def load_scales(queues, plane, rows):
+        def load_scales(queue, plane, rows, r0, r1):
             by_row = rows.rearrange("e s (q r) i -> r q (e s) i", r=ROWS)
-            for r, queue in enumerate(queues):
+            for r in range(r0, r1):
                 queue.dma_start(plane[r:P:QUADRANT, :, :].bitcast(I32), by_row[r].bitcast(I32))
 
         w2_w, w13_w, w13_s, a1_t, a3_t = {}, {}, {}, {}, {}
@@ -85,8 +87,8 @@ def tile_moe_bdx_glu_sigmoid_kernel(
             tiles[e0, e1] = keep.tile([P, PACK, (e1 - e0) * C], F32, name=f"{name}{e0}", align_bytes=64)
             nc.sync.dma_start(tiles[e0, e1][:], rows.rearrange("(p t) j -> p t j", t=PACK)[:, :, e0 * C : e1 * C])
 
-        def load_w13_words(e0, e1, k0, k1):
-            for m, rows in ((W1, w1_words), (W3, w3_words)):
+        def load_w13_words(e0, e1, k0, k1, matrices=((W3, w3_words), (W1, w1_words))):
+            for m, rows in matrices:
                 words = keep.tile([P, e1 - e0, 2 * P * (k1 - k0)], U8, name=f"w13_w{m}{e0}{k0}", align_bytes=64)
                 nc.sync.dma_start(
                     words[:].bitcast(I32),
@@ -96,34 +98,35 @@ def tile_moe_bdx_glu_sigmoid_kernel(
                     for kt in range(k0, k1):
                         w13_w[m, e, kt] = words[:, e - e0, 2 * P * (kt - k0) : 2 * P * (kt - k0 + 1)]
 
-        nc.sync.dma_start(dy_w[:, :PASSES, :].bitcast(I32), dy_words.rearrange("o p t d -> p o (t d)").bitcast(I32))
         load_w2_words(0, PAIR)
         load_saved(a1_t, a1, "a1_t", 0, MID)
         nc.sync.dma_start(gate_rows[0:E, :], gate[0].rearrange("(e c) -> e c", c=C))
-        load_scales((nc.sync,) * ROWS, w2_s_first, w2_scales[:PAIR])
-        load_scales((nc.gpsimd, nc.gpsimd, nc.gpsimd, nc.sync), w2_s_others, w2_scales[PAIR:])
+        load_scales(nc.sync, w2_s_first, w2_scales[:PAIR], 0, 2)
         load_w2_words(PAIR, MID)
+        load_scales(nc.sync, w2_s_first, w2_scales[:PAIR], 2, ROWS)
         load_saved(a3_t, a3, "a3_t", 0, MID)
+        load_scales(nc.gpsimd, w2_s_others, w2_scales[PAIR:], 0, ROWS - 1)
+        load_scales(nc.sync, w2_s_others, w2_scales[PAIR:], ROWS - 1, ROWS)
+        pos_t = [keep.tile([P, T // LIST], U16, name=f"pos_t{r}") for r in range(2)]
         load_saved(a1_t, a1, "a1_t", MID, MID + PAIR)
         load_w2_words(MID, MID + 1)
         load_saved(a1_t, a1, "a1_t", MID + PAIR, E)
+        nc.sync.dma_start(pos_t[0][:], pos1)
         load_saved(a3_t, a3, "a3_t", MID, MID + PAIR)
+        nc.sync.dma_start(pos_t[1][:], pos2)
         for e in range(MID + 1, E):
             load_w2_words(e, e + 1)
         load_saved(a3_t, a3, "a3_t", MID + PAIR, E)
-        pos_t = [keep.tile([P, T // LIST], U16, name=f"pos_t{r}") for r in range(2)]
-        nc.sync.dma_start(pos_t[0][:], pos1)
-        nc.sync.dma_start(pos_t[1][:], pos2)
 
         gate_ps = bank_tile(GATE_BANK, [P, PACK, C])
         nc.tensor.transpose(gate_ps[:, 0, :], gate_rows[:], ident[:])
         g_s = [keep.tile([P, PASSES, HALF], U8, name=name, align_bytes=64) for name in ("g_s", "gate_rows")]
         g_w = [keep.tile([P, PASSES, HALF], U32, name=f"g_w{h}", align_bytes=64) for h in range(2)]
-        for gathered, table, h in ((g_s, dy_s, 0), (g_w, dy_w, 0), (g_w, dy_w, 1), (g_s, dy_s, 1)):
-            for o in range(PASSES):
+        for gathered, table, rows, h in ((g_w, dy_w, (1, 0), 0), (g_s, dy_s, (0, 1), 0), (g_w, dy_w, (1, 0), 1), (g_s, dy_s, (0, 1), 1)):
+            for o, row in enumerate(rows):
                 nc.vector.tensor_copy(
                     gathered[h][:, o, :],
-                    table[:, o : o + 2, :].rearrange("p o t -> p (o t)").indirect(offs_t[:, h * HALF // LIST : (h + 1) * HALF // LIST]),
+                    table[:, row : row + 2, :].rearrange("p o t -> p (o t)").indirect(offs_t[:, h * HALF // LIST : (h + 1) * HALF // LIST]),
                 )
 
         dx = [keep.tile([P, S], F32, name=f"dx{kt}") for kt in range(KT)]
@@ -260,11 +263,12 @@ def tile_moe_bdx_glu_sigmoid_kernel(
         make_factor(nc.gpsimd, takes_bytes_of[0, W1], 4, together(4))
         finish(2)
 
-        for m, name, rows in ((W1, "dy_w", w1_scales), (W3, "g_w0", w3_scales)):
+        for m, name in ((W1, "dy_w"), (W3, "g_w0")):
             w13_s[m] = keep.tile([P, E, K], U8, name=name, align_bytes=64)
-            load_scales((nc.sync,) * ROWS, w13_s[m], rows)
-        load_w13_words(0, MID, 0, KT - 1)
-        load_w13_words(MID, E, 0, 1)
+        for e0, k1 in ((0, KT - 1), (MID, 1)):
+            for m, rows, words in ((W1, w1_scales, w1_words), (W3, w3_scales, w3_words)):
+                load_scales(nc.sync, w13_s[m], rows, e0 // 2, e0 // 2 + 2)
+                load_w13_words(e0, e0 + MID, 0, k1, ((m, words),))
         load_w13_words(MID, E, 1, KT)
         load_w13_words(0, MID, KT - 1, KT)
 

@@ -215,13 +215,16 @@ def tile_moe_bdx_glu_sigmoid_kernel(
                 nc.vector.quantize_mx(
                     out=da_w[g][:, m, :].bitcast(FP8X4), scales=da_s[g][:, m, :], in_=da[g, m][:].rearrange("p c t -> p (c t)"))
 
-        def second_product(e0, e1, kt, bank, copier=nc.scalar.copy):
-            acc = bank_tile(bank, [P, H])
-            for e in reversed(range(e0, e1)):
+        acc = {}
+
+        def second_product(experts, kt, bank):
+            if bank not in acc:
+                acc[bank] = bank_tile(bank, [P, MID * C])
+            for e in experts:
                 g = group_of[e]
                 for m in (W3, W1):
                     nc.tensor.matmul_mx(
-                        acc[:, (e - e0) * C : (e - e0 + 1) * C],
+                        acc[bank][:, e % MID * C : (e % MID + 1) * C],
                         lhsT=w13_w[m, e, kt].bitcast(FP4X4),
                         lhsT_scale=w13_s[m][:, e, P * kt : P * (kt + 1)],
                         rhs=da_w[g][:, m, columns(e)].bitcast(FP8X4),
@@ -229,7 +232,9 @@ def tile_moe_bdx_glu_sigmoid_kernel(
                         start=(m == W3),
                         stop=(m == W1),
                     )
-            copier(dx[kt][:, e0 * C : e1 * C], acc[:, : (e1 - e0) * C])
+
+        def copy_dx(copier, e0, e1, kt, bank):
+            copier(dx[kt][:, e0 * C : e1 * C], acc[bank][:, e0 % MID * C : ((e1 - 1) % MID + 1) * C])
 
         def singly(first):
             return ((first, first + 1), (first + 1, first + PAIR))
@@ -265,12 +270,11 @@ def tile_moe_bdx_glu_sigmoid_kernel(
 
         for m, name in ((W1, "dy_w"), (W3, "g_w0")):
             w13_s[m] = keep.tile([P, E, K], U8, name=name, align_bytes=64)
-        for e0, k1 in ((0, KT - 1), (MID, 1)):
+        for e0 in (0, MID):
             for m, rows, words in ((W1, w1_scales, w1_words), (W3, w3_scales, w3_words)):
                 load_scales(nc.sync, w13_s[m], rows, e0 // 2, e0 // 2 + 2)
-                load_w13_words(e0, e0 + MID, 0, k1, ((m, words),))
-        load_w13_words(MID, E, 1, KT)
-        load_w13_words(0, MID, KT - 1, KT)
+                load_w13_words(e0, e0 + MID, 0, KT - 1, ((m, words),))
+        load_w13_words(0, E, KT - 1, KT)
 
         first_product(5)
         make_da3(5)
@@ -289,14 +293,19 @@ def tile_moe_bdx_glu_sigmoid_kernel(
         quantise(3, "da_w3")
         quantise(4, "da_w4")
 
-        second_product(0, MID, 0, A1_BANKS[0])
-        second_product(*groups[2], 0, A1_BANKS[1])
-        second_product(*groups[3], 0, SUM_BANKS[0])
-        second_product(*groups[4], 0, SUM_BANKS[1])
-        second_product(MID, E, 1, SUM_BANKS[0])
-        second_product(0, MID, 1, SUM_BANKS[1])
-        second_product(MID, E, 2, DA3_BANKS[0], nc.vector.tensor_copy)
-        second_product(0, MID, 2, DA3_BANKS[1], nc.vector.tensor_copy)
+        for kt in (0, 1):
+            second_product(range(MID), kt, A1_BANKS[kt])
+            copy_dx(nc.scalar.copy, 0, MID, kt, A1_BANKS[kt])
+        for g in (2, 3, 4):
+            for kt, bank in enumerate((SUM_BANKS[0] if g < 4 else SUM_BANKS[1], GATE_BANK)):
+                second_product(range(*groups[g]), kt, bank)
+            if g == 3:
+                copy_dx(nc.scalar.copy, MID, E - 1, 0, SUM_BANKS[0])
+        copy_dx(nc.scalar.copy, E - 1, E, 0, SUM_BANKS[1])
+        copy_dx(nc.vector.tensor_copy, MID, E, 1, GATE_BANK)
+        for e0, bank, copier in ((0, DA3_BANKS[2], nc.vector.tensor_copy), (MID, DA3_BANKS[0], nc.scalar.copy)):
+            second_product(range(e0, e0 + MID), 2, bank)
+            copy_dx(copier, e0, e0 + MID, 2, bank)
 
         cuts = ((0, 2 * C, T), (0, 2 * C, T), (0, 2 * C, 3 * C, T))
         for kt in range(KT):

@@ -32,6 +32,7 @@ BANK = 2048
 W1, W3 = 0, 1
 
 SUM_BANKS, DA3_BANKS, A1_BANKS, GATE_BANK = (0, 1), (2, 3, 4), (5, 6), 7
+TURNED_DA3_BANK = (2, 3, 4, 5, 2, 4, 3, 2)
 
 
 def tile_moe_bdx_glu_sigmoid_kernel(
@@ -112,9 +113,10 @@ def tile_moe_bdx_glu_sigmoid_kernel(
         load_w2_words(MID, MID + 1)
         load_saved(a1_t, a1, "a1_t", MID + PAIR, E)
         nc.sync.dma_start(pos_t[0][:], pos1)
+        load_w2_words(MID + 1, MID + PAIR)
         load_saved(a3_t, a3, "a3_t", MID, MID + PAIR)
         nc.sync.dma_start(pos_t[1][:], pos2)
-        for e in range(MID + 1, E):
+        for e in range(MID + PAIR, E):
             load_w2_words(e, e + 1)
         load_saved(a3_t, a3, "a3_t", MID + PAIR, E)
 
@@ -179,11 +181,11 @@ def tile_moe_bdx_glu_sigmoid_kernel(
                 da3_t = work.tile([P, PACK, P], F32, name="da3_t")
             nc.vector.scalar_tensor_tensor(
                 da3_t[:], sig_t[e][:], gate_ps[:, 0, e : e + 1], sums[e][:].rearrange("c (p t) -> c t p", t=PACK), ALU.mult, ALU.mult)
-            da3_ps[e] = bank_tile(DA3_BANKS[e % len(DA3_BANKS)], [P, PACK, C])
+            da3_ps[e] = bank_tile(TURNED_DA3_BANK[e], [P, PACK, C])
             for t in range(PACK):
                 nc.tensor.transpose(da3_ps[e][:, t, :], da3_t[:, t, :], ident[:])
 
-        takes_bytes_of = {(0, W3): "a1_t4", (1, W3): "a1_t6", (0, W1): "sig_t2", (1, W1): "a1_t4", (2, W1): "a1_t6"}
+        takes_bytes_of = {(1, W3): "a1_t6", (0, W1): "sig_t2", (1, W1): "da01", (2, W1): "a1_t6"}
 
         def rounded(e, m):
             g = group_of[e]
@@ -204,7 +206,7 @@ def tile_moe_bdx_glu_sigmoid_kernel(
             )
 
         def finish(e):
-            for step in (make_da1, round_da3) if e < E - PAIR else (round_da3, make_da1):
+            for step in (make_da1, round_da3) if PAIR <= e < E - PAIR else (round_da3, make_da1):
                 step(e)
 
         def quantise(g, name):
@@ -217,21 +219,23 @@ def tile_moe_bdx_glu_sigmoid_kernel(
 
         acc = {}
 
-        def second_product(experts, kt, bank):
+        def second_product(experts, kt, bank, by_matrix=False):
             if bank not in acc:
                 acc[bank] = bank_tile(bank, [P, MID * C])
-            for e in experts:
+            passes = [(m, e) for e in experts for m in (W3, W1)]
+            if by_matrix:
+                passes = [(m, e) for m in (W3, W1) for e in experts]
+            for m, e in passes:
                 g = group_of[e]
-                for m in (W3, W1):
-                    nc.tensor.matmul_mx(
-                        acc[bank][:, e % MID * C : (e % MID + 1) * C],
-                        lhsT=w13_w[m, e, kt].bitcast(FP4X4),
-                        lhsT_scale=w13_s[m][:, e, P * kt : P * (kt + 1)],
-                        rhs=da_w[g][:, m, columns(e)].bitcast(FP8X4),
-                        rhs_scale=da_s[g][:, m, columns(e)],
-                        start=(m == W3),
-                        stop=(m == W1),
-                    )
+                nc.tensor.matmul_mx(
+                    acc[bank][:, e % MID * C : (e % MID + 1) * C],
+                    lhsT=w13_w[m, e, kt].bitcast(FP4X4),
+                    lhsT_scale=w13_s[m][:, e, P * kt : P * (kt + 1)],
+                    rhs=da_w[g][:, m, columns(e)].bitcast(FP8X4),
+                    rhs_scale=da_s[g][:, m, columns(e)],
+                    start=((m, e) == passes[0]) if by_matrix else (m == W3),
+                    stop=((m, e) == passes[-1]) if by_matrix else (m == W1),
+                )
 
         def copy_dx(copier, e0, e1, kt, bank):
             copier(dx[kt][:, e0 * C : e1 * C], acc[bank][:, e0 % MID * C : ((e1 - 1) % MID + 1) * C])
@@ -260,7 +264,7 @@ def tile_moe_bdx_glu_sigmoid_kernel(
             first_product(e)
             make_da3(e)
             finish(e - PAIR)
-        sigmoids(6, A1_BANKS, together(6))
+        sigmoids(6, A1_BANKS[1:] * 2, together(6))
 
         first_product(4)
         make_da3(4)
@@ -286,8 +290,9 @@ def tile_moe_bdx_glu_sigmoid_kernel(
         finish(4)
         first_product(7)
         make_da3(7)
+        round_da3(6)
         finish(5)
-        finish(6)
+        make_da1(6)
         quantise(2, "da_w2")
         finish(7)
         quantise(3, "da_w3")
@@ -303,8 +308,8 @@ def tile_moe_bdx_glu_sigmoid_kernel(
                 copy_dx(nc.scalar.copy, MID, E - 1, 0, SUM_BANKS[0])
         copy_dx(nc.scalar.copy, E - 1, E, 0, SUM_BANKS[1])
         copy_dx(nc.vector.tensor_copy, MID, E, 1, GATE_BANK)
-        for e0, bank, copier in ((0, DA3_BANKS[2], nc.vector.tensor_copy), (MID, DA3_BANKS[0], nc.scalar.copy)):
-            second_product(range(e0, e0 + MID), 2, bank)
+        for e0, bank, copier in ((0, DA3_BANKS[2], nc.vector.tensor_copy), (MID, DA3_BANKS[1], nc.scalar.copy)):
+            second_product(range(e0, e0 + MID), 2, bank, True)
             copy_dx(copier, e0, e0 + MID, 2, bank)
 
         cuts = ((0, 2 * C, T), (0, 2 * C, T), (0, 2 * C, 3 * C, T))

@@ -32,7 +32,7 @@ BANK = 2048
 W1, W3 = 0, 1
 
 SUM_BANKS, DA3_BANKS, A1_BANKS, GATE_BANK = (0, 1), (2, 3, 4), (5, 6), 7
-TURNED_DA3_BANK = (2, 3, 4, 5, 2, 4, 3, 2)
+TURNED_DA3_BANK = (2, 3, 4, 5, 2, 4, 3, 5)
 
 
 def tile_moe_bdx_glu_sigmoid_kernel(
@@ -219,12 +219,9 @@ def tile_moe_bdx_glu_sigmoid_kernel(
 
         acc = {}
 
-        def second_product(experts, kt, bank, by_matrix=False):
-            if bank not in acc:
+        def second_passes(kt, bank, passes, opens=True, closes=True):
+            if opens:
                 acc[bank] = bank_tile(bank, [P, MID * C])
-            passes = [(m, e) for e in experts for m in (W3, W1)]
-            if by_matrix:
-                passes = [(m, e) for m in (W3, W1) for e in experts]
             for m, e in passes:
                 g = group_of[e]
                 nc.tensor.matmul_mx(
@@ -233,9 +230,15 @@ def tile_moe_bdx_glu_sigmoid_kernel(
                     lhsT_scale=w13_s[m][:, e, P * kt : P * (kt + 1)],
                     rhs=da_w[g][:, m, columns(e)].bitcast(FP8X4),
                     rhs_scale=da_s[g][:, m, columns(e)],
-                    start=((m, e) == passes[0]) if by_matrix else (m == W3),
-                    stop=((m, e) == passes[-1]) if by_matrix else (m == W1),
+                    start=opens and (m, e) == passes[0],
+                    stop=closes and (m, e) == passes[-1],
                 )
+
+        def by_expert(e0, e1):
+            return [(m, e) for e in range(e0, e1) for m in (W3, W1)]
+
+        def by_matrix(e0, e1, order):
+            return [(m, e) for m in order for e in range(e0, e1)]
 
         def copy_dx(copier, e0, e1, kt, bank):
             copier(dx[kt][:, e0 * C : e1 * C], acc[bank][:, e0 % MID * C : ((e1 - 1) % MID + 1) * C])
@@ -274,10 +277,10 @@ def tile_moe_bdx_glu_sigmoid_kernel(
 
         for m, name in ((W1, "dy_w"), (W3, "g_w0")):
             w13_s[m] = keep.tile([P, E, K], U8, name=name, align_bytes=64)
-        for e0 in (0, MID):
-            for m, rows, words in ((W1, w1_scales, w1_words), (W3, w3_scales, w3_words)):
-                load_scales(nc.sync, w13_s[m], rows, e0 // 2, e0 // 2 + 2)
-                load_w13_words(e0, e0 + MID, 0, KT - 1, ((m, words),))
+        for m, rows, words in ((W1, w1_scales, w1_words), (W3, w3_scales, w3_words)):
+            load_scales(nc.sync, w13_s[m], rows, 0, ROWS)
+            load_w13_words(0, MID, 0, KT - 1, ((m, words),))
+        load_w13_words(MID, E, 0, KT - 1, ((W1, w1_words), (W3, w3_words)))
         load_w13_words(0, E, KT - 1, KT)
 
         first_product(5)
@@ -298,18 +301,20 @@ def tile_moe_bdx_glu_sigmoid_kernel(
         quantise(3, "da_w3")
         quantise(4, "da_w4")
 
-        for kt in (0, 1):
-            second_product(range(MID), kt, A1_BANKS[kt])
-            copy_dx(nc.scalar.copy, 0, MID, kt, A1_BANKS[kt])
-        for g in (2, 3, 4):
-            for kt, bank in enumerate((SUM_BANKS[0] if g < 4 else SUM_BANKS[1], GATE_BANK)):
-                second_product(range(*groups[g]), kt, bank)
-            if g == 3:
-                copy_dx(nc.scalar.copy, MID, E - 1, 0, SUM_BANKS[0])
-        copy_dx(nc.scalar.copy, E - 1, E, 0, SUM_BANKS[1])
-        copy_dx(nc.vector.tensor_copy, MID, E, 1, GATE_BANK)
-        for e0, bank, copier in ((0, DA3_BANKS[2], nc.vector.tensor_copy), (MID, DA3_BANKS[1], nc.scalar.copy)):
-            second_product(range(e0, e0 + MID), 2, bank, True)
+        for kt, bank, copier in ((0, SUM_BANKS[1], nc.scalar.copy), (1, GATE_BANK, nc.vector.tensor_copy)):
+            second_passes(kt, bank, by_expert(0, MID))
+            copy_dx(copier, 0, MID, kt, bank)
+        banks = (DA3_BANKS[2], DA3_BANKS[1])
+        for kt, bank in enumerate(banks):
+            second_passes(kt, bank, by_matrix(*groups[2], (W1, W3)), closes=False)
+        second_passes(0, banks[0], by_expert(*groups[3]), opens=False)
+        copy_dx(nc.scalar.copy, MID, E - 1, 0, banks[0])
+        second_passes(0, A1_BANKS[1], by_expert(*groups[4]))
+        copy_dx(nc.scalar.copy, E - 1, E, 0, A1_BANKS[1])
+        second_passes(1, banks[1], by_expert(E - PAIR, E), opens=False)
+        copy_dx(nc.vector.tensor_copy, MID, E, 1, banks[1])
+        for e0, bank, copier in ((0, SUM_BANKS[0], nc.vector.tensor_copy), (MID, DA3_BANKS[0], nc.scalar.copy)):
+            second_passes(2, bank, by_matrix(e0, e0 + MID, (W3, W1)))
             copy_dx(copier, e0, e0 + MID, 2, bank)
 
         cuts = ((0, 2 * C, T), (0, 2 * C, T), (0, 2 * C, 3 * C, T))

@@ -301,7 +301,7 @@ def tile_moe_bdx_glu_sigmoid_kernel(
         quantise(3, "da_w3")
         quantise(4, "da_w4")
 
-        for kt, bank, copier in ((0, SUM_BANKS[1], nc.scalar.copy), (1, GATE_BANK, nc.vector.tensor_copy)):
+        for kt, bank, copier in ((0, SUM_BANKS[1], nc.scalar.copy), (1, GATE_BANK, nc.scalar.copy)):
             second_passes(kt, bank, by_expert(0, MID))
             copy_dx(copier, 0, MID, kt, bank)
         banks = (DA3_BANKS[2], DA3_BANKS[1])
@@ -317,11 +317,21 @@ def tile_moe_bdx_glu_sigmoid_kernel(
             second_passes(2, bank, by_matrix(e0, e0 + MID, (W3, W1)))
             copy_dx(copier, e0, e0 + MID, 2, bank)
 
-        cuts = ((0, 2 * C, T), (0, 2 * C, T), (0, 2 * C, 3 * C, T))
+        stores = (
+            ((0, (C, C)), (2 * C, (2 * C,))),
+            ((0, (2 * C,)), (2 * C, (2 * C,))),
+            ((0, (2 * C,)), (2 * C, (C,)), (3 * C, (C,))),
+        )
         for kt in range(KT):
-            for t0, t1 in zip(cuts[kt], cuts[kt][1:]):
-                fetched = keep.tile([P, t1 - t0], F32, name=f"fetched{kt}_{t0}")
-                nc.scalar.activation(fetched[:], dx[kt][:].indirect(pos_t[0][:, t0 // LIST : t1 // LIST]), ACT.Copy)
-                total = keep.tile([P, t1 - t0], F32, name=f"total{kt}_{t0}")
-                nc.vector.tensor_tensor(total[:], dx[kt][:].indirect(pos_t[1][:, t0 // LIST : t1 // LIST]), fetched[:], ALU.add)
-                nc.sync.dma_start(out[kt * P : (kt + 1) * P, t0:t1], total[:])
+            for first, widths in stores[kt]:
+                name = f"w13_w{W1}0{KT - 1}" if (kt, first) == (1, 0) else f"total{kt}_{first}"
+                total = keep.tile([P, sum(widths)], F32, name=name, align_bytes=64)
+                t0 = first
+                for width in widths:
+                    entries = slice(t0 // LIST, (t0 + width) // LIST)
+                    fetched = keep.tile([P, width], F32, name=f"fetched{kt}_{t0}")
+                    nc.scalar.activation(fetched[:], dx[kt][:].indirect(pos_t[0][:, entries]), ACT.Copy)
+                    nc.vector.tensor_tensor(
+                        total[:, t0 - first : t0 - first + width], dx[kt][:].indirect(pos_t[1][:, entries]), fetched[:], ALU.add)
+                    t0 = t0 + width
+                nc.sync.dma_start(out[kt * P : (kt + 1) * P, first : first + sum(widths)], total[:])

@@ -175,10 +175,7 @@ def tile_moe_bdx_glu_sigmoid_kernel(
                 )
 
         def make_da3(e):
-            if e == PAIR:
-                da3_t = keep.tile([P, PACK, P], F32, name="sig_minus0", align_bytes=64)
-            else:
-                da3_t = work.tile([P, PACK, P], F32, name="da3_t")
+            da3_t = work.tile([P, PACK, P], F32, name="da3_t")
             nc.vector.scalar_tensor_tensor(
                 da3_t[:], sig_t[e][:], gate_ps[:, 0, e : e + 1], sums[e][:].rearrange("c (p t) -> c t p", t=PACK), ALU.mult, ALU.mult)
             da3_ps[e] = bank_tile(TURNED_DA3_BANK[e], [P, PACK, C])
@@ -260,8 +257,8 @@ def tile_moe_bdx_glu_sigmoid_kernel(
         for e in range(PAIR):
             first_product(e)
             make_da3(e)
-        make_factor(nc.vector, "factor0", 0, singly(0))
-        make_factor(nc.gpsimd, "sig_minus1", 2, together(2))
+        make_factor(nc.gpsimd, "factor0", 0, singly(0))
+        make_factor(nc.gpsimd, "factor2", 2, together(2))
         sigmoids(4, (A1_BANKS[0], DA3_BANKS[2]), together(4))
         for e in (2, 3):
             first_product(e)

@@ -112,13 +112,12 @@ def tile_moe_bdx_glu_sigmoid_kernel(
         load_saved(a1_t, a1, "a1_t", MID, MID + PAIR)
         load_w2_words(MID, MID + 1)
         load_saved(a1_t, a1, "a1_t", MID + PAIR, E)
-        nc.sync.dma_start(pos_t[0][:], pos1)
-        load_w2_words(MID + 1, MID + PAIR)
         load_saved(a3_t, a3, "a3_t", MID, MID + PAIR)
-        nc.sync.dma_start(pos_t[1][:], pos2)
+        load_w2_words(MID + 1, MID + PAIR)
         for e in range(MID + PAIR, E):
             load_w2_words(e, e + 1)
         load_saved(a3_t, a3, "a3_t", MID + PAIR, E)
+        nc.sync.dma_start(pos_t[0][:], pos1)
 
         gate_ps = bank_tile(GATE_BANK, [P, PACK, C])
         nc.tensor.transpose(gate_ps[:, 0, :], gate_rows[:], ident[:])
@@ -277,6 +276,8 @@ def tile_moe_bdx_glu_sigmoid_kernel(
         for m, rows, words in ((W1, w1_scales, w1_words), (W3, w3_scales, w3_words)):
             load_scales(nc.sync, w13_s[m], rows, 0, ROWS)
             load_w13_words(0, MID, 0, KT - 1, ((m, words),))
+            if m == W1:
+                nc.sync.dma_start(pos_t[1][:], pos2)
         load_w13_words(MID, E, 0, KT - 1, ((W1, w1_words), (W3, w3_words)))
         load_w13_words(0, E, KT - 1, KT)
 

@@ -275,11 +275,11 @@ def tile_moe_bdx_glu_sigmoid_kernel(
             w13_s[m] = keep.tile([P, E, K], U8, name=name, align_bytes=64)
         for m, rows, words in ((W1, w1_scales, w1_words), (W3, w3_scales, w3_words)):
             load_scales(nc.sync, w13_s[m], rows, 0, ROWS)
-            load_w13_words(0, MID, 0, KT - 1, ((m, words),))
+            load_w13_words(0, MID, 0, KT, ((m, words),))
             if m == W1:
                 nc.sync.dma_start(pos_t[1][:], pos2)
         load_w13_words(MID, E, 0, KT - 1, ((W1, w1_words), (W3, w3_words)))
-        load_w13_words(0, E, KT - 1, KT)
+        load_w13_words(MID, E, KT - 1, KT)
 
         first_product(5)
         make_da3(5)
@@ -299,21 +299,21 @@ def tile_moe_bdx_glu_sigmoid_kernel(
         quantise(3, "da_w3")
         quantise(4, "da_w4")
 
-        for kt, bank, copier in ((0, SUM_BANKS[1], nc.scalar.copy), (1, GATE_BANK, nc.scalar.copy)):
-            second_passes(kt, bank, by_expert(0, MID))
-            copy_dx(copier, 0, MID, kt, bank)
+        for kt, bank in enumerate((SUM_BANKS[1], GATE_BANK, SUM_BANKS[0])):
+            second_passes(kt, bank, by_matrix(0, MID, (W1, W3)))
+            copy_dx(nc.scalar.copy, 0, MID, kt, bank)
         banks = (DA3_BANKS[2], DA3_BANKS[1])
         for kt, bank in enumerate(banks):
             second_passes(kt, bank, by_matrix(*groups[2], (W1, W3)), closes=False)
-        second_passes(0, banks[0], by_expert(*groups[3]), opens=False)
-        copy_dx(nc.scalar.copy, MID, E - 1, 0, banks[0])
-        second_passes(0, A1_BANKS[1], by_expert(*groups[4]))
-        copy_dx(nc.scalar.copy, E - 1, E, 0, A1_BANKS[1])
-        second_passes(1, banks[1], by_expert(E - PAIR, E), opens=False)
-        copy_dx(nc.vector.tensor_copy, MID, E, 1, banks[1])
-        for e0, bank, copier in ((0, SUM_BANKS[0], nc.vector.tensor_copy), (MID, DA3_BANKS[0], nc.scalar.copy)):
-            second_passes(2, bank, by_matrix(e0, e0 + MID, (W3, W1)))
-            copy_dx(copier, e0, e0 + MID, 2, bank)
+        for kt, copier in enumerate((nc.scalar.copy, nc.vector.tensor_copy)):
+            second_passes(kt, banks[kt], by_expert(*groups[3]), opens=False)
+            copy_dx(copier, MID, E - 1, kt, banks[kt])
+        for kt, bank in enumerate((A1_BANKS[1], A1_BANKS[0])):
+            second_passes(kt, bank, by_expert(*groups[4]))
+            copy_dx(nc.vector.tensor_copy, E - 1, E, kt, bank)
+        for e0, bank, copier in ((MID, DA3_BANKS[0], nc.scalar.copy), (MID + PAIR, SUM_BANKS[1], nc.vector.tensor_copy)):
+            second_passes(2, bank, by_matrix(e0, e0 + PAIR, (W3, W1)))
+            copy_dx(copier, e0, e0 + PAIR, 2, bank)
 
         stores = (
             ((0, (C, C)), (2 * C, (2 * C,))),
@@ -322,7 +322,7 @@ def tile_moe_bdx_glu_sigmoid_kernel(
         )
         for kt in range(KT):
             for first, widths in stores[kt]:
-                name = f"w13_w{W1}0{KT - 1}" if (kt, first) == (1, 0) else f"total{kt}_{first}"
+                name = f"w13_w{W1}{MID}{KT - 1}" if (kt, first) == (1, 0) else f"total{kt}_{first}"
                 total = keep.tile([P, sum(widths)], F32, name=name, align_bytes=64)
                 t0 = first
                 for width in widths:

@@ -181,7 +181,7 @@ def tile_moe_bdx_glu_sigmoid_kernel(
             for t in range(PACK):
                 nc.tensor.transpose(da3_ps[e][:, t, :], da3_t[:, t, :], ident[:])
 
-        takes_bytes_of = {(1, W3): "a1_t6", (0, W1): "sig_t2", (1, W1): "da01", (2, W1): "a1_t6"}
+        takes_bytes_of = {(1, W3): "a1_t6", (0, W1): "sig_t2", (1, W1): "da01", (2, W1): "sig_t7"}
 
         def rounded(e, m):
             g = group_of[e]
@@ -202,7 +202,7 @@ def tile_moe_bdx_glu_sigmoid_kernel(
             )
 
         def finish(e):
-            for step in (make_da1, round_da3) if PAIR <= e < E - PAIR else (round_da3, make_da1):
+            for step in (make_da1, round_da3) if PAIR <= e < MID else (round_da3, make_da1):
                 step(e)
 
         def quantise(g, name):
@@ -288,15 +288,16 @@ def tile_moe_bdx_glu_sigmoid_kernel(
         make_da3(6)
         quantise(1, "sig_t6")
         make_factor(nc.gpsimd, takes_bytes_of[1, W1], 6, singly(6))
-        finish(4)
         first_product(7)
         make_da3(7)
         round_da3(6)
+        finish(4)
         finish(5)
         make_da1(6)
+        round_da3(7)
         quantise(2, "da_w2")
-        finish(7)
         quantise(3, "da_w3")
+        make_da1(7)
         quantise(4, "da_w4")
 
         for kt, bank in enumerate((SUM_BANKS[1], GATE_BANK, SUM_BANKS[0])):
@@ -305,9 +306,9 @@ def tile_moe_bdx_glu_sigmoid_kernel(
         banks = (DA3_BANKS[2], DA3_BANKS[1])
         for kt, bank in enumerate(banks):
             second_passes(kt, bank, by_matrix(*groups[2], (W1, W3)), closes=False)
-        for kt, copier in enumerate((nc.scalar.copy, nc.vector.tensor_copy)):
-            second_passes(kt, banks[kt], by_expert(*groups[3]), opens=False)
-            copy_dx(copier, MID, E - 1, kt, banks[kt])
+        for kt, bank in enumerate(banks):
+            second_passes(kt, bank, by_expert(*groups[3]), opens=False)
+            copy_dx(nc.scalar.copy, MID, E - 1, kt, bank)
         for kt, bank in enumerate((A1_BANKS[1], A1_BANKS[0])):
             second_passes(kt, bank, by_expert(*groups[4]))
             copy_dx(nc.vector.tensor_copy, E - 1, E, kt, bank)

@@ -42,7 +42,6 @@ def tile_moe_bdx_glu_sigmoid_kernel(
     nc = tc.nc
     with ExitStack() as ctx:
         keep = ctx.enter_context(tc.tile_pool(name="keep", bufs=1))
-        work = ctx.enter_context(tc.tile_pool(name="work", bufs=4))
         psum = ctx.enter_context(tc.psum_pool(name="psum", bufs=1))
 
         def bank_tile(bank, shape):
@@ -155,8 +154,9 @@ def tile_moe_bdx_glu_sigmoid_kernel(
             nc.scalar.activation(tile[:], saved(a1_t, e0, e1), ACT.Sigmoid, scale=-1.0)
             sig_minus[e0, e1] = tile
 
-        def make_factor(engine, name, first, cuts):
-            factor[first, first + PAIR] = keep.tile([P, PACK, PAIR * C], F32, name=name, align_bytes=64)
+        def make_factor(engine, name, cuts):
+            first, last = cuts[0][0], cuts[-1][1]
+            factor[first, last] = keep.tile([P, PACK, (last - first) * C], F32, name=name, align_bytes=64)
             for e0, e1 in cuts:
                 engine.tensor_tensor(saved(factor, e0, e1), saved(sig_minus, e0, e1), saved(a3_t, e0, e1), ALU.mult)
 
@@ -174,7 +174,7 @@ def tile_moe_bdx_glu_sigmoid_kernel(
                 )
 
         def make_da3(e):
-            da3_t = work.tile([P, PACK, P], F32, name="da3_t")
+            da3_t = keep.tile([P, PACK, P], F32, name=f"da3_t{e}", align_bytes=64)
             nc.vector.scalar_tensor_tensor(
                 da3_t[:], sig_t[e][:], gate_ps[:, 0, e : e + 1], sums[e][:].rearrange("c (p t) -> c t p", t=PACK), ALU.mult, ALU.mult)
             da3_ps[e] = bank_tile(TURNED_DA3_BANK[e], [P, PACK, C])
@@ -256,8 +256,8 @@ def tile_moe_bdx_glu_sigmoid_kernel(
         for e in range(PAIR):
             first_product(e)
             make_da3(e)
-        make_factor(nc.gpsimd, "factor0", 0, singly(0))
-        make_factor(nc.gpsimd, "factor2", 2, together(2))
+        make_factor(nc.gpsimd, "factor0", singly(0))
+        make_factor(nc.gpsimd, "factor2", ((2, 3),))
         sigmoids(4, (A1_BANKS[0], DA3_BANKS[2]), together(4))
         for e in (2, 3):
             first_product(e)
@@ -267,8 +267,9 @@ def tile_moe_bdx_glu_sigmoid_kernel(
 
         first_product(4)
         make_da3(4)
-        quantise(0, "sig_t4")
-        make_factor(nc.gpsimd, takes_bytes_of[0, W1], 4, together(4))
+        make_factor(nc.vector, "sig_t4", ((3, 4),))
+        quantise(0, "da3_t4")
+        make_factor(nc.gpsimd, takes_bytes_of[0, W1], together(4))
         finish(2)
 
         for m, name in ((W1, "dy_w"), (W3, "g_w0")):
@@ -278,7 +279,9 @@ def tile_moe_bdx_glu_sigmoid_kernel(
             load_w13_words(0, MID, 0, KT, ((m, words),))
             if m == W1:
                 nc.sync.dma_start(pos_t[1][:], pos2)
-        load_w13_words(MID, E, 0, KT - 1, ((W1, w1_words), (W3, w3_words)))
+        load_w13_words(MID, E, 0, KT - 1, ((W1, w1_words),))
+        for e0 in (MID, MID + PAIR):
+            load_w13_words(e0, e0 + PAIR, 0, KT - 1, ((W3, w3_words),))
         load_w13_words(MID, E, KT - 1, KT)
 
         first_product(5)
@@ -287,7 +290,7 @@ def tile_moe_bdx_glu_sigmoid_kernel(
         first_product(6)
         make_da3(6)
         quantise(1, "sig_t6")
-        make_factor(nc.gpsimd, takes_bytes_of[1, W1], 6, singly(6))
+        make_factor(nc.gpsimd, takes_bytes_of[1, W1], singly(6))
         first_product(7)
         make_da3(7)
         round_da3(6)
@@ -318,7 +321,7 @@ def tile_moe_bdx_glu_sigmoid_kernel(
 
         stores = (
             ((0, (C, C)), (2 * C, (2 * C,))),
-            ((0, (2 * C,)), (2 * C, (2 * C,))),
+            ((0, (2 * C, 2 * C)),),
             ((0, (2 * C,)), (2 * C, (C,)), (3 * C, (C,))),
         )
         for kt in range(KT):

@@ -215,9 +215,8 @@ def tile_moe_bdx_glu_sigmoid_kernel(
 
         acc = {}
 
-        def second_passes(kt, bank, passes, opens=True, closes=True):
-            if opens:
-                acc[bank] = bank_tile(bank, [P, MID * C])
+        def second_passes(kt, bank, passes):
+            acc[bank] = bank_tile(bank, [P, MID * C])
             for m, e in passes:
                 g = group_of[e]
                 nc.tensor.matmul_mx(
@@ -226,8 +225,8 @@ def tile_moe_bdx_glu_sigmoid_kernel(
                     lhsT_scale=w13_s[m][:, e, P * kt : P * (kt + 1)],
                     rhs=da_w[g][:, m, columns(e)].bitcast(FP8X4),
                     rhs_scale=da_s[g][:, m, columns(e)],
-                    start=opens and (m, e) == passes[0],
-                    stop=closes and (m, e) == passes[-1],
+                    start=(m, e) == passes[0],
+                    stop=(m, e) == passes[-1],
                 )
 
         def by_expert(e0, e1):
@@ -306,18 +305,16 @@ def tile_moe_bdx_glu_sigmoid_kernel(
         for kt, bank in enumerate((SUM_BANKS[1], GATE_BANK, SUM_BANKS[0])):
             second_passes(kt, bank, by_matrix(0, MID, (W1, W3)))
             copy_dx(nc.scalar.copy, 0, MID, kt, bank)
-        banks = (DA3_BANKS[2], DA3_BANKS[1])
-        for kt, bank in enumerate(banks):
-            second_passes(kt, bank, by_matrix(*groups[2], (W1, W3)), closes=False)
-        for kt, bank in enumerate(banks):
-            second_passes(kt, bank, by_expert(*groups[3]), opens=False)
-            copy_dx(nc.scalar.copy, MID, E - 1, kt, bank)
-        for kt, bank in enumerate((A1_BANKS[1], A1_BANKS[0])):
-            second_passes(kt, bank, by_expert(*groups[4]))
-            copy_dx(nc.vector.tensor_copy, E - 1, E, kt, bank)
-        for e0, bank, copier in ((MID, DA3_BANKS[0], nc.scalar.copy), (MID + PAIR, SUM_BANKS[1], nc.vector.tensor_copy)):
-            second_passes(2, bank, by_matrix(e0, e0 + PAIR, (W3, W1)))
-            copy_dx(copier, e0, e0 + PAIR, 2, bank)
+        third, last = (MID, MID + PAIR), (MID + PAIR, E)
+        for kt, bank in enumerate((4, 2)):
+            second_passes(kt, bank, by_matrix(*third, (W1, W3)))
+            copy_dx(nc.scalar.copy, *third, kt, bank)
+        for kt, bank in enumerate((6, 5)):
+            second_passes(kt, bank, by_expert(*last))
+            copy_dx(nc.vector.tensor_copy, *last, kt, bank)
+        for (e0, e1), bank, copier in ((third, 3, nc.scalar.copy), (last, SUM_BANKS[1], nc.vector.tensor_copy)):
+            second_passes(2, bank, by_matrix(e0, e1, (W3, W1)))
+            copy_dx(copier, e0, e1, 2, bank)
 
         stores = (
             ((0, (C, C)), (2 * C, (2 * C,))),

@@ -102,9 +102,10 @@ def tile_moe_bdx_glu_sigmoid_kernel(
         load_saved(a1_t, a1, "a1_t", 0, MID)
         nc.sync.dma_start(gate_rows[0:E, :], gate[0].rearrange("(e c) -> e c", c=C))
         load_scales(nc.sync, w2_s_first, w2_scales[:PAIR], 0, 2)
-        load_w2_words(PAIR, MID)
+        load_saved(a3_t, a3, "a3_t", 0, PAIR)
         load_scales(nc.sync, w2_s_first, w2_scales[:PAIR], 2, ROWS)
-        load_saved(a3_t, a3, "a3_t", 0, MID)
+        load_w2_words(PAIR, MID)
+        load_saved(a3_t, a3, "a3_t", PAIR, MID)
         load_scales(nc.gpsimd, w2_s_others, w2_scales[PAIR:], 0, ROWS - 1)
         load_scales(nc.sync, w2_s_others, w2_scales[PAIR:], ROWS - 1, ROWS)
         pos_t = [keep.tile([P, T // LIST], U16, name=f"pos_t{r}") for r in range(2)]
@@ -256,7 +257,7 @@ def tile_moe_bdx_glu_sigmoid_kernel(
             first_product(e)
             make_da3(e)
         make_factor(nc.gpsimd, "factor0", singly(0))
-        make_factor(nc.gpsimd, "factor2", ((2, 3),))
+        make_factor(nc.gpsimd, "factor2", together(2))
         sigmoids(4, (A1_BANKS[0], DA3_BANKS[2]), together(4))
         for e in (2, 3):
             first_product(e)
@@ -266,8 +267,7 @@ def tile_moe_bdx_glu_sigmoid_kernel(
 
         first_product(4)
         make_da3(4)
-        make_factor(nc.vector, "sig_t4", ((3, 4),))
-        quantise(0, "da3_t4")
+        quantise(0, "sig_t4")
         make_factor(nc.gpsimd, takes_bytes_of[0, W1], together(4))
         finish(2)
 
@@ -317,7 +317,7 @@ def tile_moe_bdx_glu_sigmoid_kernel(
             copy_dx(copier, e0, e1, 2, bank)
 
         stores = (
-            ((0, (C, C)), (2 * C, (2 * C,))),
+            ((0, (C, C, 2 * C)),),
             ((0, (2 * C, 2 * C)),),
             ((0, (2 * C,)), (2 * C, (C,)), (3 * C, (C,))),
         )

from contextlib import ExitStack

import concourse.mybir as mybir
from concourse.masks import make_identity

K, T, E, C, H, N = 384, 512, 8, 128, 512, 1024
S = E * C
FLOPS = 2 * S * (N * H + 2 * H * K)

F32 = mybir.dt.float32
BF16 = mybir.dt.bfloat16
I32 = mybir.dt.int32
U32 = mybir.dt.uint32
U16 = mybir.dt.uint16
U8 = mybir.dt.uint8
FP8X4 = mybir.dt.float8_e4m3fn_x4
FP4X4 = mybir.dt.float4_e2m1fn_x4
ACT = mybir.ActivationFunctionType
ALU = mybir.AluOpType

P = 128
PACK = 4
QUADRANT = 32
ROWS = 4
PASSES = N // (P * PACK)
KT = K // P
PAIR = 2
MID = E // 2
HALF = S // 2
LIST = 16
BANK = 2048
W1, W3 = 0, 1

SUM_BANKS, DA3_BANKS, A1_BANKS, GATE_BANK = (0, 1), (2, 3, 4), (5, 6), 7
TURNED_DA3_BANK = (2, 3, 4, 5, 2, 4, 3, 5)


def tile_moe_bdx_glu_sigmoid_kernel(
    tc, dy_words, dy_scales, a1, a3, w2_words, w2_scales, w1_words, w1_scales,
    w3_words, w3_scales, gate, offs, pos1, pos2, out,
):
    nc = tc.nc
    with ExitStack() as ctx:
        keep = ctx.enter_context(tc.tile_pool(name="keep", bufs=1))
        psum = ctx.enter_context(tc.psum_pool(name="psum", bufs=1))

        def bank_tile(bank, shape):
            return psum.tile(shape, F32, name=f"bank{bank}", offset=bank * BANK)

        offs_t = keep.tile([P, S // LIST], U16, name="offs_t")
        nc.sync.dma_start(offs_t[:], offs)

        dy_w = keep.tile([P, PASSES + 1, T], U32, name="dy_w", align_bytes=64)
        for o in range(PASSES):
            nc.sync.dma_start(dy_w[:, PASSES - 1 - o, :].bitcast(I32), dy_words[o].rearrange("p t d -> p (t d)").bitcast(I32))
        dy_s = keep.tile([P, PASSES + 1, T], U8, name="dy_s", align_bytes=64)
        nc.gpsimd.memset(dy_s[:, :PASSES, :].bitcast(I32), 0)
        for r in range(ROWS):
            nc.sync.dma_start(
                dy_s[r:P:QUADRANT, :PASSES, :].bitcast(I32),
                dy_scales.rearrange("o (q r) t -> r q o t", r=ROWS)[r].bitcast(I32),
            )

        gate_rows = keep.tile([P, C], F32, name="gate_rows", align_bytes=64)
        ident = keep.tile([P, P], F32, name="ident")
        w2_s_first = keep.tile([P, PAIR * PASSES, H], U8, name="w2_s_first", align_bytes=64)
        w2_s_others = keep.tile([P, (E - PAIR) * PASSES, H], U8, name="w2_s_others", align_bytes=64)
        make_identity(nc, ident[:])
        nc.vector.memset(w2_s_others[:].bitcast(I32), 0)
        nc.vector.memset(w2_s_first[:].bitcast(I32), 0)
        nc.vector.memset(gate_rows[:], 0.0)

        def load_scales(queue, plane, rows, r0, r1):
            by_row = rows.rearrange("e s (q r) i -> r q (e s) i", r=ROWS)
            for r in range(r0, r1):
                queue.dma_start(plane[r:P:QUADRANT, :, :].bitcast(I32), by_row[r].bitcast(I32))

        w2_w, w13_w, w13_s, a1_t, a3_t = {}, {}, {}, {}, {}

        def load_w2_words(e0, e1):
            words = keep.tile([P, (e1 - e0) * PASSES, 2 * H], U8, name=f"w2_w{e0}", align_bytes=64)
            nc.sync.dma_start(words[:].bitcast(I32), w2_words[e0:e1].rearrange("e s p b -> p (e s) b").bitcast(I32))
            for e in range(e0, e1):
                w2_w[e] = words[:, (e - e0) * PASSES : (e - e0 + 1) * PASSES, :]

        def load_saved(tiles, rows, name, e0, e1):
            tiles[e0, e1] = keep.tile([P, PACK, (e1 - e0) * C], F32, name=f"{name}{e0}", align_bytes=64)
            nc.sync.dma_start(tiles[e0, e1][:], rows.rearrange("(p t) j -> p t j", t=PACK)[:, :, e0 * C : e1 * C])

        def load_w13_words(e0, e1, k0, k1, matrices=((W3, w3_words), (W1, w1_words))):
            for m, rows in matrices:
                words = keep.tile([P, e1 - e0, 2 * P * (k1 - k0)], U8, name=f"w13_w{m}{e0}{k0}", align_bytes=64)
                nc.sync.dma_start(
                    words[:].bitcast(I32),
                    rows[e0:e1].rearrange("e s p b -> p (e s) b")[:, :, 2 * P * k0 : 2 * P * k1].bitcast(I32),
                )
                for e in range(e0, e1):
                    for kt in range(k0, k1):
                        w13_w[m, e, kt] = words[:, e - e0, 2 * P * (kt - k0) : 2 * P * (kt - k0 + 1)]

        load_w2_words(0, PAIR)
        load_saved(a1_t, a1, "a1_t", 0, MID)
        nc.sync.dma_start(gate_rows[0:E, :], gate[0].rearrange("(e c) -> e c", c=C))
        load_scales(nc.sync, w2_s_first, w2_scales[:PAIR], 0, 2)
        load_saved(a3_t, a3, "a3_t", 0, PAIR)
        load_scales(nc.sync, w2_s_first, w2_scales[:PAIR], 2, ROWS)
        load_w2_words(PAIR, MID)
        load_saved(a3_t, a3, "a3_t", PAIR, MID)
        load_scales(nc.gpsimd, w2_s_others, w2_scales[PAIR:], 0, ROWS - 1)
        load_scales(nc.sync, w2_s_others, w2_scales[PAIR:], ROWS - 1, ROWS)
        pos_t = [keep.tile([P, T // LIST], U16, name=f"pos_t{r}") for r in range(2)]
        load_saved(a1_t, a1, "a1_t", MID, MID + PAIR)
        load_w2_words(MID, MID + 1)
        load_saved(a1_t, a1, "a1_t", MID + PAIR, E)
        load_saved(a3_t, a3, "a3_t", MID, MID + PAIR)
        load_w2_words(MID + 1, MID + PAIR)
        for e in range(MID + PAIR, E):
            load_w2_words(e, e + 1)
        load_saved(a3_t, a3, "a3_t", MID + PAIR, E)
        nc.sync.dma_start(pos_t[0][:], pos1)

        gate_ps = bank_tile(GATE_BANK, [P, PACK, C])
        nc.tensor.transpose(gate_ps[:, 0, :], gate_rows[:], ident[:])
        g_s = [keep.tile([P, PASSES, HALF], U8, name=name, align_bytes=64) for name in ("g_s", "gate_rows")]
        g_w = [keep.tile([P, PASSES, HALF], U32, name=f"g_w{h}", align_bytes=64) for h in range(2)]
        for gathered, table, rows, h in ((g_w, dy_w, (1, 0), 0), (g_s, dy_s, (0, 1), 0), (g_w, dy_w, (1, 0), 1), (g_s, dy_s, (0, 1), 1)):
            for o, row in enumerate(rows):
                nc.vector.tensor_copy(
                    gathered[h][:, o, :],
                    table[:, row : row + 2, :].rearrange("p o t -> p (o t)").indirect(offs_t[:, h * HALF // LIST : (h + 1) * HALF // LIST]),
                )

        dx = [keep.tile([P, S], F32, name=f"dx{kt}") for kt in range(KT)]
        groups = [(0, 2), (2, 4), (4, 6), (6, 7), (7, 8)]
        group_of = {e: g for g, (e0, e1) in enumerate(groups) for e in range(e0, e1)}
        da_w, da_s, da, sig_t, sig_minus, factor, sums, da3_ps = {}, {}, {}, {}, {}, {}, {}, {}

        def saved(tiles, e0, e1):
            first, last = [cut for cut in tiles if cut[0] <= e0 < cut[1]][0]
            return tiles[first, last][:, :, (e0 - first) * C : (e1 - first) * C]

        def columns(e):
            e0 = groups[group_of[e]][0]
            return slice((e - e0) * C, (e - e0 + 1) * C)

        def make_sigmoid(e, bank):
            turned = bank_tile(bank, [P, PACK, P])
            for t in range(PACK):
                nc.tensor.transpose(turned[:, t, :], saved(a1_t, e, e + 1)[:, t, :], ident[:])
            sig_t[e] = keep.tile([P, PACK, P], F32, name=f"sig_t{e}", align_bytes=64)
            nc.scalar.activation(sig_t[e][:], turned[:], ACT.Sigmoid)

        def make_sigmoid_minus(e0, e1):
            tile = keep.tile([P, PACK, (e1 - e0) * C], F32, name=f"sig_minus{e0}", align_bytes=64)
            nc.scalar.activation(tile[:], saved(a1_t, e0, e1), ACT.Sigmoid, scale=-1.0)
            sig_minus[e0, e1] = tile

        def make_factor(engine, name, cuts):
            first, last = cuts[0][0], cuts[-1][1]
            factor[first, last] = keep.tile([P, PACK, (last - first) * C], F32, name=name, align_bytes=64)
            for e0, e1 in cuts:
                engine.tensor_tensor(saved(factor, e0, e1), saved(sig_minus, e0, e1), saved(a3_t, e0, e1), ALU.mult)

        def first_product(e):
            sums[e] = bank_tile(SUM_BANKS[e % len(SUM_BANKS)], [P, H])
            for o in range(PASSES):
                nc.tensor.matmul_mx(
                    sums[e][:],
                    lhsT=g_w[e // MID][:, o, e % MID * C : (e % MID + 1) * C].bitcast(FP8X4),
                    lhsT_scale=g_s[e // MID][:, o, e % MID * C : (e % MID + 1) * C],
                    rhs=w2_w[e][:, o, :].bitcast(FP4X4),
                    rhs_scale=w2_s_first[:, e * PASSES + o, :] if e < PAIR else w2_s_others[:, (e - PAIR) * PASSES + o, :],
                    start=(o == 0),
                    stop=(o == PASSES - 1),
                )

        def make_da3(e):
            da3_t = keep.tile([P, PACK, P], F32, name=f"da3_t{e}", align_bytes=64)
            nc.vector.scalar_tensor_tensor(
                da3_t[:], sig_t[e][:], gate_ps[:, 0, e : e + 1], sums[e][:].rearrange("c (p t) -> c t p", t=PACK), ALU.mult, ALU.mult)
            da3_ps[e] = bank_tile(TURNED_DA3_BANK[e], [P, PACK, C])
            for t in range(PACK):
                nc.tensor.transpose(da3_ps[e][:, t, :], da3_t[:, t, :], ident[:])

        takes_bytes_of = {(1, W3): "a1_t6", (0, W1): "sig_t2", (1, W1): "da01", (2, W1): "sig_t7"}

        def rounded(e, m):
            g = group_of[e]
            if (g, m) not in da:
                name = takes_bytes_of.get((g, m), f"da{g}{m}")
                da[g, m] = keep.tile([P, (groups[g][1] - e) * C, PACK], BF16, name=name, align_bytes=64)
            return da[g, m][:, columns(e)]

        def round_da3(e):
            nc.scalar.copy(rounded(e, W3), da3_ps[e][:].rearrange("p t c -> p c t"))

        def make_da1(e):
            nc.vector.tensor_tensor(
                rounded(e, W1).rearrange("p (c i) t -> p c t i", i=2),
                saved(factor, e, e + 1).rearrange("p t (c i) -> p c t i", i=2),
                da3_ps[e][:].rearrange("p t (c i) -> p c t i", i=2),
                ALU.mult,
            )

        def finish(e):
            for step in (make_da1, round_da3) if PAIR <= e < MID else (round_da3, make_da1):
                step(e)

        def quantise(g, name):
            e0, e1 = groups[g]
            da_w[g] = keep.tile([P, 2, (e1 - e0) * C], U32, name=name, align_bytes=64)
            da_s[g] = keep.tile([P, 2, (e1 - e0) * C], U8, name=f"da_s{g}", align_bytes=64)
            for m in (W3, W1):
                nc.vector.quantize_mx(
                    out=da_w[g][:, m, :].bitcast(FP8X4), scales=da_s[g][:, m, :], in_=da[g, m][:].rearrange("p c t -> p (c t)"))

        acc = {}

        def second_passes(kt, bank, passes):
            acc[bank] = bank_tile(bank, [P, MID * C])
            for m, e in passes:
                g = group_of[e]
                nc.tensor.matmul_mx(
                    acc[bank][:, e % MID * C : (e % MID + 1) * C],
                    lhsT=w13_w[m, e, kt].bitcast(FP4X4),
                    lhsT_scale=w13_s[m][:, e, P * kt : P * (kt + 1)],
                    rhs=da_w[g][:, m, columns(e)].bitcast(FP8X4),
                    rhs_scale=da_s[g][:, m, columns(e)],
                    start=(m, e) == passes[0],
                    stop=(m, e) == passes[-1],
                )

        def by_expert(e0, e1):
            return [(m, e) for e in range(e0, e1) for m in (W3, W1)]

        def by_matrix(e0, e1, order):
            return [(m, e) for m in order for e in range(e0, e1)]

        def copy_dx(copier, e0, e1, kt, bank):
            copier(dx[kt][:, e0 * C : e1 * C], acc[bank][:, e0 % MID * C : ((e1 - 1) % MID + 1) * C])

        def singly(first):
            return ((first, first + 1), (first + 1, first + PAIR))

        def together(first):
            return ((first, first + PAIR),)

        def sigmoids(first, banks, cuts):
            for e, bank in zip((first, first + 1), banks):
                make_sigmoid(e, bank)
            for e0, e1 in cuts:
                make_sigmoid_minus(e0, e1)

        sigmoids(0, A1_BANKS, singly(0))
        sigmoids(2, A1_BANKS, together(2))
        for e in range(PAIR):
            first_product(e)
            make_da3(e)
        make_factor(nc.gpsimd, "factor0", singly(0))
        make_factor(nc.gpsimd, "factor2", together(2))
        sigmoids(4, (A1_BANKS[0], DA3_BANKS[2]), together(4))
        for e in (2, 3):
            first_product(e)
            make_da3(e)
            finish(e - PAIR)
        sigmoids(6, A1_BANKS[1:] * 2, together(6))

        first_product(4)
        make_da3(4)
        quantise(0, "sig_t4")
        make_factor(nc.gpsimd, takes_bytes_of[0, W1], together(4))
        finish(2)

        for m, name in ((W1, "dy_w"), (W3, "g_w0")):
            w13_s[m] = keep.tile([P, E, K], U8, name=name, align_bytes=64)
        for m, rows, words in ((W1, w1_scales, w1_words), (W3, w3_scales, w3_words)):
            load_scales(nc.sync, w13_s[m], rows, 0, ROWS)
            load_w13_words(0, MID, 0, KT, ((m, words),))
            if m == W1:
                nc.sync.dma_start(pos_t[1][:], pos2)
        load_w13_words(MID, E, 0, KT - 1, ((W1, w1_words),))
        for e0 in (MID, MID + PAIR):
            load_w13_words(e0, e0 + PAIR, 0, KT - 1, ((W3, w3_words),))
        load_w13_words(MID, E, KT - 1, KT)

        first_product(5)
        make_da3(5)
        finish(3)
        first_product(6)
        make_da3(6)
        quantise(1, "sig_t6")
        make_factor(nc.gpsimd, takes_bytes_of[1, W1], singly(6))
        first_product(7)
        make_da3(7)
        round_da3(6)
        finish(4)
        finish(5)
        make_da1(6)
        round_da3(7)
        quantise(2, "da_w2")
        quantise(3, "da_w3")
        make_da1(7)
        quantise(4, "da_w4")

        for kt, bank in enumerate((SUM_BANKS[1], GATE_BANK, SUM_BANKS[0])):
            second_passes(kt, bank, by_matrix(0, MID, (W1, W3)))
            copy_dx(nc.scalar.copy, 0, MID, kt, bank)
        third, last = (MID, MID + PAIR), (MID + PAIR, E)
        for kt, bank in enumerate((4, 2)):
            second_passes(kt, bank, by_matrix(*third, (W1, W3)))
            copy_dx(nc.scalar.copy, *third, kt, bank)
        for kt, bank in enumerate((6, 5)):
            second_passes(kt, bank, by_expert(*last))
            copy_dx(nc.vector.tensor_copy, *last, kt, bank)
        for (e0, e1), bank, copier in ((third, 3, nc.scalar.copy), (last, SUM_BANKS[1], nc.vector.tensor_copy)):
            second_passes(2, bank, by_matrix(e0, e1, (W3, W1)))
            copy_dx(copier, e0, e1, 2, bank)

        stores = (
            ((0, (C, C, 2 * C)),),
            ((0, (2 * C, 2 * C)),),
            ((0, (2 * C,)), (2 * C, (C,)), (3 * C, (C,))),
        )
        for kt in range(KT):
            for first, widths in stores[kt]:
                name = f"w13_w{W1}{MID}{KT - 1}" if (kt, first) == (1, 0) else f"total{kt}_{first}"
                total = keep.tile([P, sum(widths)], F32, name=name, align_bytes=64)
                t0 = first
                for width in widths:
                    entries = slice(t0 // LIST, (t0 + width) // LIST)
                    fetched = keep.tile([P, width], F32, name=f"fetched{kt}_{t0}")
                    nc.scalar.activation(fetched[:], dx[kt][:].indirect(pos_t[0][:, entries]), ACT.Copy)
                    nc.vector.tensor_tensor(
                        total[:, t0 - first : t0 - first + width], dx[kt][:].indirect(pos_t[1][:, entries]), fetched[:], ALU.add)
                    t0 = t0 + width
                nc.sync.dma_start(out[kt * P : (kt + 1) * P, first : first + sum(widths)], total[:])
